import numpy as np
import ml_dtypes


def mxq(x, axis, fmt="e4m3"):
    dtype, down = {"e4m3": (ml_dtypes.float8_e4m3fn, 7), "e5m2": (ml_dtypes.float8_e5m2, 14)}[fmt]
    v = np.moveaxis(np.asarray(x, np.float32).astype(ml_dtypes.bfloat16).astype(np.float64), axis, -1)
    blocks = v.reshape(v.shape[:-1] + (-1, 32))
    amax = np.abs(blocks).max(-1, keepdims=True)
    byte = np.maximum(np.where(amax > 0, np.frexp(amax)[1] - 1 + 127, 0) - down, 1)
    scale = np.exp2(byte - 127.0)
    codes = (blocks / scale).astype(np.float32).astype(dtype).astype(np.float64)
    return np.moveaxis((codes * scale).reshape(v.shape), -1, axis)


WIDE = False


def mx_kscale(k):
    if not WIDE:
        return np.ones(k)
    levels = np.array([10, -10, 5, -5, 0])
    if k % 512:
        return np.exp2(np.random.permutation(np.resize(levels, k // 32))).repeat(32)
    a = np.empty((k // 512, 16))
    for p in range(k // 512):
        a[p, :8] = np.random.permutation(np.resize(levels, 8))
        for g in range(8):
            far = levels[np.abs(levels - a[p, g]) >= 10]
            a[p, g + 8] = far[np.random.randint(len(far))]
    return np.exp2(a.ravel()).repeat(32)


def f64(x):
    return np.asarray(x).astype(np.float64)


def striped(idx):
    return np.tile(idx.reshape(-1, 16).T, (8, 1)).astype(np.uint16)


def unstriped(offs):
    return offs[:16].T.reshape(-1).astype(np.int64)


E2M1 = np.array([0.0, 0.5, 1.0, 1.5, 2.0, 3.0, 4.0, 6.0, -0.0, -0.5, -1.0, -1.5, -2.0, -3.0, -4.0, -6.0])


def pack_weight(w, fmt):
    k, n = w.shape
    w = f64(np.asarray(w, np.float32).astype(ml_dtypes.bfloat16)).reshape(k // 32, 32, n)
    amax = np.abs(w).max(1)
    if fmt == "e4m3":
        byte = np.frexp(amax)[1] - 1 + 127 - 7
    else:
        mant, ex = np.frexp(amax / 6.0)
        byte = np.where(mant > 0.5, ex, ex - 1) + 127
    byte = np.clip(np.where(amax > 0, byte, 1), 1, 254)
    scaled = (w * np.exp2(127.0 - byte)[:, None, :]).reshape(k, n).astype(np.float32)
    by_word = np.ascontiguousarray(scaled.reshape(k // 512, 128, 4, n).transpose(0, 1, 3, 2))
    if fmt == "e4m3":
        words = by_word.astype(ml_dtypes.float8_e4m3fn).view(np.uint8)
    else:
        c = by_word.astype(ml_dtypes.float4_e2m1fn).view(np.uint8) & 0xF
        words = (c[..., 0::2] | (c[..., 1::2] << 4)).reshape(k // 512, 128, 2 * n)
    return np.ascontiguousarray(words), np.ascontiguousarray(byte.astype(np.uint8).reshape(k // 512, 16, n))


def unpack_weight(words, scales, fmt):
    g, _, n = scales.shape
    words = np.ascontiguousarray(words).reshape(g, 128, n, -1)
    if fmt == "e4m3":
        vals = words.view(ml_dtypes.float8_e4m3fn).astype(np.float64)
    else:
        nib = np.empty((g, 128, n, 4), np.uint8)
        nib[..., 0::2] = words & 0xF
        nib[..., 1::2] = words >> 4
        vals = E2M1[nib]
    vals = vals * np.repeat(np.exp2(scales.astype(np.float64) - 127.0), 8, axis=1)[..., None]
    return vals.transpose(0, 1, 3, 2).reshape(g * 512, n)


def gelu(v):
    return 0.5 * v * (1.0 + np.tanh(np.sqrt(2.0 / np.pi) * (v + 0.044715 * v**3)))


K, T, S, H, T2, P, N = 1024, 2048, 512, 1024, 1024, 512, 512

def setup_inputs():
    n = np.random.standard_normal
    s = mx_kscale(K)[:, None]
    u = mx_kscale(H)[:, None]
    tab_words, tab_scales = pack_weight(n((K, T)) * s, "e4m3")
    w3_words, w3_scales = pack_weight(n((H, N)) / np.sqrt(H) / u, "e2m1")
    return {
        "tab_words": tab_words, "tab_scales": tab_scales,
        "offs": striped(np.random.permutation(T)[:S]),
        "w1": (n((K, H)) / np.sqrt(K) / s).astype(np.float32),
        "wgs": np.exp(0.3 * n((128, S))).astype(np.float32),
        "offs2": striped(np.random.permutation(T2)[:S]),
        "rest": (0.7 * n(H)).astype(np.float32),
        "gains": (np.exp(0.4 * n((H, T2))) * u).astype(np.float32),
        "w2": (n((H, N)) / np.sqrt(H) / u).astype(np.float32),
        "w3_words": w3_words, "w3_scales": w3_scales,
        "offs3": striped(np.random.permutation(T2)[:P]),
        "expected": n((N, P)).astype(np.float32),
        "wgo": np.exp(0.3 * n((128, P))).astype(np.float32),
        "offs4": striped(np.random.permutation(T2)[:P]),
    }

def reference(tab_words, tab_scales, offs, w1, wgs, offs2, rest, gains, w2, w3_words, w3_scales, offs3, expected, wgo, offs4):
    v = unpack_weight(tab_words, tab_scales, "e4m3")[:, unstriped(offs)]
    h = np.abs(mxq(f64(w1), 0, "e4m3").T @ v)
    page = np.zeros((H, T2))
    page[:, unstriped(offs2)] = np.tile(f64(wgs), (H // 128, 1)) * h
    z = (page + f64(rest)[:, None]) * f64(gains)
    zq = mxq(z, 0, "e4m3")
    ya = mxq(f64(w2), 0, "e4m3").T @ zq
    yb = unpack_weight(w3_words, w3_scales, "e2m1").T @ zq
    y = ya * yb
    x = y[:, unstriped(offs3)] - f64(expected)
    out = np.zeros((N, T2))
    out[:, unstriped(offs4)] = np.tile(f64(wgo), (N // 128, 1)) * x
    return out

@@ -1,0 +1,288 @@
+from contextlib import ExitStack
+
+import concourse.mybir as mybir
+
+K, T, S, H, T2, N = 1024, 2048, 512, 1024, 1024, 512
+FLOPS = 2 * K * H * S + 2 * 2 * H * N * T2
+
+F32 = mybir.dt.float32
+BF16 = mybir.dt.bfloat16
+I32 = mybir.dt.int32
+U32 = mybir.dt.uint32
+U16 = mybir.dt.uint16
+U8 = mybir.dt.uint8
+FP8X4 = mybir.dt.float8_e4m3fn_x4
+FP4X4 = mybir.dt.float4_e2m1fn_x4
+ALU = mybir.AluOpType
+ACT = mybir.ActivationFunctionType
+
+P = 128
+PACK = 4
+KP = P * PACK
+BANK = 512
+
+
+def tile_list_returns_chute_grading_kernel(
+    tc, tab_words, tab_scales, offs, w1, wgs, offs2, rest, gains, w2, w3_words, w3_scales, offs3, expected, wgo, offs4, out
+):
+    nc = tc.nc
+    with ExitStack() as ctx:
+        keep = ctx.enter_context(tc.tile_pool(name="keep", bufs=1))
+        ring = ctx.enter_context(tc.tile_pool(name="ring", bufs=2))
+        psum = ctx.enter_context(tc.psum_pool(name="psum", bufs=1))
+
+        def load_list(name, src):
+            t = keep.tile([P, S // 16], U16, name=name)
+            nc.sync.dma_start(t[:], src)
+            return t
+
+        def load_weight(rows):
+            raw = ring.tile([P, PACK, BANK], F32, name="w_raw", bufs=4)
+            nc.sync.dma_start(out=raw[:], in_=rows.rearrange("(p j) c -> p j c", j=PACK))
+            return raw
+
+        def bank(n):
+            return psum.tile([P, BANK], F32, name=f"bank{n}")
+
+        def quantize(name, grouped):
+            codes = keep.tile([P, BANK], U32, name=name + "_codes", align_bytes=64)
+            scales = keep.tile([P, BANK], U8, name=name + "_scales", align_bytes=64)
+            nc.vector.quantize_mx(out=codes[:].bitcast(FP8X4), scales=scales[:], in_=grouped[:])
+            return codes, scales
+
+        def grouped_tile():
+            return ring.tile([P, BANK * PACK], BF16, name="grouped", bufs=4, align_bytes=64)
+
+        def group_w1(copy, raw):
+            g = grouped_tile()
+            copy(
+                out=g[:].rearrange("p (t m j) -> p m t j", t=PACK, j=PACK),
+                in_=raw[:].rearrange("p j (m t) -> p m t j", t=PACK),
+            )
+            return g
+
+        def group_rows(copy, rows):
+            g = grouped_tile()
+            copy(
+                out=g[:].rearrange("p (c i j) -> p c j i", i=4, j=PACK),
+                in_=rows.rearrange("p j (c i) -> p c j i", i=4),
+            )
+            return g
+
+        tab_s = keep.tile([P, T], U8, name="tab_s", align_bytes=64)
+        nc.gpsimd.memset(tab_s[:].bitcast(I32), 0)
+        for q in range(4):
+            nc.gpsimd.dma_start(
+                out=tab_s[32 * q : 32 * q + 8, :].bitcast(I32),
+                in_=tab_scales[:, 4 * q : 4 * q + 4, :].bitcast(I32),
+            )
+        w3_s = keep.tile([P, 2, N], U8, name="w3_s", align_bytes=64)
+        nc.vector.memset(w3_s[:].bitcast(I32), 0)
+        pages = [keep.tile([P, T2], F32, name=f"page{n}") for n in range(3)]
+        cages = [keep.tile([P, T2], F32, name=f"cage{n}") for n in range(2)]
+        for t in pages + cages:
+            nc.vector.memset(t[:], 0.0)
+
+        idx = load_list("idx", offs)
+        w1_raw = {}
+        for a in range(2):
+            w1_raw[0, a] = load_weight(w1[KP * a : KP * (a + 1), 0:KP])
+        tab_w = []
+        for a in range(2):
+            t = keep.tile([P, T], I32, name=f"tab_w{a}")
+            nc.sync.dma_start(out=t[:], in_=tab_words[a].rearrange("p t i -> p (t i)").bitcast(I32))
+            tab_w.append(t)
+        idx2 = load_list("idx2", offs2)
+        wgs_sb = keep.tile([P, PACK * S], F32, name="wgs_sb")
+        for q in range(4):
+            nc.sync.dma_start(out=wgs_sb[32 * q : 32 * (q + 1), :], in_=wgs.rearrange("(m i) j -> m (i j)", i=PACK))
+        rest_sb = keep.tile([P, 2, PACK], F32, name="rest_sb")
+        nc.sync.dma_start(out=rest_sb[:], in_=rest.rearrange("(b p i) -> p b i", b=2, i=PACK))
+        gains_rows = gains.rearrange("(b p i) t -> b i p t", b=2, i=PACK)
+        gains_sb = {}
+
+        def load_gains(b, i):
+            t = keep.tile([P, T2], F32, name=f"gains{b}{i}")
+            nc.sync.dma_start(out=t[:], in_=gains_rows[b, i])
+            gains_sb[b, i] = t
+
+        load_gains(0, 0)
+        load_gains(0, 1)
+        for a in range(2):
+            w1_raw[1, a] = load_weight(w1[KP * a : KP * (a + 1), KP : 2 * KP])
+        load_gains(0, 2)
+        load_gains(0, 3)
+
+        w1_q = {}
+        g0 = group_w1(nc.vector.tensor_copy, w1_raw[0, 0])
+        g1 = group_w1(nc.vector.tensor_copy, w1_raw[0, 1])
+        w1_q[0, 0] = quantize("w1_00", g0)
+        v_s = keep.tile([P, S], U8, name="v_s", align_bytes=64)
+        nc.vector.tensor_copy(v_s[:], tab_s[:].indirect(idx[:]))
+        w1_q[0, 1] = quantize("w1_01", g1)
+        v_w = []
+        for a in range(2):
+            t = keep.tile([P, S], U32, name=f"v_w{a}", align_bytes=64)
+            nc.vector.tensor_copy(t[:], tab_w[a][:].bitcast(U32).indirect(idx[:]))
+            v_w.append(t)
+
+        w2_raw = [load_weight(w2[KP * b : KP * (b + 1), :]) for b in range(2)]
+        for i in range(PACK):
+            load_gains(1, i)
+        w3_w = keep.tile([P, 2, 2 * N], U8, name="w3_w", align_bytes=64)
+        nc.sync.dma_start(out=w3_w[:].bitcast(I32), in_=w3_words.rearrange("a p n -> p a n").bitcast(I32))
+        for q in range(4):
+            nc.sync.dma_start(
+                out=w3_s[32 * q : 32 * q + 4, :, :].bitcast(I32),
+                in_=w3_scales[:, 4 * q : 4 * q + 4, :].rearrange("a r n -> r a n").bitcast(I32),
+            )
+        idx3 = load_list("idx3", offs3)
+        idx4 = load_list("idx4", offs4)
+        exp_sb = keep.tile([P, N // P, S], F32, name="exp_sb")
+        nc.sync.dma_start(out=exp_sb[:], in_=expected.rearrange("(c p) m -> p c m", p=P))
+        wgo_sb = keep.tile([P, S], F32, name="wgo_sb")
+        nc.sync.dma_start(out=wgo_sb[:], in_=wgo)
+
+        h_abs = {}
+
+        def first_product(n):
+            b, i = divmod(n, PACK)
+            acc = bank(4 + i)
+            cols = slice(P * i, P * (i + 1))
+            for a in range(2):
+                codes, scales = w1_q[b, a]
+                nc.tensor.matmul_mx(
+                    out=acc[:],
+                    lhsT=codes[:, cols].bitcast(FP8X4),
+                    lhsT_scale=scales[:, cols],
+                    rhs=v_w[a][:].bitcast(FP8X4),
+                    rhs_scale=v_s[4 * a : P, :],
+                    start=(a == 0),
+                    stop=(a == 1),
+                )
+            t = ring.tile([P, S], F32, name="h_abs", bufs=4)
+            nc.scalar.activation(out=t[:], in_=acc[:], func=ACT.Abs)
+            h_abs[n] = t
+
+        z_rows = [keep.tile([P, PACK, T2], BF16, name=f"z_rows{b}") for b in range(2)]
+
+        def place(n):
+            i = n % PACK
+            nc.vector.tensor_tensor(
+                pages[n % 3][:].indirect(idx2[:]), h_abs[n][:], wgs_sb[:, S * i : S * (i + 1)], ALU.mult
+            )
+
+        def make_z(n, cols):
+            b, i = divmod(n, PACK)
+            nc.vector.scalar_tensor_tensor(
+                out=z_rows[b][:, i, cols],
+                in0=pages[n % 3][:, cols],
+                scalar=rest_sb[:, b, i : i + 1],
+                in1=gains_sb[b, i][:, cols],
+                op0=ALU.add,
+                op1=ALU.mult,
+            )
+
+        halves = [slice(0, BANK), slice(BANK, 2 * BANK)]
+        whole = slice(0, T2)
+        z_q = {}
+        w2_q = {}
+
+        for n in range(4):
+            first_product(n)
+        w1_g = [group_w1(nc.scalar.copy, w1_raw[1, a]) for a in range(2)]
+        place(0)
+        place(1)
+        make_z(0, whole)
+        place(2)
+        make_z(1, whole)
+        for a in range(2):
+            w1_q[1, a] = quantize(f"w1_1{a}", w1_g[a])
+        place(3)
+        for n in range(4, 8):
+            first_product(n)
+        make_z(2, whole)
+        w2_g = [group_rows(nc.scalar.copy, w2_raw[b][:]) for b in range(2)]
+        place(4)
+        make_z(3, whole)
+        z_g = [group_rows(nc.scalar.copy, z_rows[0][:, :, h]) for h in halves]
+        for b in range(2):
+            w2_q[b] = quantize(f"w2_{b}", w2_g[b])
+        place(5)
+        make_z(4, whole)
+        place(6)
+        make_z(5, whole)
+        for h in range(2):
+            z_q[0, h] = quantize(f"z_0{h}", z_g[h])
+        place(7)
+        make_z(6, whole)
+        make_z(7, halves[0])
+        make_z(7, halves[1])
+        z_g = [
+            group_rows(nc.scalar.copy, z_rows[1][:, :, halves[0]]),
+            group_rows(nc.vector.tensor_copy, z_rows[1][:, :, halves[1]]),
+        ]
+        z_q[1, 1] = quantize("z_11", z_g[1])
+        z_q[1, 0] = quantize("z_10", z_g[0])
+
+        accs = {}
+
+        def second_pass(c, h, b):
+            cols = slice(P * c, P * (c + 1))
+            if b == 0:
+                accs[c, h] = (bank(4 * (c % 2) + 2 * h), bank(4 * (c % 2) + 2 * h + 1))
+            ya, yb = accs[c, h]
+            z_codes, z_scales = z_q[b, h]
+            nc.tensor.matmul_mx(
+                out=yb[:],
+                lhsT=w3_w[:, b, 2 * P * c : 2 * P * (c + 1)].bitcast(FP4X4),
+                lhsT_scale=w3_s[:, b, cols],
+                rhs=z_codes[:].bitcast(FP8X4),
+                rhs_scale=z_scales[:],
+                start=(b == 0),
+                stop=(b == 1),
+            )
+            codes, scales = w2_q[b]
+            nc.tensor.matmul_mx(
+                out=ya[:],
+                lhsT=codes[:, cols].bitcast(FP8X4),
+                lhsT_scale=scales[:, cols],
+                rhs=z_codes[:].bitcast(FP8X4),
+                rhs_scale=z_scales[:],
+                start=(b == 0),
+                stop=(b == 1),
+            )
+
+        y_sb = {}
+        x_sb = {}
+
+        def scores(c):
+            for h in (1, 0):
+                second_pass(c, h, 0)
+            for h in (1, 0):
+                second_pass(c, h, 1)
+            y = ring.tile([P, T2], F32, name="y")
+            for h in (1, 0):
+                ya, yb = accs[c, h]
+                t = ring.tile([P, BANK], F32, name="yb_sb", bufs=4)
+                nc.scalar.copy(out=t[:], in_=yb[:])
+                nc.vector.tensor_tensor(y[:, halves[h]], ya[:], t[:], ALU.mult)
+            y_sb[c] = y
+
+        def pick(c):
+            x = ring.tile([P, S], F32, name="x")
+            nc.vector.tensor_tensor(x[:], y_sb[c][:].indirect(idx3[:]), exp_sb[:, c, :], ALU.subtract)
+            x_sb[c] = x
+
+        def put(c):
+            cage = cages[c % 2]
+            nc.vector.tensor_tensor(cage[:].indirect(idx4[:]), x_sb[c][:], wgo_sb[:], ALU.mult)
+            nc.sync.dma_start(out=out[P * c : P * (c + 1), :], in_=cage[:])
+
+        scores(0)
+        pick(0)
+        for c in range(1, 4):
+            scores(c)
+            put(c - 1)
+            pick(c)
+        put(3)

@@ -30,49 +30,48 @@ def tile_list_returns_chute_grading_kernel(
         keep = ctx.enter_context(tc.tile_pool(name="keep", bufs=1))
         ring = ctx.enter_context(tc.tile_pool(name="ring", bufs=2))
         psum = ctx.enter_context(tc.psum_pool(name="psum", bufs=1))
+        halves = [slice(0, BANK), slice(BANK, 2 * BANK)]
+
+        def load(pool, name, shape, dtype, src, **kw):
+            t = pool.tile(shape, dtype, name=name, **kw)
+            nc.sync.dma_start(out=t[:], in_=src)
+            return t
 
         def load_list(name, src):
             t = keep.tile([P, S // 16], U16, name=name)
             nc.sync.dma_start(t[:], src)
             return t
 
-        def load_weight(rows):
-            raw = ring.tile([P, PACK, BANK], F32, name="w_raw", bufs=4)
-            nc.sync.dma_start(out=raw[:], in_=rows.rearrange("(p j) c -> p j c", j=PACK))
-            return raw
+        def k_rows(w, a, cols):
+            return w[KP * a : KP * (a + 1), cols].rearrange("(p j) c -> p j c", j=PACK)
 
         def bank(n):
             return psum.tile([P, BANK], F32, name=f"bank{n}")
 
-        def quantize(name, grouped):
-            codes = keep.tile([P, BANK], U32, name=name + "_codes", align_bytes=64)
-            scales = keep.tile([P, BANK], U8, name=name + "_scales", align_bytes=64)
-            nc.vector.quantize_mx(out=codes[:].bitcast(FP8X4), scales=scales[:], in_=grouped[:])
+        def quantize(name, grouped, tag=""):
+            width = grouped.shape[1] // PACK
+            codes = keep.tile([P, width], U32, name=name + "_codes", tag=tag, align_bytes=64)
+            scales = keep.tile([P, width], U8, name=name + "_scales", align_bytes=64)
+            nc.vector.quantize_mx(out=codes[:].bitcast(FP8X4), scales=scales[:], in_=grouped)
             return codes, scales
 
-        def grouped_tile():
-            return ring.tile([P, BANK * PACK], BF16, name="grouped", bufs=4, align_bytes=64)
-
-        def group_w1(copy, raw):
-            g = grouped_tile()
+        def group_rows(copy, dst, rows):
             copy(
-                out=g[:].rearrange("p (t m j) -> p m t j", t=PACK, j=PACK),
-                in_=raw[:].rearrange("p j (m t) -> p m t j", t=PACK),
-            )
-            return g
-
-        def group_rows(copy, rows):
-            g = grouped_tile()
-            copy(
-                out=g[:].rearrange("p (c i j) -> p c j i", i=4, j=PACK),
+                out=dst.rearrange("p (c i j) -> p c j i", i=4, j=PACK),
                 in_=rows.rearrange("p j (c i) -> p c j i", i=4),
             )
+
+        def group_passes(copy, name, rows):
+            width = rows[0].shape[2] * PACK
+            g = keep.tile([P, 2 * width], BF16, name=name, align_bytes=64)
+            for a in range(2):
+                group_rows(copy, g[:, width * a : width * (a + 1)], rows[a])
             return g
 
         tab_s = keep.tile([P, T], U8, name="tab_s", align_bytes=64)
         nc.gpsimd.memset(tab_s[:].bitcast(I32), 0)
         for q in range(4):
-            nc.gpsimd.dma_start(
+            nc.scalar.dma_start(
                 out=tab_s[32 * q : 32 * q + 8, :].bitcast(I32),
                 in_=tab_scales[:, 4 * q : 4 * q + 4, :].bitcast(I32),
             )
@@ -83,52 +82,53 @@ def tile_list_returns_chute_grading_kernel(
         for t in pages + cages:
             nc.vector.memset(t[:], 0.0)
 
+        def load_w1_low(name, cols):
+            width = cols.stop - cols.start
+            return [load(keep, f"{name}{a}", [P, PACK, width], F32, k_rows(w1, a, cols)) for a in range(2)]
+
+        def load_big(shape, dtype, src):
+            return load(ring, "big", shape, dtype, src, bufs=4)
+
         idx = load_list("idx", offs)
-        w1_raw = {}
-        for a in range(2):
-            w1_raw[0, a] = load_weight(w1[KP * a : KP * (a + 1), 0:KP])
-        tab_w = []
-        for a in range(2):
-            t = keep.tile([P, T], I32, name=f"tab_w{a}")
-            nc.sync.dma_start(out=t[:], in_=tab_words[a].rearrange("p t i -> p (t i)").bitcast(I32))
-            tab_w.append(t)
+        w1_c0 = load_w1_low("w1_c0", slice(0, P))
+        tab_w = [load_big([P, T], I32, tab_words[a].rearrange("p t i -> p (t i)").bitcast(I32)) for a in range(2)]
+        w1_c1 = load_w1_low("w1_c1", slice(P, 2 * P))
+        wgs_low = load(keep, "wgs_low", [P, S], F32, wgs)
         idx2 = load_list("idx2", offs2)
-        wgs_sb = keep.tile([P, PACK * S], F32, name="wgs_sb")
-        for q in range(4):
-            nc.sync.dma_start(out=wgs_sb[32 * q : 32 * (q + 1), :], in_=wgs.rearrange("(m i) j -> m (i j)", i=PACK))
-        rest_sb = keep.tile([P, 2, PACK], F32, name="rest_sb")
-        nc.sync.dma_start(out=rest_sb[:], in_=rest.rearrange("(b p i) -> p b i", b=2, i=PACK))
-        gains_rows = gains.rearrange("(b p i) t -> b i p t", b=2, i=PACK)
+        w1_c23 = load_w1_low("w1_c23", slice(2 * P, 4 * P))
+        rest_low = keep.tile([P, PACK], F32, name="rest_low")
+        with nc.allow_non_contiguous_dma(reason="one value of rest for each partition"):
+            nc.sync.dma_start(out=rest_low[:], in_=rest[0:KP].rearrange("(c p) -> p c", p=P))
+        rest_high = load(keep, "rest_high", [P, PACK], F32, rest[KP : 2 * KP].rearrange("(p i) -> p i", i=PACK))
         gains_sb = {}
-
-        def load_gains(b, i):
-            t = keep.tile([P, T2], F32, name=f"gains{b}{i}")
-            nc.sync.dma_start(out=t[:], in_=gains_rows[b, i])
-            gains_sb[b, i] = t
-
-        load_gains(0, 0)
-        load_gains(0, 1)
-        for a in range(2):
-            w1_raw[1, a] = load_weight(w1[KP * a : KP * (a + 1), KP : 2 * KP])
-        load_gains(0, 2)
-        load_gains(0, 3)
+        for c in range(2):
+            gains_sb[c] = load(keep, f"gains{c}", [P, T2], F32, gains[P * c : P * (c + 1), :])
+        w1_high = [load_big([P, PACK, KP], F32, k_rows(w1, a, slice(KP, 2 * KP))) for a in range(2)]
+        for c in range(2, 4):
+            gains_sb[c] = load(keep, f"gains{c}", [P, T2], F32, gains[P * c : P * (c + 1), :])
+        wgs_high = keep.tile([P, PACK * S], F32, name="wgs_high")
+        for q in range(4):
+            nc.sync.dma_start(out=wgs_high[32 * q : 32 * (q + 1), :], in_=wgs.rearrange("(m i) j -> m (i j)", i=PACK))
 
         w1_q = {}
-        g0 = group_w1(nc.vector.tensor_copy, w1_raw[0, 0])
-        g1 = group_w1(nc.vector.tensor_copy, w1_raw[0, 1])
-        w1_q[0, 0] = quantize("w1_00", g0)
+        g = group_passes(nc.vector.tensor_copy, "w1_g0", [t[:] for t in w1_c0])
+        w1_q0 = quantize("w1_0", g[:])
         v_s = keep.tile([P, S], U8, name="v_s", align_bytes=64)
         nc.vector.tensor_copy(v_s[:], tab_s[:].indirect(idx[:]))
-        w1_q[0, 1] = quantize("w1_01", g1)
         v_w = []
         for a in range(2):
             t = keep.tile([P, S], U32, name=f"v_w{a}", align_bytes=64)
             nc.vector.tensor_copy(t[:], tab_w[a][:].bitcast(U32).indirect(idx[:]))
             v_w.append(t)
+        g = group_passes(nc.vector.tensor_copy, "w1_g1", [t[:] for t in w1_c1])
+        w1_q1 = quantize("w1_1", g[:])
+        for a in range(2):
+            w1_q[0, a] = (w1_q0, P * a)
+            w1_q[1, a] = (w1_q1, P * a)
 
-        w2_raw = [load_weight(w2[KP * b : KP * (b + 1), :]) for b in range(2)]
-        for i in range(PACK):
-            load_gains(1, i)
+        w2_raw = [load_big([P, PACK, N], F32, k_rows(w2, b, slice(0, N))) for b in range(2)]
+        gains_high = gains[KP : 2 * KP, :].rearrange("(p i) t -> i p t", i=PACK)
+        gains_sb[4] = load(keep, "gains4", [P, T2], F32, gains_high[0])
         w3_w = keep.tile([P, 2, 2 * N], U8, name="w3_w", align_bytes=64)
         nc.sync.dma_start(out=w3_w[:].bitcast(I32), in_=w3_words.rearrange("a p n -> p a n").bitcast(I32))
         for q in range(4):
@@ -136,119 +136,132 @@ def tile_list_returns_chute_grading_kernel(
                 out=w3_s[32 * q : 32 * q + 4, :, :].bitcast(I32),
                 in_=w3_scales[:, 4 * q : 4 * q + 4, :].rearrange("a r n -> r a n").bitcast(I32),
             )
+        gains_half = {}
+        for h in range(2):
+            for i in range(1, PACK):
+                gains_half[4 + i, h] = load(keep, f"gains{4 + i}{h}", [P, BANK], F32, gains_high[i][:, halves[h]])
         idx3 = load_list("idx3", offs3)
         idx4 = load_list("idx4", offs4)
-        exp_sb = keep.tile([P, N // P, S], F32, name="exp_sb")
-        nc.sync.dma_start(out=exp_sb[:], in_=expected.rearrange("(c p) m -> p c m", p=P))
-        wgo_sb = keep.tile([P, S], F32, name="wgo_sb")
-        nc.sync.dma_start(out=wgo_sb[:], in_=wgo)
+        exp_sb = load(keep, "exp_sb", [P, N // P, S], F32, expected.rearrange("(c p) m -> p c m", p=P))
+        wgo_sb = load(keep, "wgo_sb", [P, S], F32, wgo)
 
         h_abs = {}
 
         def first_product(n):
-            b, i = divmod(n, PACK)
-            acc = bank(4 + i)
-            cols = slice(P * i, P * (i + 1))
+            acc = bank(4 + n % 4)
             for a in range(2):
-                codes, scales = w1_q[b, a]
+                (codes, scales), c0 = w1_q[n, a]
                 nc.tensor.matmul_mx(
                     out=acc[:],
-                    lhsT=codes[:, cols].bitcast(FP8X4),
-                    lhsT_scale=scales[:, cols],
+                    lhsT=codes[:, c0 : c0 + P].bitcast(FP8X4),
+                    lhsT_scale=scales[:, c0 : c0 + P],
                     rhs=v_w[a][:].bitcast(FP8X4),
                     rhs_scale=v_s[4 * a : P, :],
                     start=(a == 0),
                     stop=(a == 1),
                 )
-            t = ring.tile([P, S], F32, name="h_abs", bufs=4)
+            if n == 6:
+                t = keep.tile([P, S], F32, name="h_abs6", tag="after6", align_bytes=64)
+            else:
+                t = ring.tile([P, S], F32, name="h_abs", bufs=4)
             nc.scalar.activation(out=t[:], in_=acc[:], func=ACT.Abs)
             h_abs[n] = t
 
         z_rows = [keep.tile([P, PACK, T2], BF16, name=f"z_rows{b}") for b in range(2)]
 
         def place(n):
-            i = n % PACK
-            nc.vector.tensor_tensor(
-                pages[n % 3][:].indirect(idx2[:]), h_abs[n][:], wgs_sb[:, S * i : S * (i + 1)], ALU.mult
-            )
+            weight = wgs_low[:] if n < 4 else wgs_high[:, S * (n - 4) : S * (n - 3)]
+            nc.vector.tensor_tensor(pages[n % 3][:].indirect(idx2[:]), h_abs[n][:], weight, ALU.mult)
 
-        def make_z(n, cols):
-            b, i = divmod(n, PACK)
-            nc.vector.scalar_tensor_tensor(
-                out=z_rows[b][:, i, cols],
-                in0=pages[n % 3][:, cols],
-                scalar=rest_sb[:, b, i : i + 1],
-                in1=gains_sb[b, i][:, cols],
-                op0=ALU.add,
-                op1=ALU.mult,
-            )
+        def make_z(dst, page, level, gain):
+            nc.vector.scalar_tensor_tensor(out=dst, in0=page, scalar=level, in1=gain, op0=ALU.add, op1=ALU.mult)
 
-        halves = [slice(0, BANK), slice(BANK, 2 * BANK)]
-        whole = slice(0, T2)
-        z_q = {}
-        w2_q = {}
+        def make_z_low(c):
+            z = ring.tile([P, T2], BF16, name="z_low", bufs=4)
+            make_z(z[:], pages[c % 3][:], rest_low[:, c : c + 1], gains_sb[c][:])
+            nc.gpsimd.dma_start(out=z_rows[0][32 * c : 32 * (c + 1), :, :], in_=z[:])
 
-        for n in range(4):
-            first_product(n)
-        w1_g = [group_w1(nc.scalar.copy, w1_raw[1, a]) for a in range(2)]
+        def make_z_high(n, cols, gain):
+            i = n - 4
+            make_z(z_rows[1][:, i, cols], pages[n % 3][:, cols], rest_high[:, i : i + 1], gain)
+
+        first_product(0)
+        first_product(1)
+        g = group_passes(nc.scalar.copy, "w1_g23", [t[:] for t in w1_c23])
         place(0)
-        place(1)
-        make_z(0, whole)
-        place(2)
-        make_z(1, whole)
+        w1_q23 = quantize("w1_23", g[:])
+        for c in (2, 3):
+            for a in range(2):
+                w1_q[c, a] = (w1_q23, 2 * P * a + P * (c - 2))
+            first_product(c)
+        g = ring.tile([P, 2 * KP * PACK], BF16, name="wide", bufs=1, align_bytes=64)
         for a in range(2):
-            w1_q[1, a] = quantize(f"w1_1{a}", w1_g[a])
+            nc.scalar.copy(
+                out=g[:, KP * PACK * a : KP * PACK * (a + 1)].rearrange("p (t m j) -> p m t j", t=PACK, j=PACK),
+                in_=w1_high[a][:].rearrange("p j (m t) -> p m t j", t=PACK),
+            )
+        place(1)
+        make_z_low(0)
+        place(2)
+        make_z_low(1)
+        w1_qh = quantize("w1_h", g[:])
         place(3)
         for n in range(4, 8):
+            for a in range(2):
+                w1_q[n, a] = (w1_qh, KP * a + P * (n - 4))
             first_product(n)
-        make_z(2, whole)
-        w2_g = [group_rows(nc.scalar.copy, w2_raw[b][:]) for b in range(2)]
-        place(4)
-        make_z(3, whole)
-        z_g = [group_rows(nc.scalar.copy, z_rows[0][:, :, h]) for h in halves]
-        for b in range(2):
-            w2_q[b] = quantize(f"w2_{b}", w2_g[b])
-        place(5)
-        make_z(4, whole)
-        place(6)
-        make_z(5, whole)
-        for h in range(2):
-            z_q[0, h] = quantize(f"z_0{h}", z_g[h])
-        place(7)
-        make_z(6, whole)
-        make_z(7, halves[0])
-        make_z(7, halves[1])
-        z_g = [
-            group_rows(nc.scalar.copy, z_rows[1][:, :, halves[0]]),
-            group_rows(nc.vector.tensor_copy, z_rows[1][:, :, halves[1]]),
+        make_z_low(2)
+        w2_g = [
+            group_passes(nc.scalar.copy, f"w2_g{u}", [t[:, :, 2 * P * u : 2 * P * (u + 1)] for t in w2_raw])
+            for u in range(2)
         ]
-        z_q[1, 1] = quantize("z_11", z_g[1])
-        z_q[1, 0] = quantize("z_10", z_g[0])
+        place(4)
+        make_z_low(3)
+        g = ring.tile([P, T2 * PACK], BF16, name="wide", bufs=1, align_bytes=64)
+        for h in range(2):
+            group_rows(nc.scalar.copy, g[:, KP * PACK * h : KP * PACK * (h + 1)], z_rows[0][:, :, halves[h]])
+        w2_q = [quantize("w2_0", w2_g[0][:])]
+        place(5)
+        place(6)
+        make_z_high(4, slice(0, T2), gains_sb[4][:])
+        place(7)
+        z_q0 = quantize("z_0", g[:], tag="after6")
+        z_q = {(0, h): (z_q0, BANK * h) for h in range(2)}
+        for h in range(2):
+            for n in range(5, 8):
+                make_z_high(n, halves[h], gains_half[n, h][:])
+        g0 = keep.tile([P, BANK * PACK], BF16, name="z_g10", align_bytes=64)
+        g1 = keep.tile([P, BANK * PACK], BF16, name="z_g11", tag="late", align_bytes=64)
+        group_rows(nc.scalar.copy, g0[:], z_rows[1][:, :, halves[0]])
+        group_rows(nc.vector.tensor_copy, g1[:], z_rows[1][:, :, halves[1]])
+        z_q[1, 0] = (quantize("z_10", g0[:]), 0)
+        z_q[1, 1] = (quantize("z_11", g1[:]), 0)
+        w2_q.append(quantize("w2_1", w2_g[1][:], tag="late"))
 
         accs = {}
 
         def second_pass(c, h, b):
-            cols = slice(P * c, P * (c + 1))
             if b == 0:
                 accs[c, h] = (bank(4 * (c % 2) + 2 * h), bank(4 * (c % 2) + 2 * h + 1))
             ya, yb = accs[c, h]
-            z_codes, z_scales = z_q[b, h]
+            (z_codes, z_scales), t0 = z_q[b, h]
             nc.tensor.matmul_mx(
                 out=yb[:],
                 lhsT=w3_w[:, b, 2 * P * c : 2 * P * (c + 1)].bitcast(FP4X4),
-                lhsT_scale=w3_s[:, b, cols],
-                rhs=z_codes[:].bitcast(FP8X4),
-                rhs_scale=z_scales[:],
+                lhsT_scale=w3_s[:, b, P * c : P * (c + 1)],
+                rhs=z_codes[:, t0 : t0 + BANK].bitcast(FP8X4),
+                rhs_scale=z_scales[:, t0 : t0 + BANK],
                 start=(b == 0),
                 stop=(b == 1),
             )
-            codes, scales = w2_q[b]
+            codes, scales = w2_q[c // 2]
+            c0 = 2 * P * b + P * (c % 2)
             nc.tensor.matmul_mx(
                 out=ya[:],
-                lhsT=codes[:, cols].bitcast(FP8X4),
-                lhsT_scale=scales[:, cols],
-                rhs=z_codes[:].bitcast(FP8X4),
-                rhs_scale=z_scales[:],
+                lhsT=codes[:, c0 : c0 + P].bitcast(FP8X4),
+                lhsT_scale=scales[:, c0 : c0 + P],
+                rhs=z_codes[:, t0 : t0 + BANK].bitcast(FP8X4),
+                rhs_scale=z_scales[:, t0 : t0 + BANK],
                 start=(b == 0),
                 stop=(b == 1),
             )
@@ -257,14 +270,13 @@ def tile_list_returns_chute_grading_kernel(
         x_sb = {}
 
         def scores(c):
-            for h in (1, 0):
-                second_pass(c, h, 0)
-            for h in (1, 0):
-                second_pass(c, h, 1)
+            for b in range(2):
+                for h in range(2):
+                    second_pass(c, h, b)
             y = ring.tile([P, T2], F32, name="y")
-            for h in (1, 0):
+            for h in range(2):
                 ya, yb = accs[c, h]
-                t = ring.tile([P, BANK], F32, name="yb_sb", bufs=4)
+                t = ring.tile([P, BANK], F32, name="yb_sb", bufs=3)
                 nc.scalar.copy(out=t[:], in_=yb[:])
                 nc.vector.tensor_tensor(y[:, halves[h]], ya[:], t[:], ALU.mult)
             y_sb[c] = y

@@ -57,8 +57,8 @@ def tile_list_returns_chute_grading_kernel(
 
         def group_rows(copy, dst, rows):
             copy(
-                out=dst.rearrange("p (c i j) -> p c j i", i=4, j=PACK),
-                in_=rows.rearrange("p j (c i) -> p c j i", i=4),
+                out=dst.rearrange("p (c j) -> p c j", j=PACK),
+                in_=rows.rearrange("p j c -> p c j"),
             )
 
         def group_passes(copy, name, rows):
@@ -77,9 +77,9 @@ def tile_list_returns_chute_grading_kernel(
             )
         w3_s = keep.tile([P, 2, N], U8, name="w3_s", align_bytes=64)
         nc.vector.memset(w3_s[:].bitcast(I32), 0)
-        pages = [keep.tile([P, T2], F32, name=f"page{n}") for n in range(3)]
+        pages = [keep.tile([P, T2], F32, name=f"page{n}") for n in range(4)]
         cages = [keep.tile([P, T2], F32, name=f"cage{n}") for n in range(2)]
-        for t in pages + cages:
+        for t in pages[:2]:
             nc.vector.memset(t[:], 0.0)
 
         def load_w1_low(name, cols):
@@ -96,9 +96,9 @@ def tile_list_returns_chute_grading_kernel(
         wgs_low = load(keep, "wgs_low", [P, S], F32, wgs)
         idx2 = load_list("idx2", offs2)
         w1_c23 = load_w1_low("w1_c23", slice(2 * P, 4 * P))
-        rest_low = keep.tile([P, PACK], F32, name="rest_low")
+        rest_low = keep.tile([P, PACK, 8], F32, name="rest_low")
         with nc.allow_non_contiguous_dma(reason="one value of rest for each partition"):
-            nc.sync.dma_start(out=rest_low[:], in_=rest[0:KP].rearrange("(c p) -> p c", p=P))
+            nc.sync.dma_start(out=rest_low[:, :, 0], in_=rest[0:KP].rearrange("(c p) -> p c", p=P))
         rest_high = load(keep, "rest_high", [P, PACK], F32, rest[KP : 2 * KP].rearrange("(p i) -> p i", i=PACK))
         gains_sb = {}
         for c in range(2):
@@ -122,13 +122,14 @@ def tile_list_returns_chute_grading_kernel(
             v_w.append(t)
         g = group_passes(nc.vector.tensor_copy, "w1_g1", [t[:] for t in w1_c1])
         w1_q1 = quantize("w1_1", g[:])
+        for t in pages[2:] + cages:
+            nc.vector.memset(t[:], 0.0)
         for a in range(2):
             w1_q[0, a] = (w1_q0, P * a)
             w1_q[1, a] = (w1_q1, P * a)
 
         w2_raw = [load_big([P, PACK, N], F32, k_rows(w2, b, slice(0, N))) for b in range(2)]
         gains_high = gains[KP : 2 * KP, :].rearrange("(p i) t -> i p t", i=PACK)
-        gains_sb[4] = load(keep, "gains4", [P, T2], F32, gains_high[0])
         w3_w = keep.tile([P, 2, 2 * N], U8, name="w3_w", align_bytes=64)
         nc.sync.dma_start(out=w3_w[:].bitcast(I32), in_=w3_words.rearrange("a p n -> p a n").bitcast(I32))
         for q in range(4):
@@ -136,13 +137,8 @@ def tile_list_returns_chute_grading_kernel(
                 out=w3_s[32 * q : 32 * q + 4, :, :].bitcast(I32),
                 in_=w3_scales[:, 4 * q : 4 * q + 4, :].rearrange("a r n -> r a n").bitcast(I32),
             )
-        gains_half = {}
-        for h in range(2):
-            for i in range(1, PACK):
-                gains_half[4 + i, h] = load(keep, f"gains{4 + i}{h}", [P, BANK], F32, gains_high[i][:, halves[h]])
         idx3 = load_list("idx3", offs3)
         idx4 = load_list("idx4", offs4)
-        exp_sb = load(keep, "exp_sb", [P, N // P, S], F32, expected.rearrange("(c p) m -> p c m", p=P))
         wgo_sb = load(keep, "wgo_sb", [P, S], F32, wgo)
 
         h_abs = {}
@@ -167,23 +163,24 @@ def tile_list_returns_chute_grading_kernel(
             nc.scalar.activation(out=t[:], in_=acc[:], func=ACT.Abs)
             h_abs[n] = t
 
-        z_rows = [keep.tile([P, PACK, T2], BF16, name=f"z_rows{b}") for b in range(2)]
+        z_rows = [keep.tile([P, PACK, T2], BF16, name="z_rows0")]
 
         def place(n):
             weight = wgs_low[:] if n < 4 else wgs_high[:, S * (n - 4) : S * (n - 3)]
-            nc.vector.tensor_tensor(pages[n % 3][:].indirect(idx2[:]), h_abs[n][:], weight, ALU.mult)
+            nc.vector.tensor_tensor(pages[n % 4][:].indirect(idx2[:]), h_abs[n][:], weight, ALU.mult)
 
         def make_z(dst, page, level, gain):
             nc.vector.scalar_tensor_tensor(out=dst, in0=page, scalar=level, in1=gain, op0=ALU.add, op1=ALU.mult)
 
+        z_low = keep.tile([P, PACK, T2], BF16, name="z_low")
+
         def make_z_low(c):
-            z = ring.tile([P, T2], BF16, name="z_low", bufs=4)
-            make_z(z[:], pages[c % 3][:], rest_low[:, c : c + 1], gains_sb[c][:])
-            nc.gpsimd.dma_start(out=z_rows[0][32 * c : 32 * (c + 1), :, :], in_=z[:])
+            make_z(z_low[:, c, :], pages[c][:], rest_low[:, c, 0:1], gains_sb[c][:])
+            nc.sync.dma_start(out=z_rows[0][32 * c : 32 * (c + 1), :, :], in_=z_low[:, c, :])
 
         def make_z_high(n, cols, gain):
             i = n - 4
-            make_z(z_rows[1][:, i, cols], pages[n % 3][:, cols], rest_high[:, i : i + 1], gain)
+            make_z(z_rows[1][:, i, cols], pages[n % 4][:, cols], rest_high[:, i : i + 1], gain)
 
         first_product(0)
         first_product(1)
@@ -215,21 +212,24 @@ def tile_list_returns_chute_grading_kernel(
             group_passes(nc.scalar.copy, f"w2_g{u}", [t[:, :, 2 * P * u : 2 * P * (u + 1)] for t in w2_raw])
             for u in range(2)
         ]
-        place(4)
         make_z_low(3)
+        for i in range(PACK):
+            gains_sb[4 + i] = load(keep, f"gains{i}", [P, T2], F32, gains_high[i])
+        exp_sb = load(keep, "z_low", [P, N // P, S], F32, expected.rearrange("(c p) m -> p c m", p=P))
+        place(4)
         g = ring.tile([P, T2 * PACK], BF16, name="wide", bufs=1, align_bytes=64)
         for h in range(2):
             group_rows(nc.scalar.copy, g[:, KP * PACK * h : KP * PACK * (h + 1)], z_rows[0][:, :, halves[h]])
         w2_q = [quantize("w2_0", w2_g[0][:])]
         place(5)
         place(6)
-        make_z_high(4, slice(0, T2), gains_sb[4][:])
         place(7)
         z_q0 = quantize("z_0", g[:], tag="after6")
         z_q = {(0, h): (z_q0, BANK * h) for h in range(2)}
+        z_rows.append(ring.tile([P, PACK, T2], BF16, name="wide", bufs=1, align_bytes=64))
         for h in range(2):
-            for n in range(5, 8):
-                make_z_high(n, halves[h], gains_half[n, h][:])
+            for n in range(4, 8):
+                make_z_high(n, halves[h], gains_sb[n][:, halves[h]])
         g0 = keep.tile([P, BANK * PACK], BF16, name="z_g10", align_bytes=64)
         g1 = keep.tile([P, BANK * PACK], BF16, name="z_g11", tag="late", align_bytes=64)
         group_rows(nc.scalar.copy, g0[:], z_rows[1][:, :, halves[0]])

@@ -1,6 +1,7 @@
 from contextlib import ExitStack
 
 import concourse.mybir as mybir
+from concourse.masks import make_identity
 
 K, T, S, H, T2, N = 1024, 2048, 512, 1024, 1024, 512
 FLOPS = 2 * K * H * S + 2 * 2 * H * N * T2
@@ -19,7 +20,15 @@ ACT = mybir.ActivationFunctionType
 P = 128
 PACK = 4
 KP = P * PACK
+PASSES = 2
 BANK = 512
+QUAD = 32
+QUADS = P // QUAD
+SCALE_ROWS = 4
+LOW = 4
+HALVES = [slice(0, BANK), slice(BANK, 2 * BANK)]
+ALIGN = 64
+VECTOR_SLOTS = T2 // 4
 
 
 def tile_list_returns_chute_grading_kernel(
@@ -30,271 +39,284 @@ def tile_list_returns_chute_grading_kernel(
         keep = ctx.enter_context(tc.tile_pool(name="keep", bufs=1))
         ring = ctx.enter_context(tc.tile_pool(name="ring", bufs=2))
         psum = ctx.enter_context(tc.psum_pool(name="psum", bufs=1))
-        halves = [slice(0, BANK), slice(BANK, 2 * BANK)]
 
-        def load(pool, name, shape, dtype, src, **kw):
-            t = pool.tile(shape, dtype, name=name, **kw)
-            nc.sync.dma_start(out=t[:], in_=src)
-            return t
+        def load(name, shape, dtype, src):
+            loaded = keep.tile(shape, dtype, name=name)
+            nc.sync.dma_start(out=loaded[:], in_=src)
+            return loaded
 
         def load_list(name, src):
-            t = keep.tile([P, S // 16], U16, name=name)
-            nc.sync.dma_start(t[:], src)
-            return t
+            loaded = keep.tile([P, S // 16], U16, name=name)
+            nc.sync.dma_start(loaded[:], src)
+            return loaded
 
-        def k_rows(w, a, cols):
-            return w[KP * a : KP * (a + 1), cols].rearrange("(p j) c -> p j c", j=PACK)
+        def pass_rows(weight, a, cols):
+            return weight[KP * a : KP * (a + 1), cols].rearrange("(p i) c -> p i c", i=PACK)
 
-        def bank(n):
-            return psum.tile([P, BANK], F32, name=f"bank{n}")
+        def bank(index):
+            return psum.tile([P, BANK], F32, name=f"bank{index}")
 
         def quantize(name, grouped, tag=""):
             width = grouped.shape[1] // PACK
-            codes = keep.tile([P, width], U32, name=name + "_codes", tag=tag, align_bytes=64)
-            scales = keep.tile([P, width], U8, name=name + "_scales", align_bytes=64)
+            codes = keep.tile([P, width], U32, name=name + "_codes", tag=tag, align_bytes=ALIGN)
+            scales = keep.tile([P, width], U8, name=name + "_scales", align_bytes=ALIGN)
             nc.vector.quantize_mx(out=codes[:].bitcast(FP8X4), scales=scales[:], in_=grouped)
             return codes, scales
 
         def group_rows(copy, dst, rows):
-            copy(
-                out=dst.rearrange("p (c j) -> p c j", j=PACK),
-                in_=rows.rearrange("p j c -> p c j"),
-            )
+            copy(out=dst.rearrange("p (c i) -> p c i", i=PACK), in_=rows.rearrange("p i c -> p c i"))
 
         def group_passes(copy, name, rows):
             width = rows[0].shape[2] * PACK
-            g = keep.tile([P, 2 * width], BF16, name=name, align_bytes=64)
-            for a in range(2):
-                group_rows(copy, g[:, width * a : width * (a + 1)], rows[a])
-            return g
+            grouped = keep.tile([P, PASSES * width], BF16, name=name, align_bytes=ALIGN)
+            for a in range(PASSES):
+                group_rows(copy, grouped[:, width * a : width * (a + 1)], rows[a])
+            return grouped
 
-        tab_s = keep.tile([P, T], U8, name="tab_s", align_bytes=64)
+        tab_s = keep.tile([P, T], U8, name="tab_s", align_bytes=ALIGN)
         nc.gpsimd.memset(tab_s[:].bitcast(I32), 0)
-        for q in range(4):
+        for q in range(QUADS):
             nc.scalar.dma_start(
-                out=tab_s[32 * q : 32 * q + 8, :].bitcast(I32),
-                in_=tab_scales[:, 4 * q : 4 * q + 4, :].bitcast(I32),
+                out=tab_s[QUAD * q : QUAD * q + PASSES * SCALE_ROWS, :].bitcast(I32),
+                in_=tab_scales[:, SCALE_ROWS * q : SCALE_ROWS * (q + 1), :].bitcast(I32),
             )
-        w3_s = keep.tile([P, 2, N], U8, name="w3_s", align_bytes=64)
+        w3_s = keep.tile([P, PASSES, N], U8, name="w3_s", align_bytes=ALIGN)
         nc.vector.memset(w3_s[:].bitcast(I32), 0)
-        pages = [keep.tile([P, T2], F32, name=f"page{n}") for n in range(4)]
-        cages = [keep.tile([P, T2], F32, name=f"cage{n}") for n in range(2)]
-        for t in pages[:2]:
-            nc.vector.memset(t[:], 0.0)
+        identity = keep.tile([P, P], F32, name="identity")
+        make_identity(nc, identity[:])
+        rest_rows = keep.tile([P, P], F32, name="rest_rows")
+        nc.vector.memset(rest_rows[:], 0.0)
+        pages = [keep.tile([P, T2], F32, name=f"page{index}") for index in range(LOW)]
+        cages = [keep.tile([P, T2], F32, name=f"cage{index}") for index in range(2)]
+        for window in pages + cages:
+            nc.vector.memset(window[:], 0.0)
 
-        def load_w1_low(name, cols):
+        def load_w1(name, cols):
             width = cols.stop - cols.start
-            return [load(keep, f"{name}{a}", [P, PACK, width], F32, k_rows(w1, a, cols)) for a in range(2)]
+            return [load(f"{name}{a}", [P, PACK, width], F32, pass_rows(w1, a, cols)) for a in range(PASSES)]
 
         def load_big(shape, dtype, src):
-            return load(ring, "big", shape, dtype, src, bufs=4)
+            loaded = ring.tile(shape, dtype, name="big", bufs=2 * PASSES)
+            nc.sync.dma_start(out=loaded[:], in_=src)
+            return loaded
 
         idx = load_list("idx", offs)
-        w1_c0 = load_w1_low("w1_c0", slice(0, P))
-        tab_w = [load_big([P, T], I32, tab_words[a].rearrange("p t i -> p (t i)").bitcast(I32)) for a in range(2)]
-        w1_c1 = load_w1_low("w1_c1", slice(P, 2 * P))
-        wgs_low = load(keep, "wgs_low", [P, S], F32, wgs)
+        w1_slab0 = load_w1("w1_slab0_", slice(0, P))
+        tab_w = [
+            load_big([P, T], I32, tab_words[a].rearrange("p t i -> p (t i)").bitcast(I32)) for a in range(PASSES)
+        ]
+        w1_slab1 = load_w1("w1_slab1_", slice(P, 2 * P))
+        wgs_low = load("wgs_low", [P, S], F32, wgs)
         idx2 = load_list("idx2", offs2)
-        w1_c23 = load_w1_low("w1_c23", slice(2 * P, 4 * P))
-        rest_low = keep.tile([P, PACK, 8], F32, name="rest_low")
-        with nc.allow_non_contiguous_dma(reason="one value of rest for each partition"):
-            nc.sync.dma_start(out=rest_low[:, :, 0], in_=rest[0:KP].rearrange("(c p) -> p c", p=P))
-        rest_high = load(keep, "rest_high", [P, PACK], F32, rest[KP : 2 * KP].rearrange("(p i) -> p i", i=PACK))
+        w1_slab23 = load_w1("w1_slab23_", slice(2 * P, KP))
+        nc.sync.dma_start(out=rest_rows[0:LOW, :], in_=rest[0:KP].rearrange("(n p) -> n p", p=P))
+        rest_high = load("rest_high", [P, PACK], F32, rest[KP:H].rearrange("(p i) -> p i", i=PACK))
         gains_sb = {}
-        for c in range(2):
-            gains_sb[c] = load(keep, f"gains{c}", [P, T2], F32, gains[P * c : P * (c + 1), :])
-        w1_high = [load_big([P, PACK, KP], F32, k_rows(w1, a, slice(KP, 2 * KP))) for a in range(2)]
-        for c in range(2, 4):
-            gains_sb[c] = load(keep, f"gains{c}", [P, T2], F32, gains[P * c : P * (c + 1), :])
+        w1_high = []
+        for a in range(PASSES):
+            w1_high.append(load_big([P, PACK, KP], F32, pass_rows(w1, a, slice(KP, H))))
+            gains_sb[a] = load(f"gains{a}", [P, T2], F32, gains[P * a : P * (a + 1), :])
+        for n in range(PASSES, LOW):
+            gains_sb[n] = load(f"gains{n}", [P, T2], F32, gains[P * n : P * (n + 1), :])
         wgs_high = keep.tile([P, PACK * S], F32, name="wgs_high")
-        for q in range(4):
-            nc.sync.dma_start(out=wgs_high[32 * q : 32 * (q + 1), :], in_=wgs.rearrange("(m i) j -> m (i j)", i=PACK))
+        for q in range(QUADS):
+            nc.sync.dma_start(
+                out=wgs_high[QUAD * q : QUAD * (q + 1), :], in_=wgs.rearrange("(m s) j -> m (s j)", s=PACK)
+            )
 
         w1_q = {}
-        g = group_passes(nc.vector.tensor_copy, "w1_g0", [t[:] for t in w1_c0])
-        w1_q0 = quantize("w1_0", g[:])
-        v_s = keep.tile([P, S], U8, name="v_s", align_bytes=64)
+        w1_q0 = quantize("w1_0", group_passes(nc.vector.tensor_copy, "w1_g0", [t[:] for t in w1_slab0])[:])
+        v_s = keep.tile([P, S], U8, name="v_s", align_bytes=ALIGN)
         nc.vector.tensor_copy(v_s[:], tab_s[:].indirect(idx[:]))
         v_w = []
-        for a in range(2):
-            t = keep.tile([P, S], U32, name=f"v_w{a}", align_bytes=64)
-            nc.vector.tensor_copy(t[:], tab_w[a][:].bitcast(U32).indirect(idx[:]))
-            v_w.append(t)
-        g = group_passes(nc.vector.tensor_copy, "w1_g1", [t[:] for t in w1_c1])
-        w1_q1 = quantize("w1_1", g[:])
-        for t in pages[2:] + cages:
-            nc.vector.memset(t[:], 0.0)
-        for a in range(2):
+        for a in range(PASSES):
+            words = keep.tile([P, S], U32, name=f"v_w{a}", align_bytes=ALIGN)
+            nc.vector.tensor_copy(words[:], tab_w[a][:].bitcast(U32).indirect(idx[:]))
+            v_w.append(words)
+        w1_q1 = quantize("w1_1", group_passes(nc.vector.tensor_copy, "w1_g1", [t[:] for t in w1_slab1])[:])
+        for a in range(PASSES):
             w1_q[0, a] = (w1_q0, P * a)
             w1_q[1, a] = (w1_q1, P * a)
 
-        w2_raw = [load_big([P, PACK, N], F32, k_rows(w2, b, slice(0, N))) for b in range(2)]
-        gains_high = gains[KP : 2 * KP, :].rearrange("(p i) t -> i p t", i=PACK)
-        w3_w = keep.tile([P, 2, 2 * N], U8, name="w3_w", align_bytes=64)
-        nc.sync.dma_start(out=w3_w[:].bitcast(I32), in_=w3_words.rearrange("a p n -> p a n").bitcast(I32))
-        for q in range(4):
-            nc.sync.dma_start(
-                out=w3_s[32 * q : 32 * q + 4, :, :].bitcast(I32),
-                in_=w3_scales[:, 4 * q : 4 * q + 4, :].rearrange("a r n -> r a n").bitcast(I32),
-            )
-        idx3 = load_list("idx3", offs3)
-        idx4 = load_list("idx4", offs4)
-        wgo_sb = load(keep, "wgo_sb", [P, S], F32, wgo)
+        w2_raw = [load_big([P, PACK, N], F32, pass_rows(w2, a, slice(0, N))) for a in range(PASSES)]
 
+        before_w1_high, before_z_low = 2, 6
         h_abs = {}
 
         def first_product(n):
-            acc = bank(4 + n % 4)
-            for a in range(2):
-                (codes, scales), c0 = w1_q[n, a]
+            acc = bank(LOW + n % LOW)
+            for a in range(PASSES):
+                (codes, scales), first = w1_q[n, a]
                 nc.tensor.matmul_mx(
                     out=acc[:],
-                    lhsT=codes[:, c0 : c0 + P].bitcast(FP8X4),
-                    lhsT_scale=scales[:, c0 : c0 + P],
+                    lhsT=codes[:, first : first + P].bitcast(FP8X4),
+                    lhsT_scale=scales[:, first : first + P],
                     rhs=v_w[a][:].bitcast(FP8X4),
-                    rhs_scale=v_s[4 * a : P, :],
+                    rhs_scale=v_s[SCALE_ROWS * a : P, :],
                     start=(a == 0),
-                    stop=(a == 1),
+                    stop=(a == PASSES - 1),
                 )
-            if n == 6:
-                t = keep.tile([P, S], F32, name="h_abs6", tag="after6", align_bytes=64)
+            if n in (before_w1_high, before_z_low):
+                h_abs[n] = keep.tile([P, S], F32, name=f"h_abs{n}", tag=f"after{n}", align_bytes=ALIGN)
             else:
-                t = ring.tile([P, S], F32, name="h_abs", bufs=4)
-            nc.scalar.activation(out=t[:], in_=acc[:], func=ACT.Abs)
-            h_abs[n] = t
-
-        z_rows = [keep.tile([P, PACK, T2], BF16, name="z_rows0")]
+                h_abs[n] = ring.tile([P, S], F32, name="h_abs", bufs=LOW)
+            nc.scalar.activation(out=h_abs[n][:], in_=acc[:], func=ACT.Abs)
 
         def place(n):
-            weight = wgs_low[:] if n < 4 else wgs_high[:, S * (n - 4) : S * (n - 3)]
-            nc.vector.tensor_tensor(pages[n % 4][:].indirect(idx2[:]), h_abs[n][:], weight, ALU.mult)
+            weight = wgs_low[:] if n < LOW else wgs_high[:, S * (n - LOW) : S * (n - LOW + 1)]
+            nc.vector.tensor_tensor(pages[n % LOW][:].indirect(idx2[:]), h_abs[n][:], weight, ALU.mult)
 
         def make_z(dst, page, level, gain):
             nc.vector.scalar_tensor_tensor(out=dst, in0=page, scalar=level, in1=gain, op0=ALU.add, op1=ALU.mult)
 
-        z_low = keep.tile([P, PACK, T2], BF16, name="z_low")
+        z_rows_low = keep.tile([P, PACK, T2], BF16, name="z_rows_low")
+        z_slabs = keep.tile([P, LOW, T2], BF16, name="z_slabs")
 
-        def make_z_low(c):
-            make_z(z_low[:, c, :], pages[c][:], rest_low[:, c, 0:1], gains_sb[c][:])
-            nc.sync.dma_start(out=z_rows[0][32 * c : 32 * (c + 1), :, :], in_=z_low[:, c, :])
-
-        def make_z_high(n, cols, gain):
-            i = n - 4
-            make_z(z_rows[1][:, i, cols], pages[n % 4][:, cols], rest_high[:, i : i + 1], gain)
+        def make_z_low(n):
+            make_z(z_slabs[:, n, :], pages[n][:], rest_low[:, n : n + 1], gains_sb[n][:])
+            nc.sync.dma_start(out=z_rows_low[QUAD * n : QUAD * (n + 1), :, :], in_=z_slabs[:, n, :])
 
         first_product(0)
         first_product(1)
-        g = group_passes(nc.scalar.copy, "w1_g23", [t[:] for t in w1_c23])
+        rest_turned = bank(LOW + 1)
+        nc.tensor.transpose(rest_turned[:, 0:P], rest_rows[:], identity[:])
+        rest_low = keep.tile([P, LOW], F32, name="rest_low")
+        nc.scalar.copy(out=rest_low[:], in_=rest_turned[:, 0:LOW])
+        w1_g23 = group_passes(nc.scalar.copy, "w1_g23", [t[:] for t in w1_slab23])
         place(0)
-        w1_q23 = quantize("w1_23", g[:])
-        for c in (2, 3):
-            for a in range(2):
-                w1_q[c, a] = (w1_q23, 2 * P * a + P * (c - 2))
-            first_product(c)
-        g = ring.tile([P, 2 * KP * PACK], BF16, name="wide", bufs=1, align_bytes=64)
-        for a in range(2):
+        w1_q23 = quantize("w1_23", w1_g23[:])
+        for n in (2, 3):
+            for a in range(PASSES):
+                w1_q[n, a] = (w1_q23, 2 * P * a + P * (n - 2))
+            first_product(n)
+
+        w1_gh = keep.tile([P, PASSES * KP * PACK], BF16, name="wide", align_bytes=ALIGN)
+        for a in range(PASSES):
             nc.scalar.copy(
-                out=g[:, KP * PACK * a : KP * PACK * (a + 1)].rearrange("p (t m j) -> p m t j", t=PACK, j=PACK),
-                in_=w1_high[a][:].rearrange("p j (m t) -> p m t j", t=PACK),
+                out=w1_gh[:, KP * PACK * a : KP * PACK * (a + 1)].rearrange("p (s m i) -> p m s i", s=PACK, i=PACK),
+                in_=w1_high[a][:].rearrange("p i (m s) -> p m s i", s=PACK),
             )
+
         place(1)
         make_z_low(0)
         place(2)
         make_z_low(1)
-        w1_qh = quantize("w1_h", g[:])
+        w1_qh = quantize("w1_h", w1_gh[:], tag=f"after{before_w1_high}")
         place(3)
-        for n in range(4, 8):
-            for a in range(2):
-                w1_q[n, a] = (w1_qh, KP * a + P * (n - 4))
+        for n in range(LOW, 2 * LOW):
+            for a in range(PASSES):
+                w1_q[n, a] = (w1_qh, KP * a + P * (n - LOW))
             first_product(n)
         make_z_low(2)
         w2_g = [
-            group_passes(nc.scalar.copy, f"w2_g{u}", [t[:, :, 2 * P * u : 2 * P * (u + 1)] for t in w2_raw])
-            for u in range(2)
+            group_passes(nc.scalar.copy, f"w2_g{pair}", [t[:, :, 2 * P * pair : 2 * P * (pair + 1)] for t in w2_raw])
+            for pair in range(2)
         ]
         make_z_low(3)
-        for i in range(PACK):
-            gains_sb[4 + i] = load(keep, f"gains{i}", [P, T2], F32, gains_high[i])
-        exp_sb = load(keep, "z_low", [P, N // P, S], F32, expected.rearrange("(c p) m -> p c m", p=P))
+
+        gains_high = gains[KP:H, :].rearrange("(p i) t -> i p t", i=PACK)
+        for s in range(PACK):
+            gains_sb[LOW + s] = load(f"gains{s}", [P, T2], F32, gains_high[s])
+        w3_w = keep.tile([P, PASSES, 2 * N], U8, name="w3_w", align_bytes=ALIGN)
+        nc.sync.dma_start(out=w3_w[:].bitcast(I32), in_=w3_words.rearrange("a p n -> p a n").bitcast(I32))
+        for q in range(QUADS):
+            nc.sync.dma_start(
+                out=w3_s[QUAD * q : QUAD * q + SCALE_ROWS, :, :].bitcast(I32),
+                in_=w3_scales[:, SCALE_ROWS * q : SCALE_ROWS * (q + 1), :].rearrange("a r n -> r a n").bitcast(I32),
+            )
+        idx3 = load_list("idx3", offs3)
+        idx4 = load_list("idx4", offs4)
+        wgo_sb = load("wgo_sb", [P, S], F32, wgo)
+        exp_sb = load("z_slabs", [P, N // P, S], F32, expected.rearrange("(c p) m -> p c m", p=P))
+
         place(4)
-        g = ring.tile([P, T2 * PACK], BF16, name="wide", bufs=1, align_bytes=64)
-        for h in range(2):
-            group_rows(nc.scalar.copy, g[:, KP * PACK * h : KP * PACK * (h + 1)], z_rows[0][:, :, halves[h]])
+        z_g_low = keep.tile([P, T2 * PACK], BF16, name="wide", align_bytes=ALIGN)
+        for half in range(2):
+            group_rows(
+                nc.scalar.copy,
+                z_g_low[:, BANK * PACK * half : BANK * PACK * (half + 1)],
+                z_rows_low[:, :, HALVES[half]],
+            )
         w2_q = [quantize("w2_0", w2_g[0][:])]
         place(5)
         place(6)
         place(7)
-        z_q0 = quantize("z_0", g[:], tag="after6")
-        z_q = {(0, h): (z_q0, BANK * h) for h in range(2)}
-        z_rows.append(ring.tile([P, PACK, T2], BF16, name="wide", bufs=1, align_bytes=64))
-        for h in range(2):
-            for n in range(4, 8):
-                make_z_high(n, halves[h], gains_sb[n][:, halves[h]])
-        g0 = keep.tile([P, BANK * PACK], BF16, name="z_g10", align_bytes=64)
-        g1 = keep.tile([P, BANK * PACK], BF16, name="z_g11", tag="late", align_bytes=64)
-        group_rows(nc.scalar.copy, g0[:], z_rows[1][:, :, halves[0]])
-        group_rows(nc.vector.tensor_copy, g1[:], z_rows[1][:, :, halves[1]])
-        z_q[1, 0] = (quantize("z_10", g0[:]), 0)
-        z_q[1, 1] = (quantize("z_11", g1[:]), 0)
+        z_q_low = quantize("z_0", z_g_low[:], tag=f"after{before_z_low}")
+        z_q = {(0, half): (z_q_low, BANK * half) for half in range(2)}
+
+        z_rows_high = keep.tile([P, PACK, T2], BF16, name="wide", align_bytes=ALIGN)
+        for cols in HALVES:
+            for s in range(PACK):
+                make_z(
+                    z_rows_high[:, s, cols],
+                    pages[s][:, cols],
+                    rest_high[:, s : s + 1],
+                    gains_sb[LOW + s][:, cols],
+                )
+        z_g_first = keep.tile([P, BANK * PACK], BF16, name="z_g_first", align_bytes=ALIGN)
+        z_g_second = keep.tile([P, BANK * PACK], BF16, name="z_g_second", tag="late", align_bytes=ALIGN)
+        split = T2 - VECTOR_SLOTS
+        group_rows(nc.scalar.copy, z_g_first[:], z_rows_high[:, :, HALVES[0]])
+        group_rows(nc.scalar.copy, z_g_second[:, 0 : (split - BANK) * PACK], z_rows_high[:, :, BANK:split])
+        group_rows(nc.vector.tensor_copy, z_g_second[:, (split - BANK) * PACK :], z_rows_high[:, :, split:T2])
+        z_q[1, 0] = (quantize("z_10", z_g_first[:]), 0)
+        z_q[1, 1] = (quantize("z_11", z_g_second[:]), 0)
         w2_q.append(quantize("w2_1", w2_g[1][:], tag="late"))
-
-        accs = {}
-
-        def second_pass(c, h, b):
-            if b == 0:
-                accs[c, h] = (bank(4 * (c % 2) + 2 * h), bank(4 * (c % 2) + 2 * h + 1))
-            ya, yb = accs[c, h]
-            (z_codes, z_scales), t0 = z_q[b, h]
-            nc.tensor.matmul_mx(
-                out=yb[:],
-                lhsT=w3_w[:, b, 2 * P * c : 2 * P * (c + 1)].bitcast(FP4X4),
-                lhsT_scale=w3_s[:, b, P * c : P * (c + 1)],
-                rhs=z_codes[:, t0 : t0 + BANK].bitcast(FP8X4),
-                rhs_scale=z_scales[:, t0 : t0 + BANK],
-                start=(b == 0),
-                stop=(b == 1),
-            )
-            codes, scales = w2_q[c // 2]
-            c0 = 2 * P * b + P * (c % 2)
-            nc.tensor.matmul_mx(
-                out=ya[:],
-                lhsT=codes[:, c0 : c0 + P].bitcast(FP8X4),
-                lhsT_scale=scales[:, c0 : c0 + P],
-                rhs=z_codes[:, t0 : t0 + BANK].bitcast(FP8X4),
-                rhs_scale=z_scales[:, t0 : t0 + BANK],
-                start=(b == 0),
-                stop=(b == 1),
-            )
 
         y_sb = {}
         x_sb = {}
 
         def scores(c):
-            for b in range(2):
-                for h in range(2):
-                    second_pass(c, h, b)
-            y = ring.tile([P, T2], F32, name="y")
-            for h in range(2):
-                ya, yb = accs[c, h]
-                t = ring.tile([P, BANK], F32, name="yb_sb", bufs=3)
-                nc.scalar.copy(out=t[:], in_=yb[:])
-                nc.vector.tensor_tensor(y[:, halves[h]], ya[:], t[:], ALU.mult)
-            y_sb[c] = y
+            accs = {}
+            for a in range(PASSES):
+                for half in range(2):
+                    if a == 0:
+                        base = LOW * (c % 2) + 2 * half
+                        accs[half] = (bank(base), bank(base + 1))
+                    ya, yb = accs[half]
+                    (z_codes, z_scales), first_slot = z_q[a, half]
+                    slots = slice(first_slot, first_slot + BANK)
+                    nc.tensor.matmul_mx(
+                        out=yb[:],
+                        lhsT=w3_w[:, a, 2 * P * c : 2 * P * (c + 1)].bitcast(FP4X4),
+                        lhsT_scale=w3_s[:, a, P * c : P * (c + 1)],
+                        rhs=z_codes[:, slots].bitcast(FP8X4),
+                        rhs_scale=z_scales[:, slots],
+                        start=(a == 0),
+                        stop=(a == PASSES - 1),
+                    )
+                    codes, scales = w2_q[c // 2]
+                    first = 2 * P * a + P * (c % 2)
+                    nc.tensor.matmul_mx(
+                        out=ya[:],
+                        lhsT=codes[:, first : first + P].bitcast(FP8X4),
+                        lhsT_scale=scales[:, first : first + P],
+                        rhs=z_codes[:, slots].bitcast(FP8X4),
+                        rhs_scale=z_scales[:, slots],
+                        start=(a == 0),
+                        stop=(a == PASSES - 1),
+                    )
+            y_sb[c] = ring.tile([P, T2], F32, name="y")
+            for half in range(2):
+                ya, yb = accs[half]
+                yb_sb = ring.tile([P, BANK], F32, name="yb_sb", bufs=3)
+                nc.scalar.copy(out=yb_sb[:], in_=yb[:])
+                nc.vector.tensor_tensor(y_sb[c][:, HALVES[half]], ya[:], yb_sb[:], ALU.mult)
 
         def pick(c):
-            x = ring.tile([P, S], F32, name="x")
-            nc.vector.tensor_tensor(x[:], y_sb[c][:].indirect(idx3[:]), exp_sb[:, c, :], ALU.subtract)
-            x_sb[c] = x
+            x_sb[c] = ring.tile([P, S], F32, name="x")
+            nc.vector.tensor_tensor(x_sb[c][:], y_sb[c][:].indirect(idx3[:]), exp_sb[:, c, :], ALU.subtract)
 
         def put(c):
             cage = cages[c % 2]
             nc.vector.tensor_tensor(cage[:].indirect(idx4[:]), x_sb[c][:], wgo_sb[:], ALU.mult)
             nc.sync.dma_start(out=out[P * c : P * (c + 1), :], in_=cage[:])
 
+        blocks = N // P
         scores(0)
         pick(0)
-        for c in range(1, 4):
+        for c in range(1, blocks):
             scores(c)
             put(c - 1)
             pick(c)
-        put(3)
+        put(blocks - 1)

@@ -265,6 +265,7 @@ def tile_list_returns_chute_grading_kernel(
 
         y_sb = {}
         x_sb = {}
+        xw_sb = {}
 
         def scores(c):
             accs = {}
@@ -301,15 +302,26 @@ def tile_list_returns_chute_grading_kernel(
                 ya, yb = accs[half]
                 yb_sb = ring.tile([P, BANK], F32, name="yb_sb", bufs=3)
                 nc.scalar.copy(out=yb_sb[:], in_=yb[:])
-                nc.vector.tensor_tensor(y_sb[c][:, HALVES[half]], ya[:], yb_sb[:], ALU.mult)
+                if c < 2:
+                    nc.vector.tensor_tensor(y_sb[c][:, HALVES[half]], ya[:], yb_sb[:], ALU.mult)
+                else:
+                    ya_sb = ring.tile([P, BANK], F32, name="ya_sb")
+                    nc.scalar.copy(out=ya_sb[:], in_=ya[:])
+                    nc.gpsimd.tensor_tensor(y_sb[c][:, HALVES[half]], ya_sb[:], yb_sb[:], ALU.mult)
 
         def pick(c):
             x_sb[c] = ring.tile([P, S], F32, name="x")
             nc.vector.tensor_tensor(x_sb[c][:], y_sb[c][:].indirect(idx3[:]), exp_sb[:, c, :], ALU.subtract)
+            if c < 2:
+                xw_sb[c] = ring.tile([P, S], F32, name="xw")
+                nc.gpsimd.tensor_tensor(xw_sb[c][:], x_sb[c][:], wgo_sb[:], ALU.mult)
 
         def put(c):
             cage = cages[c % 2]
-            nc.vector.tensor_tensor(cage[:].indirect(idx4[:]), x_sb[c][:], wgo_sb[:], ALU.mult)
+            if c < 2:
+                nc.vector.tensor_copy(cage[:].indirect(idx4[:]), xw_sb[c][:])
+            else:
+                nc.vector.tensor_tensor(cage[:].indirect(idx4[:]), x_sb[c][:], wgo_sb[:], ALU.mult)
             nc.sync.dma_start(out=out[P * c : P * (c + 1), :], in_=cage[:])
 
         blocks = N // P
@@ -317,6 +329,6 @@ def tile_list_returns_chute_grading_kernel(
         pick(0)
         for c in range(1, blocks):
             scores(c)
-            put(c - 1)
             pick(c)
+            put(c - 1)
         put(blocks - 1)

@@ -37,11 +37,10 @@ def tile_list_returns_chute_grading_kernel(
     nc = tc.nc
     with ExitStack() as ctx:
         keep = ctx.enter_context(tc.tile_pool(name="keep", bufs=1))
-        ring = ctx.enter_context(tc.tile_pool(name="ring", bufs=2))
         psum = ctx.enter_context(tc.psum_pool(name="psum", bufs=1))
 
-        def load(name, shape, dtype, src):
-            loaded = keep.tile(shape, dtype, name=name)
+        def load(name, shape, dtype, src, tag=""):
+            loaded = keep.tile(shape, dtype, name=name, tag=tag, align_bytes=ALIGN)
             nc.sync.dma_start(out=loaded[:], in_=src)
             return loaded
 
@@ -64,7 +63,10 @@ def tile_list_returns_chute_grading_kernel(
             return codes, scales
 
         def group_rows(copy, dst, rows):
-            copy(out=dst.rearrange("p (c i) -> p c i", i=PACK), in_=rows.rearrange("p i c -> p c i"))
+            copy(
+                out=dst.rearrange("p (c j i) -> p c i j", i=PACK, j=PACK),
+                in_=rows.rearrange("p i (c j) -> p c i j", j=PACK),
+            )
 
         def group_passes(copy, name, rows):
             width = rows[0].shape[2] * PACK
@@ -86,62 +88,82 @@ def tile_list_returns_chute_grading_kernel(
         make_identity(nc, identity[:])
         rest_rows = keep.tile([P, P], F32, name="rest_rows")
         nc.vector.memset(rest_rows[:], 0.0)
-        pages = [keep.tile([P, T2], F32, name=f"page{index}") for index in range(LOW)]
+        pages = [keep.tile([P, T2], F32, name=f"page{index}") for index in range(2)]
         cages = [keep.tile([P, T2], F32, name=f"cage{index}") for index in range(2)]
         for window in pages + cages:
             nc.vector.memset(window[:], 0.0)
 
-        def load_w1(name, cols):
-            width = cols.stop - cols.start
-            return [load(f"{name}{a}", [P, PACK, width], F32, pass_rows(w1, a, cols)) for a in range(PASSES)]
+        def load_w1(n):
+            cols = slice(P * n, P * (n + 1))
+            return [load(f"w1_slab{n}_{a}", [P, PACK, P], F32, pass_rows(w1, a, cols)) for a in range(PASSES)]
 
-        def load_big(shape, dtype, src):
-            loaded = ring.tile(shape, dtype, name="big", bufs=2 * PASSES)
-            nc.sync.dma_start(out=loaded[:], in_=src)
-            return loaded
+        def reuse(name, shape, dtype, tag):
+            return keep.tile(shape, dtype, name=name, tag=tag, align_bytes=ALIGN)
 
         idx = load_list("idx", offs)
-        w1_slab0 = load_w1("w1_slab0_", slice(0, P))
+        w1_low = [load_w1(0)]
         tab_w = [
-            load_big([P, T], I32, tab_words[a].rearrange("p t i -> p (t i)").bitcast(I32)) for a in range(PASSES)
+            load(f"tab_w{a}", [P, T], I32, tab_words[a].rearrange("p t i -> p (t i)").bitcast(I32), tag=f"big{a}")
+            for a in range(PASSES)
         ]
-        w1_slab1 = load_w1("w1_slab1_", slice(P, 2 * P))
+        w1_low.append(load_w1(1))
+        w1_low.append(load_w1(2))
         wgs_low = load("wgs_low", [P, S], F32, wgs)
         idx2 = load_list("idx2", offs2)
-        w1_slab23 = load_w1("w1_slab23_", slice(2 * P, KP))
         nc.sync.dma_start(out=rest_rows[0:LOW, :], in_=rest[0:KP].rearrange("(n p) -> n p", p=P))
-        rest_high = load("rest_high", [P, PACK], F32, rest[KP:H].rearrange("(p i) -> p i", i=PACK))
+        w1_low.append(load_w1(3))
+        w1_high = [
+            load(f"w1_high{a}", [P, PACK, KP], F32, pass_rows(w1, a, slice(KP, H))) for a in range(PASSES)
+        ]
         gains_sb = {}
-        w1_high = []
-        for a in range(PASSES):
-            w1_high.append(load_big([P, PACK, KP], F32, pass_rows(w1, a, slice(KP, H))))
-            gains_sb[a] = load(f"gains{a}", [P, T2], F32, gains[P * a : P * (a + 1), :])
-        for n in range(PASSES, LOW):
-            gains_sb[n] = load(f"gains{n}", [P, T2], F32, gains[P * n : P * (n + 1), :])
+
+        def load_gains_low(n):
+            gains_sb[n] = load(f"gains{n}", [P, T2], F32, gains[P * n : P * (n + 1), :], tag=f"gains{n}")
+
+        gains_high = gains[KP:H, :].rearrange("(p i) t -> i p t", i=PACK)
+
+        def load_gains_high(s):
+            tag = f"gains{s}"
+            gains_sb[LOW + s] = load(f"gains{LOW + s}", [P, T2], F32, gains_high[s], tag=tag)
+
+        load_gains_low(0)
+        load_gains_low(1)
+        w2_raw = [
+            load(f"w2_raw{a}", [P, PACK, N], F32, pass_rows(w2, a, slice(0, N)), tag=f"w2_raw{a}") for a in range(PASSES)
+        ]
         wgs_high = keep.tile([P, PACK * S], F32, name="wgs_high")
         for q in range(QUADS):
             nc.sync.dma_start(
                 out=wgs_high[QUAD * q : QUAD * (q + 1), :], in_=wgs.rearrange("(m s) j -> m (s j)", s=PACK)
             )
+        load_gains_low(2)
+        load_gains_low(3)
 
         w1_q = {}
-        w1_q0 = quantize("w1_0", group_passes(nc.vector.tensor_copy, "w1_g0", [t[:] for t in w1_slab0])[:])
+
+        def quantize_w1_low(n, copy):
+            codes = quantize(f"w1_{n}", group_passes(copy, f"w1_g{n}", [t[:] for t in w1_low[n]])[:])
+            for a in range(PASSES):
+                w1_q[n, a] = (codes, P * a)
+
+        quantize_w1_low(0, nc.scalar.copy)
         v_s = keep.tile([P, S], U8, name="v_s", align_bytes=ALIGN)
-        nc.vector.tensor_copy(v_s[:], tab_s[:].indirect(idx[:]))
         v_w = []
         for a in range(PASSES):
             words = keep.tile([P, S], U32, name=f"v_w{a}", align_bytes=ALIGN)
             nc.vector.tensor_copy(words[:], tab_w[a][:].bitcast(U32).indirect(idx[:]))
             v_w.append(words)
-        w1_q1 = quantize("w1_1", group_passes(nc.vector.tensor_copy, "w1_g1", [t[:] for t in w1_slab1])[:])
-        for a in range(PASSES):
-            w1_q[0, a] = (w1_q0, P * a)
-            w1_q[1, a] = (w1_q1, P * a)
+            if a == 0:
+                nc.vector.tensor_copy(v_s[:], tab_s[:].indirect(idx[:]))
+        quantize_w1_low(1, nc.vector.tensor_copy)
 
-        w2_raw = [load_big([P, PACK, N], F32, pass_rows(w2, a, slice(0, N))) for a in range(PASSES)]
+        rest_high = load("rest_high", [P, PACK], F32, rest[KP:H].rearrange("(p i) -> p i", i=PACK))
 
-        before_w1_high, before_z_low = 2, 6
         h_abs = {}
+        h_tags = {1: "w1_slab2_1", 2: "w1_high0", 3: "w1_high1"}
+        weighted = {}
+        level = {}
+        page_of = [pages[0], pages[1]] + [pages[(n + 1) % 2] for n in range(2, 2 * LOW)]
 
         def first_product(n):
             acc = bank(LOW + n % LOW)
@@ -156,67 +178,117 @@ def tile_list_returns_chute_grading_kernel(
                     start=(a == 0),
                     stop=(a == PASSES - 1),
                 )
-            if n in (before_w1_high, before_z_low):
-                h_abs[n] = keep.tile([P, S], F32, name=f"h_abs{n}", tag=f"after{n}", align_bytes=ALIGN)
+            if n in (4, 5):
+                h_abs[n] = h_abs45[:, S * (n - LOW) : S * (n - LOW + 1)]
             else:
-                h_abs[n] = ring.tile([P, S], F32, name="h_abs", bufs=LOW)
-            nc.scalar.activation(out=h_abs[n][:], in_=acc[:], func=ACT.Abs)
+                h_abs[n] = reuse(f"h_abs{n}", [P, S], F32, h_tags.get(n, f"h_abs{n}"))[:]
+            nc.scalar.activation(out=h_abs[n], in_=acc[:], func=ACT.Abs)
+
+        def weigh(engine, n, tag):
+            weight = wgs_low[:] if n < LOW else wgs_high[:, S * (n - LOW) : S * (n - LOW + 1)]
+            weighted[n] = reuse(f"weighted{n}", [P, S], F32, tag)[:]
+            engine.tensor_tensor(weighted[n], h_abs[n], weight, ALU.mult)
+
+        def place_fused(n):
+            nc.vector.tensor_tensor(page_of[n][:].indirect(idx2[:]), h_abs[n], wgs_low[:], ALU.mult)
 
         def place(n):
-            weight = wgs_low[:] if n < LOW else wgs_high[:, S * (n - LOW) : S * (n - LOW + 1)]
-            nc.vector.tensor_tensor(pages[n % LOW][:].indirect(idx2[:]), h_abs[n][:], weight, ALU.mult)
+            nc.vector.tensor_copy(page_of[n][:].indirect(idx2[:]), weighted[n])
 
-        def make_z(dst, page, level, gain):
-            nc.vector.scalar_tensor_tensor(out=dst, in0=page, scalar=level, in1=gain, op0=ALU.add, op1=ALU.mult)
+        def rest_of(n):
+            return rest_low[:, n : n + 1] if n < LOW else rest_high[:, n - LOW : n - LOW + 1]
+
+        def make_z(dst, n, cols):
+            nc.vector.scalar_tensor_tensor(
+                out=dst, in0=page_of[n][:, cols], scalar=rest_of(n), in1=gains_sb[n][:, cols], op0=ALU.add, op1=ALU.mult
+            )
+
+        def add_rest(n, tag):
+            level[n] = reuse(f"level{n}", [P, T2], F32, tag)
+            nc.scalar.activation(out=level[n][:], in_=page_of[n][:], func=ACT.Identity, bias=rest_of(n))
+
+        def apply_gains(dst, n):
+            nc.gpsimd.tensor_tensor(dst, level[n][:], gains_sb[n][:], ALU.mult)
 
         z_rows_low = keep.tile([P, PACK, T2], BF16, name="z_rows_low")
-        z_slabs = keep.tile([P, LOW, T2], BF16, name="z_slabs")
+        z_slab = {}
+        z_tags = ["z_slab0", "z_slab1", "z_slab2", "h_abs6"]
 
-        def make_z_low(n):
-            make_z(z_slabs[:, n, :], pages[n][:], rest_low[:, n : n + 1], gains_sb[n][:])
-            nc.sync.dma_start(out=z_rows_low[QUAD * n : QUAD * (n + 1), :, :], in_=z_slabs[:, n, :])
+        def move_z(n):
+            nc.sync.dma_start(out=z_rows_low[QUAD * n : QUAD * (n + 1), :, :], in_=z_slab[n][:])
 
+        everything = slice(0, T2)
         first_product(0)
+        quantize_w1_low(2, nc.scalar.copy)
         first_product(1)
-        rest_turned = bank(LOW + 1)
-        nc.tensor.transpose(rest_turned[:, 0:P], rest_rows[:], identity[:])
-        rest_low = keep.tile([P, LOW], F32, name="rest_low")
-        nc.scalar.copy(out=rest_low[:], in_=rest_turned[:, 0:LOW])
-        w1_g23 = group_passes(nc.scalar.copy, "w1_g23", [t[:] for t in w1_slab23])
-        place(0)
-        w1_q23 = quantize("w1_23", w1_g23[:])
-        for n in (2, 3):
-            for a in range(PASSES):
-                w1_q[n, a] = (w1_q23, 2 * P * a + P * (n - 2))
-            first_product(n)
-
-        w1_gh = keep.tile([P, PASSES * KP * PACK], BF16, name="wide", align_bytes=ALIGN)
+        place_fused(0)
+        quantize_w1_low(3, nc.scalar.copy)
+        w1_gh = reuse("w1_gh", [P, PASSES * KP * PACK], BF16, "wide")
         for a in range(PASSES):
             nc.scalar.copy(
                 out=w1_gh[:, KP * PACK * a : KP * PACK * (a + 1)].rearrange("p (s m i) -> p m s i", s=PACK, i=PACK),
                 in_=w1_high[a][:].rearrange("p i (m s) -> p m s i", s=PACK),
             )
+        first_product(2)
+        place_fused(1)
+        rest_turned = bank(0)
+        nc.tensor.transpose(rest_turned[:, 0:P], rest_rows[:], identity[:])
+        rest_low = keep.tile([P, LOW], F32, name="rest_low")
+        nc.scalar.copy(out=rest_low[:], in_=rest_turned[:, 0:LOW])
+        first_product(3)
 
-        place(1)
-        make_z_low(0)
+        for n in range(2):
+            z_slab[n] = reuse(f"z_slab{n}", [P, T2], BF16, z_tags[n])
+            make_z(z_slab[n][:], n, everything)
+        w1_qh = quantize("w1_h", w1_gh[:], tag="chain")
+        weigh(nc.vector, 2, "wide")
         place(2)
-        make_z_low(1)
-        w1_qh = quantize("w1_h", w1_gh[:], tag=f"after{before_w1_high}")
-        place(3)
+        weigh(nc.gpsimd, 3, "w1_high0")
+        w2_both = reuse("w2_both", [P, PASSES * N * PACK], BF16, "w2_both")
+        w2_g = [w2_both[:, N * PACK * pair : N * PACK * (pair + 1)] for pair in range(2)]
+
+        def group_w2(a):
+            for pair in range(2):
+                group_rows(
+                    nc.scalar.copy,
+                    w2_g[pair][:, 2 * P * PACK * a : 2 * P * PACK * (a + 1)],
+                    w2_raw[a][:, :, 2 * P * pair : 2 * P * (pair + 1)],
+                )
+
+        group_w2(0)
+        group_w2(1)
+        h_abs45 = reuse("h_abs45", [P, 2 * S], F32, "w2_raw1")
         for n in range(LOW, 2 * LOW):
             for a in range(PASSES):
                 w1_q[n, a] = (w1_qh, KP * a + P * (n - LOW))
             first_product(n)
-        make_z_low(2)
-        w2_g = [
-            group_passes(nc.scalar.copy, f"w2_g{pair}", [t[:, :, 2 * P * pair : 2 * P * (pair + 1)] for t in w2_raw])
-            for pair in range(2)
-        ]
-        make_z_low(3)
+        weighted45 = reuse("weighted45", [P, 2 * S], F32, "weighted45")
+        nc.gpsimd.tensor_tensor(weighted45[:], h_abs45[:], wgs_high[:, 0 : 2 * S], ALU.mult)
+        weighted[4] = weighted45[:, 0:S]
+        weighted[5] = weighted45[:, S : 2 * S]
+        load_gains_high(0)
+        move_z(0)
+        move_z(1)
+        load_gains_high(1)
 
-        gains_high = gains[KP:H, :].rearrange("(p i) t -> i p t", i=PACK)
-        for s in range(PACK):
-            gains_sb[LOW + s] = load(f"gains{s}", [P, T2], F32, gains_high[s])
+        add_rest(2, "chain")
+        place(3)
+        z_slab[2] = reuse("z_slab2", [P, T2], BF16, z_tags[2])
+        apply_gains(z_slab[2][:], 2)
+        move_z(2)
+        load_gains_high(2)
+        weigh(nc.gpsimd, 6, "chain")
+        add_rest(3, "big0")
+        place(4)
+        z_slab[3] = reuse("z_slab3", [P, T2], BF16, z_tags[3])
+        apply_gains(z_slab[3][:], 3)
+        move_z(3)
+        load_gains_high(3)
+        weigh(nc.gpsimd, 7, "big0")
+
+        add_rest(4, "w2_raw0")
+        place(5)
+
         w3_w = keep.tile([P, PASSES, 2 * N], U8, name="w3_w", align_bytes=ALIGN)
         nc.sync.dma_start(out=w3_w[:].bitcast(I32), in_=w3_words.rearrange("a p n -> p a n").bitcast(I32))
         for q in range(QUADS):
@@ -227,45 +299,39 @@ def tile_list_returns_chute_grading_kernel(
         idx3 = load_list("idx3", offs3)
         idx4 = load_list("idx4", offs4)
         wgo_sb = load("wgo_sb", [P, S], F32, wgo)
-        exp_sb = load("z_slabs", [P, N // P, S], F32, expected.rearrange("(c p) m -> p c m", p=P))
+        exp_sb = [
+            load(f"exp{c}", [P, S], F32, expected[P * c : P * (c + 1), :], tag=z_tags[c]) for c in range(N // P)
+        ]
 
-        place(4)
-        z_g_low = keep.tile([P, T2 * PACK], BF16, name="wide", align_bytes=ALIGN)
-        for half in range(2):
-            group_rows(
-                nc.scalar.copy,
-                z_g_low[:, BANK * PACK * half : BANK * PACK * (half + 1)],
-                z_rows_low[:, :, HALVES[half]],
-            )
-        w2_q = [quantize("w2_0", w2_g[0][:])]
-        place(5)
+        z_rows_high = reuse("z_rows_high", [P, PACK, T2], BF16, "h_abs7")
+        apply_gains(z_rows_high[:, 0, :], 4)
+        add_rest(5, "big1")
         place(6)
+        apply_gains(z_rows_high[:, 1, :], 5)
+        w2_q = [quantize("w2_0", w2_g[0], tag="chain")]
+        add_rest(6, "w2_raw0")
         place(7)
-        z_q_low = quantize("z_0", z_g_low[:], tag=f"after{before_z_low}")
-        z_q = {(0, half): (z_q_low, BANK * half) for half in range(2)}
-
-        z_rows_high = keep.tile([P, PACK, T2], BF16, name="wide", align_bytes=ALIGN)
+        apply_gains(z_rows_high[:, 2, :], 6)
+        z_g_low = [reuse(f"z_g_low{half}", [P, BANK * PACK], BF16, ["wide", "big1"][half]) for half in range(2)]
+        for half in range(2):
+            group_rows(nc.scalar.copy, z_g_low[half][:], z_rows_low[:, :, HALVES[half]])
         for cols in HALVES:
-            for s in range(PACK):
-                make_z(
-                    z_rows_high[:, s, cols],
-                    pages[s][:, cols],
-                    rest_high[:, s : s + 1],
-                    gains_sb[LOW + s][:, cols],
-                )
-        z_g_first = keep.tile([P, BANK * PACK], BF16, name="z_g_first", align_bytes=ALIGN)
-        z_g_second = keep.tile([P, BANK * PACK], BF16, name="z_g_second", tag="late", align_bytes=ALIGN)
+            make_z(z_rows_high[:, 3, cols], 7, cols)
+        z_q = {}
+        for half in range(2):
+            z_q[0, half] = (quantize(f"z_0{half}", z_g_low[half][:]), 0)
+        z_g_first = reuse("z_g_first", [P, BANK * PACK], BF16, "late")
+        z_g_second = reuse("z_g_second", [P, BANK * PACK], BF16, "z_g_second")
         split = T2 - VECTOR_SLOTS
         group_rows(nc.scalar.copy, z_g_first[:], z_rows_high[:, :, HALVES[0]])
         group_rows(nc.scalar.copy, z_g_second[:, 0 : (split - BANK) * PACK], z_rows_high[:, :, BANK:split])
         group_rows(nc.vector.tensor_copy, z_g_second[:, (split - BANK) * PACK :], z_rows_high[:, :, split:T2])
         z_q[1, 0] = (quantize("z_10", z_g_first[:]), 0)
+        w2_q.append(quantize("w2_1", w2_g[1], tag="late"))
         z_q[1, 1] = (quantize("z_11", z_g_second[:]), 0)
-        w2_q.append(quantize("w2_1", w2_g[1][:], tag="late"))
 
         y_sb = {}
         x_sb = {}
-        xw_sb = {}
 
         def scores(c):
             accs = {}
@@ -297,24 +363,28 @@ def tile_list_returns_chute_grading_kernel(
                         start=(a == 0),
                         stop=(a == PASSES - 1),
                     )
-            y_sb[c] = ring.tile([P, T2], F32, name="y")
-            for half in range(2):
-                ya, yb = accs[half]
-                yb_sb = ring.tile([P, BANK], F32, name="yb_sb", bufs=3)
-                nc.scalar.copy(out=yb_sb[:], in_=yb[:])
-                if c < 2:
+            if c < 2:
+                y_sb[c] = reuse(f"y{c}", [P, T2], F32, f"y{c}")
+                for half in range(2):
+                    ya, yb = accs[half]
+                    yb_sb = reuse(f"yb{c}{half}", [P, BANK], F32, f"w1_slab{c}_{half}")
+                    nc.scalar.copy(out=yb_sb[:], in_=yb[:])
                     nc.vector.tensor_tensor(y_sb[c][:, HALVES[half]], ya[:], yb_sb[:], ALU.mult)
-                else:
-                    ya_sb = ring.tile([P, BANK], F32, name="ya_sb")
-                    nc.scalar.copy(out=ya_sb[:], in_=ya[:])
-                    nc.gpsimd.tensor_tensor(y_sb[c][:, HALVES[half]], ya_sb[:], yb_sb[:], ALU.mult)
+                    if (c, half) == (1, 0):
+                        xw_sb[0] = reuse("xw0", [P, S], F32, "xw0")
+                        nc.vector.tensor_tensor(xw_sb[0][:], x_sb[0][:], wgo_sb[:], ALU.mult)
+            else:
+                both = reuse(f"y_parts{c}", [P, 2 * T2], F32, f"w1_high{c - 2}")
+                for half in range(2):
+                    for part in range(2):
+                        first = T2 * part + BANK * half
+                        nc.scalar.copy(out=both[:, first : first + BANK], in_=accs[half][part][:])
+                y_sb[c] = reuse(f"y{c}", [P, T2], F32, "x1" if c == 2 else "y1")
+                nc.gpsimd.tensor_tensor(y_sb[c][:], both[:, 0:T2], both[:, T2 : 2 * T2], ALU.mult)
 
         def pick(c):
-            x_sb[c] = ring.tile([P, S], F32, name="x")
-            nc.vector.tensor_tensor(x_sb[c][:], y_sb[c][:].indirect(idx3[:]), exp_sb[:, c, :], ALU.subtract)
-            if c < 2:
-                xw_sb[c] = ring.tile([P, S], F32, name="xw")
-                nc.gpsimd.tensor_tensor(xw_sb[c][:], x_sb[c][:], wgo_sb[:], ALU.mult)
+            x_sb[c] = reuse(f"x{c}", [P, S], F32, f"x{c}")
+            nc.vector.tensor_tensor(x_sb[c][:], y_sb[c][:].indirect(idx3[:]), exp_sb[c][:], ALU.subtract)
 
         def put(c):
             cage = cages[c % 2]
@@ -324,11 +394,18 @@ def tile_list_returns_chute_grading_kernel(
                 nc.vector.tensor_tensor(cage[:].indirect(idx4[:]), x_sb[c][:], wgo_sb[:], ALU.mult)
             nc.sync.dma_start(out=out[P * c : P * (c + 1), :], in_=cage[:])
 
-        blocks = N // P
+        xw_sb = {}
         scores(0)
         pick(0)
-        for c in range(1, blocks):
-            scores(c)
-            pick(c)
-            put(c - 1)
-        put(blocks - 1)
+        scores(1)
+        pick(1)
+        xw_sb[1] = reuse("xw1", [P, S], F32, "xw1")
+        nc.gpsimd.tensor_tensor(xw_sb[1][:], x_sb[1][:], wgo_sb[:], ALU.mult)
+        put(0)
+        put(1)
+        scores(2)
+        scores(3)
+        pick(2)
+        pick(3)
+        put(2)
+        put(3)

@@ -55,11 +55,12 @@ def tile_list_returns_chute_grading_kernel(
         def bank(index):
             return psum.tile([P, BANK], F32, name=f"bank{index}")
 
-        def quantize(name, grouped, tag=""):
+        def quantize(name, grouped, tag="", codes=None):
             width = grouped.shape[1] // PACK
-            codes = keep.tile([P, width], U32, name=name + "_codes", tag=tag, align_bytes=ALIGN)
-            scales = keep.tile([P, width], U8, name=name + "_scales", align_bytes=ALIGN)
-            nc.vector.quantize_mx(out=codes[:].bitcast(FP8X4), scales=scales[:], in_=grouped)
+            if codes is None:
+                codes = keep.tile([P, width], U32, name=name + "_codes", tag=tag, align_bytes=ALIGN)[:]
+            scales = keep.tile([P, width], U8, name=name + "_scales", tag=name + "_scales", align_bytes=ALIGN)
+            nc.vector.quantize_mx(out=codes.bitcast(FP8X4), scales=scales[:], in_=grouped)
             return codes, scales
 
         def group_rows(copy, dst, rows):
@@ -86,87 +87,100 @@ def tile_list_returns_chute_grading_kernel(
         nc.vector.memset(w3_s[:].bitcast(I32), 0)
         identity = keep.tile([P, P], F32, name="identity")
         make_identity(nc, identity[:])
-        rest_rows = keep.tile([P, P], F32, name="rest_rows")
-        nc.vector.memset(rest_rows[:], 0.0)
-        pages = [keep.tile([P, T2], F32, name=f"page{index}") for index in range(2)]
+        pages = [keep.tile([P, T2], F32, name="page0")]
         cages = [keep.tile([P, T2], F32, name=f"cage{index}") for index in range(2)]
         for window in pages + cages:
             nc.vector.memset(window[:], 0.0)
 
-        def load_w1(n):
-            cols = slice(P * n, P * (n + 1))
-            return [load(f"w1_slab{n}_{a}", [P, PACK, P], F32, pass_rows(w1, a, cols)) for a in range(PASSES)]
-
         def reuse(name, shape, dtype, tag):
             return keep.tile(shape, dtype, name=name, tag=tag, align_bytes=ALIGN)
 
-        idx = load_list("idx", offs)
-        w1_low = [load_w1(0)]
-        tab_w = [
-            load(f"tab_w{a}", [P, T], I32, tab_words[a].rearrange("p t i -> p (t i)").bitcast(I32), tag=f"big{a}")
-            for a in range(PASSES)
-        ]
-        w1_low.append(load_w1(1))
-        w1_low.append(load_w1(2))
-        wgs_low = load("wgs_low", [P, S], F32, wgs)
-        idx2 = load_list("idx2", offs2)
-        nc.sync.dma_start(out=rest_rows[0:LOW, :], in_=rest[0:KP].rearrange("(n p) -> n p", p=P))
-        w1_low.append(load_w1(3))
-        w1_high = [
-            load(f"w1_high{a}", [P, PACK, KP], F32, pass_rows(w1, a, slice(KP, H))) for a in range(PASSES)
-        ]
+        def load_w1(side, a):
+            cols = slice(KP * side, KP * (side + 1))
+            return load(f"w1_raw{side}{a}", [P, PACK, KP], F32, pass_rows(w1, a, cols), tag=f"w1_raw{side}{a}")
+
+        def load_table(a):
+            words = tab_words[a].rearrange("p t i -> p (t i)").bitcast(I32)
+            return load(f"tab_w{a}", [P, T], I32, words, tag=f"tab_w{a}")
+
+        gains_rows = gains.rearrange("(side p i) t -> side i p t", side=2, i=PACK)
         gains_sb = {}
 
-        def load_gains_low(n):
-            gains_sb[n] = load(f"gains{n}", [P, T2], F32, gains[P * n : P * (n + 1), :], tag=f"gains{n}")
+        def load_gains(n):
+            gains_sb[n] = load(f"gains{n}", [P, T2], F32, gains_rows[n // PACK, n % PACK], tag=f"gains{n % PACK}")
 
-        gains_high = gains[KP:H, :].rearrange("(p i) t -> i p t", i=PACK)
+        idx = load_list("idx", offs)
+        wgs_sb = load("wgs_sb", [P, S], F32, wgs)
+        w1_raw = {}
+        tab_w = []
+        for a in range(PASSES):
+            w1_raw[0, a] = load_w1(0, a)
+            tab_w.append(load_table(a))
+        idx2 = load_list("idx2", offs2)
+        rest_sb = load("rest_sb", [P, 2, PACK], F32, rest.rearrange("(side p i) -> p side i", side=2, i=PACK))
+        for a in range(PASSES):
+            w1_raw[1, a] = load_w1(1, a)
+        load_gains(0)
+        load_gains(1)
+        w2_raw = {}
+        for a in range(PASSES):
+            for pair in range(2):
+                cols = slice(2 * P * pair, 2 * P * (pair + 1))
+                name = f"w2_raw{a}{pair}"
+                w2_raw[a, pair] = load(name, [P, PACK, 2 * P], F32, pass_rows(w2, a, cols), tag=name)
+        load_gains(2)
+        load_gains(3)
 
-        def load_gains_high(s):
-            tag = f"gains{s}"
-            gains_sb[LOW + s] = load(f"gains{LOW + s}", [P, T2], F32, gains_high[s], tag=tag)
+        turned = bank(LOW)
+        for block in range(PACK):
+            nc.tensor.transpose(turned[:, P * block : P * (block + 1)], wgs_sb[:, P * block : P * (block + 1)], identity[:])
+        picked = reuse("picked", [P, PACK * S], F32, "picked")
+        nc.scalar.copy(
+            out=picked[:].rearrange("p (b s q m) -> p b s q m", b=PACK, s=PACK, q=QUADS),
+            in_=turned[:].rearrange("p (b m s) -> p b s m", b=PACK, s=PACK).unsqueeze(3).to_broadcast([P, PACK, PACK, QUADS, QUAD]),
+        )
+        wgs_dealt = keep.tile([P, PACK * S], F32, name="wgs_dealt")
+        for s in range(PACK):
+            back = bank(LOW + s)
+            for block in range(PACK):
+                first = S * block + P * s
+                nc.tensor.transpose(back[:, P * block : P * (block + 1)], picked[:, first : first + P], identity[:])
+            nc.scalar.copy(out=wgs_dealt[:, S * s : S * (s + 1)], in_=back[:])
 
-        load_gains_low(0)
-        load_gains_low(1)
-        w2_raw = [
-            load(f"w2_raw{a}", [P, PACK, N], F32, pass_rows(w2, a, slice(0, N)), tag=f"w2_raw{a}") for a in range(PASSES)
-        ]
-        wgs_high = keep.tile([P, PACK * S], F32, name="wgs_high")
-        for q in range(QUADS):
-            nc.sync.dma_start(
-                out=wgs_high[QUAD * q : QUAD * (q + 1), :], in_=wgs.rearrange("(m s) j -> m (s j)", s=PACK)
+        def group_w1(copy, dst, side, a, first, count):
+            copy(
+                out=dst.rearrange("p (s m i) -> p m s i", s=PACK, i=PACK)[:, first : first + count],
+                in_=w1_raw[side, a][:].rearrange("p i (m s) -> p m s i", s=PACK)[:, first : first + count],
             )
-        load_gains_low(2)
-        load_gains_low(3)
 
         w1_q = {}
-
-        def quantize_w1_low(n, copy):
-            codes = quantize(f"w1_{n}", group_passes(copy, f"w1_g{n}", [t[:] for t in w1_low[n]])[:])
-            for a in range(PASSES):
-                w1_q[n, a] = (codes, P * a)
-
-        quantize_w1_low(0, nc.scalar.copy)
         v_s = keep.tile([P, S], U8, name="v_s", align_bytes=ALIGN)
         v_w = []
         for a in range(PASSES):
+            grouped = reuse(f"w1_g0{a}", [P, KP * PACK], BF16, ["w1_g00", "picked"][a])
+            share = P if a == 0 else P // 2
+            group_w1(nc.vector.tensor_copy, grouped[:], 0, a, 0, share)
+            if share < P:
+                group_w1(nc.scalar.copy, grouped[:], 0, a, share, P - share)
+            codes = quantize(f"w1_0{a}", grouped[:], tag=f"w1_q0{a}")
+            for s in range(PACK):
+                w1_q[s, a] = (codes, P * s)
             words = keep.tile([P, S], U32, name=f"v_w{a}", align_bytes=ALIGN)
             nc.vector.tensor_copy(words[:], tab_w[a][:].bitcast(U32).indirect(idx[:]))
             v_w.append(words)
             if a == 0:
                 nc.vector.tensor_copy(v_s[:], tab_s[:].indirect(idx[:]))
-        quantize_w1_low(1, nc.vector.tensor_copy)
-
-        rest_high = load("rest_high", [P, PACK], F32, rest[KP:H].rearrange("(p i) -> p i", i=PACK))
 
         h_abs = {}
-        h_tags = {1: "w1_slab2_1", 2: "w1_high0", 3: "w1_high1"}
         weighted = {}
         level = {}
-        page_of = [pages[0], pages[1]] + [pages[(n + 1) % 2] for n in range(2, 2 * LOW)]
+        page_of = {n: pages[0] for n in (0, 1, 2, 4, 6)}
+
+        h_acc = {}
 
         def first_product(n):
             acc = bank(LOW + n % LOW)
+            h_acc[n] = acc
             for a in range(PASSES):
                 (codes, scales), first = w1_q[n, a]
                 nc.tensor.matmul_mx(
@@ -178,73 +192,88 @@ def tile_list_returns_chute_grading_kernel(
                     start=(a == 0),
                     stop=(a == PASSES - 1),
                 )
-            if n in (4, 5):
-                h_abs[n] = h_abs45[:, S * (n - LOW) : S * (n - LOW + 1)]
-            else:
-                h_abs[n] = reuse(f"h_abs{n}", [P, S], F32, h_tags.get(n, f"h_abs{n}"))[:]
-            nc.scalar.activation(out=h_abs[n], in_=acc[:], func=ACT.Abs)
 
-        def weigh(engine, n, tag):
-            weight = wgs_low[:] if n < LOW else wgs_high[:, S * (n - LOW) : S * (n - LOW + 1)]
-            weighted[n] = reuse(f"weighted{n}", [P, S], F32, tag)[:]
-            engine.tensor_tensor(weighted[n], h_abs[n], weight, ALU.mult)
+        def take_abs(n, dst):
+            h_abs[n] = dst
+            nc.scalar.activation(out=dst, in_=h_acc[n][:], func=ACT.Abs)
 
-        def place_fused(n):
-            nc.vector.tensor_tensor(page_of[n][:].indirect(idx2[:]), h_abs[n], wgs_low[:], ALU.mult)
+        def weights_of(n, count):
+            return wgs_dealt[:, S * (n % PACK) : S * (n % PACK + count)]
+
+        def products_of_pair(n):
+            both = reuse(f"h_abs{n}", [P, 2 * S], F32, f"h_abs{n}")
+            for k in range(2):
+                first_product(n + k)
+                take_abs(n + k, both[:, S * k : S * (k + 1)])
+            return both
+
+        def weigh_pair(n, both, dst):
+            nc.gpsimd.tensor_tensor(dst, both[:], weights_of(n, 2), ALU.mult)
+            weighted[n] = dst[:, 0:S]
+            weighted[n + 1] = dst[:, S : 2 * S]
 
         def place(n):
             nc.vector.tensor_copy(page_of[n][:].indirect(idx2[:]), weighted[n])
 
         def rest_of(n):
-            return rest_low[:, n : n + 1] if n < LOW else rest_high[:, n - LOW : n - LOW + 1]
+            return rest_sb[:, n // PACK, n % PACK : n % PACK + 1]
 
-        def make_z(dst, n, cols):
+        z_rows = [keep.tile([P, PACK, T2], BF16, name=f"z_rows{side}") for side in range(2)]
+
+        def make_z(n, cols):
             nc.vector.scalar_tensor_tensor(
-                out=dst, in0=page_of[n][:, cols], scalar=rest_of(n), in1=gains_sb[n][:, cols], op0=ALU.add, op1=ALU.mult
+                out=z_rows[n // PACK][:, n % PACK, cols],
+                in0=page_of[n][:, cols],
+                scalar=rest_of(n),
+                in1=gains_sb[n][:, cols],
+                op0=ALU.add,
+                op1=ALU.mult,
             )
 
-        def add_rest(n, tag):
-            level[n] = reuse(f"level{n}", [P, T2], F32, tag)
-            nc.scalar.activation(out=level[n][:], in_=page_of[n][:], func=ACT.Identity, bias=rest_of(n))
+        def add_rest(n, dst):
+            level[n] = dst
+            nc.scalar.activation(out=dst, in_=page_of[n][:], func=ACT.Identity, bias=rest_of(n))
 
-        def apply_gains(dst, n):
-            nc.gpsimd.tensor_tensor(dst, level[n][:], gains_sb[n][:], ALU.mult)
+        def apply_gains(n):
+            nc.gpsimd.tensor_tensor(z_rows[n // PACK][:, n % PACK, :], level[n], gains_sb[n][:], ALU.mult)
 
-        z_rows_low = keep.tile([P, PACK, T2], BF16, name="z_rows_low")
-        z_slab = {}
-        z_tags = ["z_slab0", "z_slab1", "z_slab2", "h_abs6"]
-
-        def move_z(n):
-            nc.sync.dma_start(out=z_rows_low[QUAD * n : QUAD * (n + 1), :, :], in_=z_slab[n][:])
-
-        everything = slice(0, T2)
-        first_product(0)
-        quantize_w1_low(2, nc.scalar.copy)
-        first_product(1)
-        place_fused(0)
-        quantize_w1_low(3, nc.scalar.copy)
-        w1_gh = reuse("w1_gh", [P, PASSES * KP * PACK], BF16, "wide")
-        for a in range(PASSES):
-            nc.scalar.copy(
-                out=w1_gh[:, KP * PACK * a : KP * PACK * (a + 1)].rearrange("p (s m i) -> p m s i", s=PACK, i=PACK),
-                in_=w1_high[a][:].rearrange("p i (m s) -> p m s i", s=PACK),
-            )
-        first_product(2)
-        place_fused(1)
-        rest_turned = bank(0)
-        nc.tensor.transpose(rest_turned[:, 0:P], rest_rows[:], identity[:])
-        rest_low = keep.tile([P, LOW], F32, name="rest_low")
-        nc.scalar.copy(out=rest_low[:], in_=rest_turned[:, 0:LOW])
-        first_product(3)
+        def level_tile(n, tag):
+            return reuse(f"level{n}", [P, T2], F32, tag)[:]
 
         for n in range(2):
-            z_slab[n] = reuse(f"z_slab{n}", [P, T2], BF16, z_tags[n])
-            make_z(z_slab[n][:], n, everything)
-        w1_qh = quantize("w1_h", w1_gh[:], tag="chain")
-        weigh(nc.vector, 2, "wide")
+            first_product(n)
+            take_abs(n, reuse(f"h_abs{n}", [P, S], F32, f"h_abs{n}")[:])
+        h_abs23 = products_of_pair(2)
+        nc.vector.tensor_tensor(page_of[0][:].indirect(idx2[:]), h_abs[0], weights_of(0, 1), ALU.mult)
+        weighted[1] = reuse("weighted1", [P, S], F32, "weighted1")[:]
+        nc.vector.tensor_tensor(weighted[1], h_abs[1], weights_of(1, 1), ALU.mult)
+        make_z(0, slice(0, T2))
+        place(1)
+        weigh_pair(2, h_abs23, reuse("weighted23", [P, 2 * S], F32, "gains0")[:])
+        w1_gh = [reuse(f"w1_g1{a}", [P, KP * PACK], BF16, ["w1_q01", "w1_g11"][a])[:] for a in range(PASSES)]
+        for a in range(PASSES):
+            group_w1(nc.scalar.copy, w1_gh[a], 1, a, 0, P)
+            codes = quantize(f"w1_1{a}", w1_gh[a], tag=["weighted1", "chain"][a])
+            for s in range(PACK):
+                w1_q[LOW + s, a] = (codes, P * s)
+        second_page = reuse("page1", [P, T2], F32, "w1_g11")
+        nc.vector.memset(second_page[:], 0.0)
+        for n in (3, 5, 7):
+            page_of[n] = second_page
+        add_rest(1, level_tile(1, "w1_raw11"))
         place(2)
-        weigh(nc.gpsimd, 3, "w1_high0")
-        w2_both = reuse("w2_both", [P, PASSES * N * PACK], BF16, "w2_both")
+        apply_gains(1)
+        load_gains(5)
+        h_abs45 = products_of_pair(4)
+        h_abs67 = products_of_pair(6)
+        weigh_pair(4, h_abs45, reuse("weighted45", [P, 2 * S], F32, "weighted45")[:])
+        add_rest(2, level_tile(2, "chain"))
+        place(3)
+        load_gains(4)
+        apply_gains(2)
+        load_gains(6)
+
+        w2_both = reuse("w2_both", [P, PASSES * N * PACK], BF16, "w1_11_scales")
         w2_g = [w2_both[:, N * PACK * pair : N * PACK * (pair + 1)] for pair in range(2)]
 
         def group_w2(a):
@@ -252,41 +281,18 @@ def tile_list_returns_chute_grading_kernel(
                 group_rows(
                     nc.scalar.copy,
                     w2_g[pair][:, 2 * P * PACK * a : 2 * P * PACK * (a + 1)],
-                    w2_raw[a][:, :, 2 * P * pair : 2 * P * (pair + 1)],
+                    w2_raw[a, pair][:],
                 )
 
         group_w2(0)
-        group_w2(1)
-        h_abs45 = reuse("h_abs45", [P, 2 * S], F32, "w2_raw1")
-        for n in range(LOW, 2 * LOW):
-            for a in range(PASSES):
-                w1_q[n, a] = (w1_qh, KP * a + P * (n - LOW))
-            first_product(n)
-        weighted45 = reuse("weighted45", [P, 2 * S], F32, "weighted45")
-        nc.gpsimd.tensor_tensor(weighted45[:], h_abs45[:], wgs_high[:, 0 : 2 * S], ALU.mult)
-        weighted[4] = weighted45[:, 0:S]
-        weighted[5] = weighted45[:, S : 2 * S]
-        load_gains_high(0)
-        move_z(0)
-        move_z(1)
-        load_gains_high(1)
-
-        add_rest(2, "chain")
-        place(3)
-        z_slab[2] = reuse("z_slab2", [P, T2], BF16, z_tags[2])
-        apply_gains(z_slab[2][:], 2)
-        move_z(2)
-        load_gains_high(2)
-        weigh(nc.gpsimd, 6, "chain")
-        add_rest(3, "big0")
+        add_rest(3, level_tile(3, "w2_raw00"))
         place(4)
-        z_slab[3] = reuse("z_slab3", [P, T2], BF16, z_tags[3])
-        apply_gains(z_slab[3][:], 3)
-        move_z(3)
-        load_gains_high(3)
-        weigh(nc.gpsimd, 7, "big0")
-
-        add_rest(4, "w2_raw0")
+        apply_gains(3)
+        load_gains(7)
+        after3 = reuse("after3", [P, 2 * T2], F32, "w2_raw00")
+        weigh_pair(6, h_abs67, after3[:, 0:T2])
+        group_w2(1)
+        add_rest(4, level_tile(4, "w2_raw10"))
         place(5)
 
         w3_w = keep.tile([P, PASSES, 2 * N], U8, name="w3_w", align_bytes=ALIGN)
@@ -299,33 +305,32 @@ def tile_list_returns_chute_grading_kernel(
         idx3 = load_list("idx3", offs3)
         idx4 = load_list("idx4", offs4)
         wgo_sb = load("wgo_sb", [P, S], F32, wgo)
-        exp_sb = [
-            load(f"exp{c}", [P, S], F32, expected[P * c : P * (c + 1), :], tag=z_tags[c]) for c in range(N // P)
-        ]
+        exp_all = load("exp_all", [P, N // P, S], F32, expected.rearrange("(c p) m -> p c m", p=P), tag="tab_w0")
+        exp_sb = [exp_all[:, c, :] for c in range(N // P)]
 
-        z_rows_high = reuse("z_rows_high", [P, PACK, T2], BF16, "h_abs7")
-        apply_gains(z_rows_high[:, 0, :], 4)
-        add_rest(5, "big1")
+        apply_gains(4)
+        z_g_low = [reuse("z_g_low0", [P, BANK * PACK], BF16, "w1_g00")]
+        group_rows(nc.scalar.copy, z_g_low[0][:], z_rows[0][:, :, HALVES[0]])
+        add_rest(5, after3[:, T2 : 2 * T2])
         place(6)
-        apply_gains(z_rows_high[:, 1, :], 5)
-        w2_q = [quantize("w2_0", w2_g[0], tag="chain")]
-        add_rest(6, "w2_raw0")
+        apply_gains(5)
+        add_rest(6, level_tile(6, "w2_raw10"))
         place(7)
-        apply_gains(z_rows_high[:, 2, :], 6)
-        z_g_low = [reuse(f"z_g_low{half}", [P, BANK * PACK], BF16, ["wide", "big1"][half]) for half in range(2)]
-        for half in range(2):
-            group_rows(nc.scalar.copy, z_g_low[half][:], z_rows_low[:, :, HALVES[half]])
+        apply_gains(6)
+        z_g_low.append(reuse("z_g_low1", [P, BANK * PACK], BF16, "gains1"))
+        group_rows(nc.scalar.copy, z_g_low[1][:], z_rows[0][:, :, HALVES[1]])
         for cols in HALVES:
-            make_z(z_rows_high[:, 3, cols], 7, cols)
-        z_q = {}
-        for half in range(2):
-            z_q[0, half] = (quantize(f"z_0{half}", z_g_low[half][:]), 0)
+            make_z(7, cols)
+        late_codes = reuse("late_codes", [P, 2 * BANK], U32, "w2_raw00")
+        w2_q = [quantize("w2_0", w2_g[0], codes=late_codes[:, 0:BANK])]
+        z_q = {(0, 0): (quantize("z_00", z_g_low[0][:], codes=late_codes[:, BANK : 2 * BANK]), 0)}
+        z_q[0, 1] = (quantize("z_01", z_g_low[1][:]), 0)
         z_g_first = reuse("z_g_first", [P, BANK * PACK], BF16, "late")
-        z_g_second = reuse("z_g_second", [P, BANK * PACK], BF16, "z_g_second")
+        z_g_second = reuse("z_g_second", [P, BANK * PACK], BF16, "picked")
         split = T2 - VECTOR_SLOTS
-        group_rows(nc.scalar.copy, z_g_first[:], z_rows_high[:, :, HALVES[0]])
-        group_rows(nc.scalar.copy, z_g_second[:, 0 : (split - BANK) * PACK], z_rows_high[:, :, BANK:split])
-        group_rows(nc.vector.tensor_copy, z_g_second[:, (split - BANK) * PACK :], z_rows_high[:, :, split:T2])
+        group_rows(nc.scalar.copy, z_g_first[:], z_rows[1][:, :, HALVES[0]])
+        group_rows(nc.scalar.copy, z_g_second[:, 0 : (split - BANK) * PACK], z_rows[1][:, :, BANK:split])
+        group_rows(nc.vector.tensor_copy, z_g_second[:, (split - BANK) * PACK :], z_rows[1][:, :, split:T2])
         z_q[1, 0] = (quantize("z_10", z_g_first[:]), 0)
         w2_q.append(quantize("w2_1", w2_g[1], tag="late"))
         z_q[1, 1] = (quantize("z_11", z_g_second[:]), 0)
@@ -364,17 +369,17 @@ def tile_list_returns_chute_grading_kernel(
                         stop=(a == PASSES - 1),
                     )
             if c < 2:
-                y_sb[c] = reuse(f"y{c}", [P, T2], F32, f"y{c}")
+                y_sb[c] = reuse(f"y{c}", [P, T2], F32, ["tab_w1", "y1"][c])
                 for half in range(2):
                     ya, yb = accs[half]
-                    yb_sb = reuse(f"yb{c}{half}", [P, BANK], F32, f"w1_slab{c}_{half}")
+                    yb_sb = reuse(f"yb{c}{half}", [P, BANK], F32, ["h_abs0", "weighted1", "h_abs2", "h_abs6"][2 * c + half])
                     nc.scalar.copy(out=yb_sb[:], in_=yb[:])
                     nc.vector.tensor_tensor(y_sb[c][:, HALVES[half]], ya[:], yb_sb[:], ALU.mult)
                     if (c, half) == (1, 0):
                         xw_sb[0] = reuse("xw0", [P, S], F32, "xw0")
                         nc.vector.tensor_tensor(xw_sb[0][:], x_sb[0][:], wgo_sb[:], ALU.mult)
             else:
-                both = reuse(f"y_parts{c}", [P, 2 * T2], F32, f"w1_high{c - 2}")
+                both = reuse(f"y_parts{c}", [P, 2 * T2], F32, f"w1_raw0{c - 2}")
                 for half in range(2):
                     for part in range(2):
                         first = T2 * part + BANK * half
@@ -384,7 +389,7 @@ def tile_list_returns_chute_grading_kernel(
 
         def pick(c):
             x_sb[c] = reuse(f"x{c}", [P, S], F32, f"x{c}")
-            nc.vector.tensor_tensor(x_sb[c][:], y_sb[c][:].indirect(idx3[:]), exp_sb[c][:], ALU.subtract)
+            nc.vector.tensor_tensor(x_sb[c][:], y_sb[c][:].indirect(idx3[:]), exp_sb[c], ALU.subtract)
 
         def put(c):
             cage = cages[c % 2]

@@ -27,6 +27,7 @@ QUADS = P // QUAD
 SCALE_ROWS = 4
 LOW = 4
 HALVES = [slice(0, BANK), slice(BANK, 2 * BANK)]
+LIST_HALVES = [(slice(0, S // 2), slice(0, S // 32)), (slice(S // 2, S), slice(S // 32, S // 16))]
 ALIGN = 64
 VECTOR_SLOTS = T2 // 4
 
@@ -76,20 +77,14 @@ def tile_list_returns_chute_grading_kernel(
                 group_rows(copy, grouped[:, width * a : width * (a + 1)], rows[a])
             return grouped
 
-        tab_s = keep.tile([P, T], U8, name="tab_s", align_bytes=ALIGN)
+        tab_s = keep.tile([P, T], U8, name="tab_s", tag="w1_g00", align_bytes=ALIGN)
         nc.gpsimd.memset(tab_s[:].bitcast(I32), 0)
-        for q in range(QUADS):
-            nc.scalar.dma_start(
-                out=tab_s[QUAD * q : QUAD * q + PASSES * SCALE_ROWS, :].bitcast(I32),
-                in_=tab_scales[:, SCALE_ROWS * q : SCALE_ROWS * (q + 1), :].bitcast(I32),
-            )
         w3_s = keep.tile([P, PASSES, N], U8, name="w3_s", align_bytes=ALIGN)
         nc.vector.memset(w3_s[:].bitcast(I32), 0)
         identity = keep.tile([P, P], F32, name="identity")
         make_identity(nc, identity[:])
-        pages = [keep.tile([P, T2], F32, name="page0")]
-        cages = [keep.tile([P, T2], F32, name=f"cage{index}") for index in range(2)]
-        for window in pages + cages:
+        pages = [keep.tile([P, T2], F32, name=f"page{index}") for index in range(2)]
+        for window in pages:
             nc.vector.memset(window[:], 0.0)
 
         def reuse(name, shape, dtype, tag):
@@ -110,6 +105,13 @@ def tile_list_returns_chute_grading_kernel(
             gains_sb[n] = load(f"gains{n}", [P, T2], F32, gains_rows[n // PACK, n % PACK], tag=f"gains{n % PACK}")
 
         idx = load_list("idx", offs)
+        tab_s_rows = keep.tile([P, T // PACK], I32, name="tab_s_rows")
+        for q in range(QUADS):
+            rows = slice(QUAD * q, QUAD * q + PASSES * SCALE_ROWS)
+            nc.sync.dma_start(
+                out=tab_s_rows[rows, :], in_=tab_scales[:, SCALE_ROWS * q : SCALE_ROWS * (q + 1), :].bitcast(I32)
+            )
+            nc.vector.tensor_copy(tab_s[rows, :].bitcast(I32), tab_s_rows[rows, :])
         wgs_sb = load("wgs_sb", [P, S], F32, wgs)
         w1_raw = {}
         tab_w = []
@@ -154,48 +156,51 @@ def tile_list_returns_chute_grading_kernel(
             )
 
         w1_q = {}
-        v_s = keep.tile([P, S], U8, name="v_s", align_bytes=ALIGN)
         v_w = []
+        v_s = reuse("v_s", [P, S], U8, "v_s")
+        nc.vector.tensor_copy(v_s[:], tab_s[:].indirect(idx[:]))
         for a in range(PASSES):
-            grouped = reuse(f"w1_g0{a}", [P, KP * PACK], BF16, ["w1_g00", "picked"][a])
-            share = P if a == 0 else P // 2
-            group_w1(nc.vector.tensor_copy, grouped[:], 0, a, 0, share)
-            if share < P:
-                group_w1(nc.scalar.copy, grouped[:], 0, a, share, P - share)
+            grouped = reuse(f"w1_g0{a}", [P, KP * PACK], BF16, ["w1_g00", "tab_w0"][a])
+            group_w1(nc.vector.tensor_copy, grouped[:], 0, a, 0, P)
             codes = quantize(f"w1_0{a}", grouped[:], tag=f"w1_q0{a}")
             for s in range(PACK):
                 w1_q[s, a] = (codes, P * s)
-            words = keep.tile([P, S], U32, name=f"v_w{a}", align_bytes=ALIGN)
-            nc.vector.tensor_copy(words[:], tab_w[a][:].bitcast(U32).indirect(idx[:]))
+            words = reuse(f"v_w{a}", [P, S], U32, ["w1_g00", "tab_w0"][a])
             v_w.append(words)
             if a == 0:
-                nc.vector.tensor_copy(v_s[:], tab_s[:].indirect(idx[:]))
+                nc.vector.tensor_copy(words[:], tab_w[a][:].bitcast(U32).indirect(idx[:]))
+            else:
+                for entries, columns in LIST_HALVES:
+                    nc.vector.tensor_copy(words[:, entries], tab_w[a][:].bitcast(U32).indirect(idx[:, columns]))
+
+        cages = [reuse(f"cage{index}", [P, T2], F32, tag) for index, tag in enumerate(["tab_w1", "w1_raw00"])]
+        for window in cages:
+            nc.vector.memset(window[:], 0.0)
 
         h_abs = {}
         weighted = {}
         level = {}
-        page_of = {n: pages[0] for n in (0, 1, 2, 4, 6)}
+        page_of = [pages[0], pages[1]] + [pages[(n + 1) % 2] for n in range(2, 2 * LOW)]
 
         h_acc = {}
 
-        def first_product(n):
-            acc = bank(LOW + n % LOW)
+        def first_product(n, acc, entries):
             h_acc[n] = acc
             for a in range(PASSES):
                 (codes, scales), first = w1_q[n, a]
                 nc.tensor.matmul_mx(
-                    out=acc[:],
+                    out=acc,
                     lhsT=codes[:, first : first + P].bitcast(FP8X4),
                     lhsT_scale=scales[:, first : first + P],
-                    rhs=v_w[a][:].bitcast(FP8X4),
-                    rhs_scale=v_s[SCALE_ROWS * a : P, :],
+                    rhs=v_w[a][:, entries].bitcast(FP8X4),
+                    rhs_scale=v_s[SCALE_ROWS * a : P, entries],
                     start=(a == 0),
                     stop=(a == PASSES - 1),
                 )
 
         def take_abs(n, dst):
             h_abs[n] = dst
-            nc.scalar.activation(out=dst, in_=h_acc[n][:], func=ACT.Abs)
+            nc.scalar.activation(out=dst, in_=h_acc[n], func=ACT.Abs)
 
         def weights_of(n, count):
             return wgs_dealt[:, S * (n % PACK) : S * (n % PACK + count)]
@@ -203,7 +208,7 @@ def tile_list_returns_chute_grading_kernel(
         def products_of_pair(n):
             both = reuse(f"h_abs{n}", [P, 2 * S], F32, f"h_abs{n}")
             for k in range(2):
-                first_product(n + k)
+                first_product(n + k, bank(LOW + (n + k) % LOW)[:], slice(0, S))
                 take_abs(n + k, both[:, S * k : S * (k + 1)])
             return both
 
@@ -218,7 +223,7 @@ def tile_list_returns_chute_grading_kernel(
         def rest_of(n):
             return rest_sb[:, n // PACK, n % PACK : n % PACK + 1]
 
-        z_rows = [keep.tile([P, PACK, T2], BF16, name=f"z_rows{side}") for side in range(2)]
+        z_rows = []
 
         def make_z(n, cols):
             nc.vector.scalar_tensor_tensor(
@@ -240,26 +245,36 @@ def tile_list_returns_chute_grading_kernel(
         def level_tile(n, tag):
             return reuse(f"level{n}", [P, T2], F32, tag)[:]
 
-        for n in range(2):
-            first_product(n)
-            take_abs(n, reuse(f"h_abs{n}", [P, S], F32, f"h_abs{n}")[:])
+        h_abs0 = reuse("h_abs0", [P, S], F32, "h_abs0")
+        for half, (entries, columns) in enumerate(LIST_HALVES):
+            first_product(0, bank(LOW + (LOW - 1) * half)[:, 0 : S // 2], entries)
+            take_abs(0, h_abs0[:, entries])
+        first_product(1, bank(LOW + 1)[:], slice(0, S))
+        take_abs(1, reuse("h_abs1", [P, S], F32, "h_abs1")[:])
         h_abs23 = products_of_pair(2)
-        nc.vector.tensor_tensor(page_of[0][:].indirect(idx2[:]), h_abs[0], weights_of(0, 1), ALU.mult)
+        for entries, columns in LIST_HALVES:
+            nc.vector.tensor_tensor(
+                page_of[0][:].indirect(idx2[:, columns]), h_abs0[:, entries], wgs_dealt[:, entries], ALU.mult
+            )
         weighted[1] = reuse("weighted1", [P, S], F32, "weighted1")[:]
         nc.vector.tensor_tensor(weighted[1], h_abs[1], weights_of(1, 1), ALU.mult)
-        make_z(0, slice(0, T2))
         place(1)
-        weigh_pair(2, h_abs23, reuse("weighted23", [P, 2 * S], F32, "gains0")[:])
-        w1_gh = [reuse(f"w1_g1{a}", [P, KP * PACK], BF16, ["w1_q01", "w1_g11"][a])[:] for a in range(PASSES)]
+        weigh_pair(2, h_abs23, reuse("weighted23", [P, 2 * S], F32, "h_abs1")[:])
+        w1_g1 = reuse("w1_g1", [P, PASSES * KP * PACK], BF16, "w1_q01")
+        w1_gh = [w1_g1[:, KP * PACK * a : KP * PACK * (a + 1)] for a in range(PASSES)]
         for a in range(PASSES):
-            group_w1(nc.scalar.copy, w1_gh[a], 1, a, 0, P)
+            if a == 0:
+                group_w1(nc.scalar.copy, w1_gh[a], 1, a, 0, QUAD)
+                group_w1(nc.scalar.copy, w1_gh[a], 1, a, QUAD, P - QUAD)
+            else:
+                group_w1(nc.scalar.copy, w1_gh[a], 1, a, 0, P)
             codes = quantize(f"w1_1{a}", w1_gh[a], tag=["weighted1", "chain"][a])
             for s in range(PACK):
                 w1_q[LOW + s, a] = (codes, P * s)
-        second_page = reuse("page1", [P, T2], F32, "w1_g11")
-        nc.vector.memset(second_page[:], 0.0)
-        for n in (3, 5, 7):
-            page_of[n] = second_page
+        z_rows.append(reuse("z_rows0", [P, PACK, T2], BF16, "w1_q01"))
+        z_rows.append(reuse("z_rows1", [P, PACK, T2], BF16, "z_rows1"))
+        make_z(0, slice(0, T2))
+        load_gains(4)
         add_rest(1, level_tile(1, "w1_raw11"))
         place(2)
         apply_gains(1)
@@ -269,7 +284,6 @@ def tile_list_returns_chute_grading_kernel(
         weigh_pair(4, h_abs45, reuse("weighted45", [P, 2 * S], F32, "weighted45")[:])
         add_rest(2, level_tile(2, "chain"))
         place(3)
-        load_gains(4)
         apply_gains(2)
         load_gains(6)
 
@@ -369,7 +383,7 @@ def tile_list_returns_chute_grading_kernel(
                         stop=(a == PASSES - 1),
                     )
             if c < 2:
-                y_sb[c] = reuse(f"y{c}", [P, T2], F32, ["tab_w1", "y1"][c])
+                y_sb[c] = reuse(f"y{c}", [P, T2], F32, ["w1_raw01", "y1"][c])
                 for half in range(2):
                     ya, yb = accs[half]
                     yb_sb = reuse(f"yb{c}{half}", [P, BANK], F32, ["h_abs0", "weighted1", "h_abs2", "h_abs6"][2 * c + half])
@@ -379,7 +393,7 @@ def tile_list_returns_chute_grading_kernel(
                         xw_sb[0] = reuse("xw0", [P, S], F32, "xw0")
                         nc.vector.tensor_tensor(xw_sb[0][:], x_sb[0][:], wgo_sb[:], ALU.mult)
             else:
-                both = reuse(f"y_parts{c}", [P, 2 * T2], F32, f"w1_raw0{c - 2}")
+                both = reuse(f"y_parts{c}", [P, 2 * T2], F32, f"w1_raw1{c - 2}")
                 for half in range(2):
                     for part in range(2):
                         first = T2 * part + BANK * half

@@ -298,13 +298,12 @@ def tile_list_returns_chute_grading_kernel(
                     w2_raw[a, pair][:],
                 )
 
+        weigh_pair(6, h_abs67, reuse("weighted67", [P, 2 * S], F32, "chain")[:])
         group_w2(0)
         add_rest(3, level_tile(3, "w2_raw00"))
         place(4)
         apply_gains(3)
         load_gains(7)
-        after3 = reuse("after3", [P, 2 * T2], F32, "w2_raw00")
-        weigh_pair(6, h_abs67, after3[:, 0:T2])
         group_w2(1)
         add_rest(4, level_tile(4, "w2_raw10"))
         place(5)
@@ -323,11 +322,11 @@ def tile_list_returns_chute_grading_kernel(
         exp_sb = [exp_all[:, c, :] for c in range(N // P)]
 
         apply_gains(4)
-        z_g_low = [reuse("z_g_low0", [P, BANK * PACK], BF16, "w1_g00")]
-        group_rows(nc.scalar.copy, z_g_low[0][:], z_rows[0][:, :, HALVES[0]])
-        add_rest(5, after3[:, T2 : 2 * T2])
+        add_rest(5, level_tile(5, "w2_raw01"))
         place(6)
         apply_gains(5)
+        z_g_low = [reuse("z_g_low0", [P, BANK * PACK], BF16, "w1_g00")]
+        group_rows(nc.scalar.copy, z_g_low[0][:], z_rows[0][:, :, HALVES[0]])
         add_rest(6, level_tile(6, "w2_raw10"))
         place(7)
         apply_gains(6)
@@ -335,30 +334,30 @@ def tile_list_returns_chute_grading_kernel(
         group_rows(nc.scalar.copy, z_g_low[1][:], z_rows[0][:, :, HALVES[1]])
         for cols in HALVES:
             make_z(7, cols)
-        late_codes = reuse("late_codes", [P, 2 * BANK], U32, "w2_raw00")
+        z_g_high = [reuse(f"z_g_high{half}", [P, BANK * PACK], BF16, ["late", "picked"][half]) for half in range(2)]
+        split = BANK - VECTOR_SLOTS
+        group_rows(nc.scalar.copy, z_g_high[0][:, 0 : split * PACK], z_rows[1][:, :, 0:split])
+        group_rows(nc.vector.tensor_copy, z_g_high[0][:, split * PACK :], z_rows[1][:, :, split:BANK])
+        group_rows(nc.scalar.copy, z_g_high[1][:], z_rows[1][:, :, HALVES[1]])
+        z_q = {(1, 0): (quantize("z_10", z_g_high[0][:]), 0)}
+        late_codes = reuse("late_codes", [P, 3 * BANK], U32, "chain")
         w2_q = [quantize("w2_0", w2_g[0], codes=late_codes[:, 0:BANK])]
-        z_q = {(0, 0): (quantize("z_00", z_g_low[0][:], codes=late_codes[:, BANK : 2 * BANK]), 0)}
-        z_q[0, 1] = (quantize("z_01", z_g_low[1][:]), 0)
-        z_g_first = reuse("z_g_first", [P, BANK * PACK], BF16, "late")
-        z_g_second = reuse("z_g_second", [P, BANK * PACK], BF16, "picked")
-        split = T2 - VECTOR_SLOTS
-        group_rows(nc.scalar.copy, z_g_first[:], z_rows[1][:, :, HALVES[0]])
-        group_rows(nc.scalar.copy, z_g_second[:, 0 : (split - BANK) * PACK], z_rows[1][:, :, BANK:split])
-        group_rows(nc.vector.tensor_copy, z_g_second[:, (split - BANK) * PACK :], z_rows[1][:, :, split:T2])
-        z_q[1, 0] = (quantize("z_10", z_g_first[:]), 0)
-        w2_q.append(quantize("w2_1", w2_g[1], tag="late"))
-        z_q[1, 1] = (quantize("z_11", z_g_second[:]), 0)
+        for half in range(2):
+            codes = late_codes[:, BANK * (half + 1) : BANK * (half + 2)]
+            z_q[0, half] = (quantize(f"z_0{half}", z_g_low[half][:], codes=codes), 0)
+        z_q[1, 1] = (quantize("z_11", z_g_high[1][:]), 0)
+        w2_q.append(quantize("w2_1", w2_g[1], tag="picked"))
 
         y_sb = {}
         x_sb = {}
 
         def scores(c):
             accs = {}
-            for a in range(PASSES):
-                for half in range(2):
-                    if a == 0:
-                        base = LOW * (c % 2) + 2 * half
-                        accs[half] = (bank(base), bank(base + 1))
+            for half in range(2):
+                base = LOW * (c % 2) + 2 * half
+                accs[half] = (bank(base), bank(base + 1))
+                order = (1, 0) if (c == 0) == (half == 0) else (0, 1)
+                for a in order:
                     ya, yb = accs[half]
                     (z_codes, z_scales), first_slot = z_q[a, half]
                     slots = slice(first_slot, first_slot + BANK)
@@ -368,8 +367,8 @@ def tile_list_returns_chute_grading_kernel(
                         lhsT_scale=w3_s[:, a, P * c : P * (c + 1)],
                         rhs=z_codes[:, slots].bitcast(FP8X4),
                         rhs_scale=z_scales[:, slots],
-                        start=(a == 0),
-                        stop=(a == PASSES - 1),
+                        start=(a == order[0]),
+                        stop=(a == order[1]),
                     )
                     codes, scales = w2_q[c // 2]
                     first = 2 * P * a + P * (c % 2)
@@ -379,8 +378,8 @@ def tile_list_returns_chute_grading_kernel(
                         lhsT_scale=scales[:, first : first + P],
                         rhs=z_codes[:, slots].bitcast(FP8X4),
                         rhs_scale=z_scales[:, slots],
-                        start=(a == 0),
-                        stop=(a == PASSES - 1),
+                        start=(a == order[0]),
+                        stop=(a == order[1]),
                     )
             if c < 2:
                 y_sb[c] = reuse(f"y{c}", [P, T2], F32, ["w1_raw01", "y1"][c])

@@ -225,12 +225,12 @@ def tile_list_returns_chute_grading_kernel(
 
         z_rows = []
 
-        def make_z(n, cols):
+        def make_z(n, half):
             nc.vector.scalar_tensor_tensor(
-                out=z_rows[n // PACK][:, n % PACK, cols],
-                in0=page_of[n][:, cols],
+                out=z_rows[n // PACK][:, half, n % PACK, :],
+                in0=page_of[n][:, HALVES[half]],
                 scalar=rest_of(n),
-                in1=gains_sb[n][:, cols],
+                in1=gains_sb[n][:, HALVES[half]],
                 op0=ALU.add,
                 op1=ALU.mult,
             )
@@ -240,7 +240,12 @@ def tile_list_returns_chute_grading_kernel(
             nc.scalar.activation(out=dst, in_=page_of[n][:], func=ACT.Identity, bias=rest_of(n))
 
         def apply_gains(n):
-            nc.gpsimd.tensor_tensor(z_rows[n // PACK][:, n % PACK, :], level[n], gains_sb[n][:], ALU.mult)
+            nc.gpsimd.tensor_tensor(
+                z_rows[n // PACK][:, :, n % PACK, :],
+                level[n].rearrange("p (half t) -> p half t", half=2),
+                gains_sb[n][:].rearrange("p (half t) -> p half t", half=2),
+                ALU.mult,
+            )
 
         def level_tile(n, tag):
             return reuse(f"level{n}", [P, T2], F32, tag)[:]
@@ -261,6 +266,9 @@ def tile_list_returns_chute_grading_kernel(
         place(1)
         weigh_pair(2, h_abs23, reuse("weighted23", [P, 2 * S], F32, "h_abs1")[:])
         w1_g1 = reuse("w1_g1", [P, PASSES * KP * PACK], BF16, "w1_q01")
+        z_high = reuse("z_high", [P, PACK * T2], BF16, "z_high")
+        for rows in (w1_g1, z_high):
+            z_rows.append(rows[:].rearrange("p (half i t) -> p half i t", half=2, i=PACK))
         w1_gh = [w1_g1[:, KP * PACK * a : KP * PACK * (a + 1)] for a in range(PASSES)]
         for a in range(PASSES):
             if a == 0:
@@ -271,13 +279,14 @@ def tile_list_returns_chute_grading_kernel(
             codes = quantize(f"w1_1{a}", w1_gh[a], tag=["weighted1", "chain"][a])
             for s in range(PACK):
                 w1_q[LOW + s, a] = (codes, P * s)
-        z_rows.append(reuse("z_rows0", [P, PACK, T2], BF16, "w1_q01"))
-        z_rows.append(reuse("z_rows1", [P, PACK, T2], BF16, "z_rows1"))
-        make_z(0, slice(0, T2))
+            make_z(0, a)
+            if a == 0:
+                make_z(1, 0)
         load_gains(4)
-        add_rest(1, level_tile(1, "w1_raw11"))
+        level1 = reuse("level1", [P, BANK], F32, "w1_raw11")
+        nc.scalar.activation(out=level1[:], in_=page_of[1][:, HALVES[1]], func=ACT.Identity, bias=rest_of(1))
         place(2)
-        apply_gains(1)
+        nc.gpsimd.tensor_tensor(z_rows[0][:, 1, 1, :], level1[:], gains_sb[1][:, HALVES[1]], ALU.mult)
         load_gains(5)
         h_abs45 = products_of_pair(4)
         h_abs67 = products_of_pair(6)
@@ -326,19 +335,19 @@ def tile_list_returns_chute_grading_kernel(
         place(6)
         apply_gains(5)
         z_g_low = [reuse("z_g_low0", [P, BANK * PACK], BF16, "w1_g00")]
-        group_rows(nc.scalar.copy, z_g_low[0][:], z_rows[0][:, :, HALVES[0]])
+        group_rows(nc.scalar.copy, z_g_low[0][:], z_rows[0][:, 0])
         add_rest(6, level_tile(6, "w2_raw10"))
         place(7)
         apply_gains(6)
         z_g_low.append(reuse("z_g_low1", [P, BANK * PACK], BF16, "gains1"))
-        group_rows(nc.scalar.copy, z_g_low[1][:], z_rows[0][:, :, HALVES[1]])
-        for cols in HALVES:
-            make_z(7, cols)
+        group_rows(nc.scalar.copy, z_g_low[1][:], z_rows[0][:, 1])
+        for half in range(2):
+            make_z(7, half)
         z_g_high = [reuse(f"z_g_high{half}", [P, BANK * PACK], BF16, ["late", "picked"][half]) for half in range(2)]
         split = BANK - VECTOR_SLOTS
-        group_rows(nc.scalar.copy, z_g_high[0][:, 0 : split * PACK], z_rows[1][:, :, 0:split])
-        group_rows(nc.vector.tensor_copy, z_g_high[0][:, split * PACK :], z_rows[1][:, :, split:BANK])
-        group_rows(nc.scalar.copy, z_g_high[1][:], z_rows[1][:, :, HALVES[1]])
+        group_rows(nc.scalar.copy, z_g_high[0][:, 0 : split * PACK], z_rows[1][:, 0, :, 0:split])
+        group_rows(nc.vector.tensor_copy, z_g_high[0][:, split * PACK :], z_rows[1][:, 0, :, split:BANK])
+        group_rows(nc.scalar.copy, z_g_high[1][:], z_rows[1][:, 1])
         z_q = {(1, 0): (quantize("z_10", z_g_high[0][:]), 0)}
         late_codes = reuse("late_codes", [P, 3 * BANK], U32, "chain")
         w2_q = [quantize("w2_0", w2_g[0], codes=late_codes[:, 0:BANK])]
@@ -397,11 +406,11 @@ def tile_list_returns_chute_grading_kernel(
                     for part in range(2):
                         first = T2 * part + BANK * half
                         nc.scalar.copy(out=both[:, first : first + BANK], in_=accs[half][part][:])
-                y_sb[c] = reuse(f"y{c}", [P, T2], F32, "x1" if c == 2 else "y1")
+                y_sb[c] = reuse(f"y{c}", [P, T2], F32, "x1" if c == 2 else "w1_raw10")
                 nc.gpsimd.tensor_tensor(y_sb[c][:], both[:, 0:T2], both[:, T2 : 2 * T2], ALU.mult)
 
         def pick(c):
-            x_sb[c] = reuse(f"x{c}", [P, S], F32, f"x{c}")
+            x_sb[c] = reuse(f"x{c}", [P, S], F32, "w1_raw11" if c == 2 else f"x{c}")
             nc.vector.tensor_tensor(x_sb[c][:], y_sb[c][:].indirect(idx3[:]), exp_sb[c], ALU.subtract)
 
         def put(c):

@@ -149,10 +149,10 @@ def tile_list_returns_chute_grading_kernel(
                 nc.tensor.transpose(back[:, P * block : P * (block + 1)], picked[:, first : first + P], identity[:])
             nc.scalar.copy(out=wgs_dealt[:, S * s : S * (s + 1)], in_=back[:])
 
-        def group_w1(copy, dst, side, a, first, count):
+        def group_w1(copy, dst, side, a):
             copy(
-                out=dst.rearrange("p (s m i) -> p m s i", s=PACK, i=PACK)[:, first : first + count],
-                in_=w1_raw[side, a][:].rearrange("p i (m s) -> p m s i", s=PACK)[:, first : first + count],
+                out=dst.rearrange("p (s m i) -> p m i s", s=PACK, i=PACK),
+                in_=w1_raw[side, a][:].rearrange("p i (m s) -> p m i s", s=PACK),
             )
 
         w1_q = {}
@@ -161,7 +161,7 @@ def tile_list_returns_chute_grading_kernel(
         nc.vector.tensor_copy(v_s[:], tab_s[:].indirect(idx[:]))
         for a in range(PASSES):
             grouped = reuse(f"w1_g0{a}", [P, KP * PACK], BF16, ["w1_g00", "tab_w0"][a])
-            group_w1(nc.vector.tensor_copy, grouped[:], 0, a, 0, P)
+            group_w1(nc.vector.tensor_copy, grouped[:], 0, a)
             codes = quantize(f"w1_0{a}", grouped[:], tag=f"w1_q0{a}")
             for s in range(PACK):
                 w1_q[s, a] = (codes, P * s)
@@ -251,18 +251,21 @@ def tile_list_returns_chute_grading_kernel(
             return reuse(f"level{n}", [P, T2], F32, tag)[:]
 
         h_abs0 = reuse("h_abs0", [P, S], F32, "h_abs0")
-        for half, (entries, columns) in enumerate(LIST_HALVES):
-            first_product(0, bank(LOW + (LOW - 1) * half)[:, 0 : S // 2], entries)
+        def half_of_slab0(half, acc):
+            entries, columns = LIST_HALVES[half]
+            first_product(0, acc[:, 0 : S // 2], entries)
             take_abs(0, h_abs0[:, entries])
-        first_product(1, bank(LOW + 1)[:], slice(0, S))
-        take_abs(1, reuse("h_abs1", [P, S], F32, "h_abs1")[:])
-        h_abs23 = products_of_pair(2)
-        for entries, columns in LIST_HALVES:
             nc.vector.tensor_tensor(
                 page_of[0][:].indirect(idx2[:, columns]), h_abs0[:, entries], wgs_dealt[:, entries], ALU.mult
             )
+
+        half_of_slab0(0, bank(LOW))
+        first_product(1, bank(LOW + 1)[:], slice(0, S))
+        take_abs(1, reuse("h_abs1", [P, S], F32, "h_abs1")[:])
         weighted[1] = reuse("weighted1", [P, S], F32, "weighted1")[:]
         nc.vector.tensor_tensor(weighted[1], h_abs[1], weights_of(1, 1), ALU.mult)
+        half_of_slab0(1, bank(2 * LOW - 1))
+        h_abs23 = products_of_pair(2)
         place(1)
         weigh_pair(2, h_abs23, reuse("weighted23", [P, 2 * S], F32, "h_abs1")[:])
         w1_g1 = reuse("w1_g1", [P, PASSES * KP * PACK], BF16, "w1_q01")
@@ -271,11 +274,7 @@ def tile_list_returns_chute_grading_kernel(
             z_rows.append(rows[:].rearrange("p (half i t) -> p half i t", half=2, i=PACK))
         w1_gh = [w1_g1[:, KP * PACK * a : KP * PACK * (a + 1)] for a in range(PASSES)]
         for a in range(PASSES):
-            if a == 0:
-                group_w1(nc.scalar.copy, w1_gh[a], 1, a, 0, QUAD)
-                group_w1(nc.scalar.copy, w1_gh[a], 1, a, QUAD, P - QUAD)
-            else:
-                group_w1(nc.scalar.copy, w1_gh[a], 1, a, 0, P)
+            group_w1(nc.scalar.copy, w1_gh[a], 1, a)
             codes = quantize(f"w1_1{a}", w1_gh[a], tag=["weighted1", "chain"][a])
             for s in range(PACK):
                 w1_q[LOW + s, a] = (codes, P * s)

@@ -104,7 +104,7 @@ def tile_list_returns_chute_grading_kernel(
         def load_gains(n):
             gains_sb[n] = load(f"gains{n}", [P, T2], F32, gains_rows[n // PACK, n % PACK], tag=f"gains{n % PACK}")
 
-        idx = load_list("idx", offs)
+        wgs_sb = load("wgs_sb", [P, S], F32, wgs)
         tab_s_rows = keep.tile([P, T // PACK], I32, name="tab_s_rows")
         for q in range(QUADS):
             rows = slice(QUAD * q, QUAD * q + PASSES * SCALE_ROWS)
@@ -112,7 +112,7 @@ def tile_list_returns_chute_grading_kernel(
                 out=tab_s_rows[rows, :], in_=tab_scales[:, SCALE_ROWS * q : SCALE_ROWS * (q + 1), :].bitcast(I32)
             )
             nc.vector.tensor_copy(tab_s[rows, :].bitcast(I32), tab_s_rows[rows, :])
-        wgs_sb = load("wgs_sb", [P, S], F32, wgs)
+        idx = load_list("idx", offs)
         w1_raw = {}
         tab_w = []
         for a in range(PASSES):
@@ -342,17 +342,16 @@ def tile_list_returns_chute_grading_kernel(
         group_rows(nc.scalar.copy, z_g_low[1][:], z_rows[0][:, 1])
         for half in range(2):
             make_z(7, half)
+        late_codes = reuse("late_codes", [P, 3 * BANK], U32, "chain")
+        w2_q = [quantize("w2_0", w2_g[0], codes=late_codes[:, 0:BANK])]
+        z_q = {(0, 0): (quantize("z_00", z_g_low[0][:], codes=late_codes[:, BANK : 2 * BANK]), 0)}
         z_g_high = [reuse(f"z_g_high{half}", [P, BANK * PACK], BF16, ["late", "picked"][half]) for half in range(2)]
         split = BANK - VECTOR_SLOTS
         group_rows(nc.scalar.copy, z_g_high[0][:, 0 : split * PACK], z_rows[1][:, 0, :, 0:split])
         group_rows(nc.vector.tensor_copy, z_g_high[0][:, split * PACK :], z_rows[1][:, 0, :, split:BANK])
         group_rows(nc.scalar.copy, z_g_high[1][:], z_rows[1][:, 1])
-        z_q = {(1, 0): (quantize("z_10", z_g_high[0][:]), 0)}
-        late_codes = reuse("late_codes", [P, 3 * BANK], U32, "chain")
-        w2_q = [quantize("w2_0", w2_g[0], codes=late_codes[:, 0:BANK])]
-        for half in range(2):
-            codes = late_codes[:, BANK * (half + 1) : BANK * (half + 2)]
-            z_q[0, half] = (quantize(f"z_0{half}", z_g_low[half][:], codes=codes), 0)
+        z_q[1, 0] = (quantize("z_10", z_g_high[0][:]), 0)
+        z_q[0, 1] = (quantize("z_01", z_g_low[1][:], codes=late_codes[:, 2 * BANK : 3 * BANK]), 0)
         z_q[1, 1] = (quantize("z_11", z_g_high[1][:]), 0)
         w2_q.append(quantize("w2_1", w2_g[1], tag="picked"))
 
@@ -364,7 +363,7 @@ def tile_list_returns_chute_grading_kernel(
             for half in range(2):
                 base = LOW * (c % 2) + 2 * half
                 accs[half] = (bank(base), bank(base + 1))
-                order = (1, 0) if (c == 0) == (half == 0) else (0, 1)
+                order = (0, 1)
                 for a in order:
                     ya, yb = accs[half]
                     (z_codes, z_scales), first_slot = z_q[a, half]

@@ -27,7 +27,7 @@ QUADS = P // QUAD
 SCALE_ROWS = 4
 LOW = 4
 HALVES = [slice(0, BANK), slice(BANK, 2 * BANK)]
-LIST_HALVES = [(slice(0, S // 2), slice(0, S // 32)), (slice(S // 2, S), slice(S // 32, S // 16))]
+LIST_PIECES = [(slice(first, last), slice(first // 16, last // 16)) for first, last in ((0, 128), (128, 256), (256, 512))]
 ALIGN = 64
 VECTOR_SLOTS = T2 // 4
 
@@ -117,6 +117,7 @@ def tile_list_returns_chute_grading_kernel(
         tab_w = []
         for a in range(PASSES):
             w1_raw[0, a] = load_w1(0, a)
+        for a in range(PASSES):
             tab_w.append(load_table(a))
         idx2 = load_list("idx2", offs2)
         rest_sb = load("rest_sb", [P, 2, PACK], F32, rest.rearrange("(side p i) -> p side i", side=2, i=PACK))
@@ -160,22 +161,23 @@ def tile_list_returns_chute_grading_kernel(
         v_s = reuse("v_s", [P, S], U8, "v_s")
         nc.vector.tensor_copy(v_s[:], tab_s[:].indirect(idx[:]))
         for a in range(PASSES):
-            grouped = reuse(f"w1_g0{a}", [P, KP * PACK], BF16, ["w1_g00", "tab_w0"][a])
+            grouped = reuse(f"w1_g0{a}", [P, KP * PACK], BF16, "w1_g00")
             group_w1(nc.vector.tensor_copy, grouped[:], 0, a)
             codes = quantize(f"w1_0{a}", grouped[:], tag=f"w1_q0{a}")
             for s in range(PACK):
                 w1_q[s, a] = (codes, P * s)
+        for a in range(PASSES):
             words = reuse(f"v_w{a}", [P, S], U32, ["w1_g00", "tab_w0"][a])
             v_w.append(words)
             if a == 0:
                 nc.vector.tensor_copy(words[:], tab_w[a][:].bitcast(U32).indirect(idx[:]))
             else:
-                for entries, columns in LIST_HALVES:
+                for entries, columns in LIST_PIECES:
                     nc.vector.tensor_copy(words[:, entries], tab_w[a][:].bitcast(U32).indirect(idx[:, columns]))
 
         cages = [reuse(f"cage{index}", [P, T2], F32, tag) for index, tag in enumerate(["tab_w1", "w1_raw00"])]
-        for window in cages:
-            nc.vector.memset(window[:], 0.0)
+        nc.gpsimd.memset(cages[0][:], 0.0)
+        nc.vector.memset(cages[1][:], 0.0)
 
         h_abs = {}
         weighted = {}
@@ -208,7 +210,7 @@ def tile_list_returns_chute_grading_kernel(
         def products_of_pair(n):
             both = reuse(f"h_abs{n}", [P, 2 * S], F32, f"h_abs{n}")
             for k in range(2):
-                first_product(n + k, bank(LOW + (n + k) % LOW)[:], slice(0, S))
+                first_product(n + k, bank(LOW + (n + k + 2) % LOW)[:], slice(0, S))
                 take_abs(n + k, both[:, S * k : S * (k + 1)])
             return both
 
@@ -252,19 +254,20 @@ def tile_list_returns_chute_grading_kernel(
 
         h_abs0 = reuse("h_abs0", [P, S], F32, "h_abs0")
         def half_of_slab0(half, acc):
-            entries, columns = LIST_HALVES[half]
-            first_product(0, acc[:, 0 : S // 2], entries)
+            entries, columns = LIST_PIECES[half]
+            first_product(0, acc[:, 0 : entries.stop - entries.start], entries)
             take_abs(0, h_abs0[:, entries])
             nc.vector.tensor_tensor(
                 page_of[0][:].indirect(idx2[:, columns]), h_abs0[:, entries], wgs_dealt[:, entries], ALU.mult
             )
 
         half_of_slab0(0, bank(LOW))
-        first_product(1, bank(LOW + 1)[:], slice(0, S))
+        half_of_slab0(1, bank(LOW + 1))
+        first_product(1, bank(LOW + 2)[:], slice(0, S))
         take_abs(1, reuse("h_abs1", [P, S], F32, "h_abs1")[:])
         weighted[1] = reuse("weighted1", [P, S], F32, "weighted1")[:]
         nc.vector.tensor_tensor(weighted[1], h_abs[1], weights_of(1, 1), ALU.mult)
-        half_of_slab0(1, bank(2 * LOW - 1))
+        half_of_slab0(2, bank(2 * LOW - 1))
         h_abs23 = products_of_pair(2)
         place(1)
         weigh_pair(2, h_abs23, reuse("weighted23", [P, 2 * S], F32, "h_abs1")[:])

@@ -30,6 +30,7 @@ HALVES = [slice(0, BANK), slice(BANK, 2 * BANK)]
 LIST_PIECES = [(slice(first, last), slice(first // 16, last // 16)) for first, last in ((0, 128), (128, 256), (256, 512))]
 ALIGN = 64
 VECTOR_SLOTS = T2 // 4
+SCORE_BANKS = [[(0, 1), (2, 3)], [(0, 3), (4, 5)], [(2, 5), (4, 3)], [(0, 5), (2, 4)]]
 
 
 def tile_list_returns_chute_grading_kernel(
@@ -102,7 +103,7 @@ def tile_list_returns_chute_grading_kernel(
         gains_sb = {}
 
         def load_gains(n):
-            gains_sb[n] = load(f"gains{n}", [P, T2], F32, gains_rows[n // PACK, n % PACK], tag=f"gains{n % PACK}")
+            gains_sb[n] = load(f"gains{n}", [P, T2], F32, gains_rows[n // PACK, n % PACK], tag=f"gains{n % PACK if n < 6 else n}")
 
         wgs_sb = load("wgs_sb", [P, S], F32, wgs)
         tab_s_rows = keep.tile([P, T // PACK], I32, name="tab_s_rows")
@@ -133,6 +134,8 @@ def tile_list_returns_chute_grading_kernel(
                 w2_raw[a, pair] = load(name, [P, PACK, 2 * P], F32, pass_rows(w2, a, cols), tag=name)
         load_gains(2)
         load_gains(3)
+        load_gains(6)
+        load_gains(7)
 
         turned = bank(LOW)
         for block in range(PACK):
@@ -186,9 +189,9 @@ def tile_list_returns_chute_grading_kernel(
 
         h_acc = {}
 
-        def first_product(n, acc, entries):
+        def first_product(n, acc, entries, passes=range(PASSES)):
             h_acc[n] = acc
-            for a in range(PASSES):
+            for a in passes:
                 (codes, scales), first = w1_q[n, a]
                 nc.tensor.matmul_mx(
                     out=acc,
@@ -210,7 +213,10 @@ def tile_list_returns_chute_grading_kernel(
         def products_of_pair(n):
             both = reuse(f"h_abs{n}", [P, 2 * S], F32, f"h_abs{n}")
             for k in range(2):
-                first_product(n + k, bank(LOW + (n + k + 2) % LOW)[:], slice(0, S))
+                if n < LOW:
+                    first_product(n + k, bank(LOW + (n + k + 2) % LOW)[:], slice(0, S))
+                else:
+                    first_product(n + k, h_acc[n + k], slice(0, S), [1])
                 take_abs(n + k, both[:, S * k : S * (k + 1)])
             return both
 
@@ -283,6 +289,8 @@ def tile_list_returns_chute_grading_kernel(
                 w1_q[LOW + s, a] = (codes, P * s)
             make_z(0, a)
             if a == 0:
+                for n in range(LOW, 2 * LOW):
+                    first_product(n, bank(n - LOW)[:], slice(0, S), [0])
                 make_z(1, 0)
         load_gains(4)
         level1 = reuse("level1", [P, BANK], F32, "w1_raw11")
@@ -296,7 +304,6 @@ def tile_list_returns_chute_grading_kernel(
         add_rest(2, level_tile(2, "chain"))
         place(3)
         apply_gains(2)
-        load_gains(6)
 
         w2_both = reuse("w2_both", [P, PASSES * N * PACK], BF16, "w1_11_scales")
         w2_g = [w2_both[:, N * PACK * pair : N * PACK * (pair + 1)] for pair in range(2)]
@@ -314,7 +321,6 @@ def tile_list_returns_chute_grading_kernel(
         add_rest(3, level_tile(3, "w2_raw00"))
         place(4)
         apply_gains(3)
-        load_gains(7)
         group_w2(1)
         add_rest(4, level_tile(4, "w2_raw10"))
         place(5)
@@ -363,10 +369,10 @@ def tile_list_returns_chute_grading_kernel(
 
         def scores(c):
             accs = {}
-            for half in range(2):
-                base = LOW * (c % 2) + 2 * half
-                accs[half] = (bank(base), bank(base + 1))
-                order = (0, 1)
+            halves = (1, 0) if c == 1 else (0, 1)
+            for half in halves:
+                accs[half] = tuple(bank(index) for index in SCORE_BANKS[c][half])
+                order = (1, 0) if (c, half) == (1, 1) else (0, 1)
                 for a in order:
                     ya, yb = accs[half]
                     (z_codes, z_scales), first_slot = z_q[a, half]
@@ -393,13 +399,13 @@ def tile_list_returns_chute_grading_kernel(
                     )
             if c < 2:
                 y_sb[c] = reuse(f"y{c}", [P, T2], F32, ["w1_raw01", "y1"][c])
-                for half in range(2):
+                for half in halves:
                     ya, yb = accs[half]
                     yb_sb = reuse(f"yb{c}{half}", [P, BANK], F32, ["h_abs0", "weighted1", "h_abs2", "h_abs6"][2 * c + half])
                     nc.scalar.copy(out=yb_sb[:], in_=yb[:])
                     nc.vector.tensor_tensor(y_sb[c][:, HALVES[half]], ya[:], yb_sb[:], ALU.mult)
                     if (c, half) == (1, 0):
-                        xw_sb[0] = reuse("xw0", [P, S], F32, "xw0")
+                        xw_sb[0] = reuse("xw0", [P, S], F32, "h_abs2")
                         nc.vector.tensor_tensor(xw_sb[0][:], x_sb[0][:], wgo_sb[:], ALU.mult)
             else:
                 both = reuse(f"y_parts{c}", [P, 2 * T2], F32, f"w1_raw1{c - 2}")

@@ -178,8 +178,7 @@ def tile_list_returns_chute_grading_kernel(
                 for entries, columns in LIST_PIECES:
                     nc.vector.tensor_copy(words[:, entries], tab_w[a][:].bitcast(U32).indirect(idx[:, columns]))
 
-        cages = [reuse(f"cage{index}", [P, T2], F32, tag) for index, tag in enumerate(["tab_w1", "w1_raw00"])]
-        nc.gpsimd.memset(cages[0][:], 0.0)
+        cages = {1: reuse("cage1", [P, T2], F32, "w1_raw00")}
         nc.vector.memset(cages[1][:], 0.0)
 
         h_abs = {}
@@ -404,9 +403,9 @@ def tile_list_returns_chute_grading_kernel(
                     yb_sb = reuse(f"yb{c}{half}", [P, BANK], F32, ["h_abs0", "weighted1", "h_abs2", "h_abs6"][2 * c + half])
                     nc.scalar.copy(out=yb_sb[:], in_=yb[:])
                     nc.vector.tensor_tensor(y_sb[c][:, HALVES[half]], ya[:], yb_sb[:], ALU.mult)
-                    if (c, half) == (1, 0):
-                        xw_sb[0] = reuse("xw0", [P, S], F32, "h_abs2")
-                        nc.vector.tensor_tensor(xw_sb[0][:], x_sb[0][:], wgo_sb[:], ALU.mult)
+                    if (c, half) == (1, 1):
+                        xw_sb[0] = reuse("xw0", [P, S], F32, "xw0")
+                        nc.gpsimd.tensor_tensor(xw_sb[0][:], x_sb[0][:], wgo_sb[:], ALU.mult)
             else:
                 both = reuse(f"y_parts{c}", [P, 2 * T2], F32, f"w1_raw1{c - 2}")
                 for half in range(2):
@@ -432,6 +431,8 @@ def tile_list_returns_chute_grading_kernel(
         scores(0)
         pick(0)
         scores(1)
+        cages[0] = reuse("cage0", [P, T2], F32, "h_abs2")
+        nc.gpsimd.memset(cages[0][:], 0.0)
         pick(1)
         xw_sb[1] = reuse("xw1", [P, S], F32, "xw1")
         nc.gpsimd.tensor_tensor(xw_sb[1][:], x_sb[1][:], wgo_sb[:], ALU.mult)

@@ -30,7 +30,9 @@ HALVES = [slice(0, BANK), slice(BANK, 2 * BANK)]
 LIST_PIECES = [(slice(first, last), slice(first // 16, last // 16)) for first, last in ((0, 128), (128, 256), (256, 512))]
 ALIGN = 64
 VECTOR_SLOTS = T2 // 4
-SCORE_BANKS = [[(0, 1), (2, 3)], [(0, 3), (4, 5)], [(2, 5), (4, 3)], [(0, 5), (2, 4)]]
+Z6_VECTOR = 128
+QUARTERS = [slice(0, BANK // 2), slice(BANK // 2, BANK)]
+SCORE_BANKS = [[(0, 1), (2, 3), (6, 7)], [(0, 3), (4, 5)], [(2, 5), (4, 3)], [(0, 5), (2, 4)]]
 
 
 def tile_list_returns_chute_grading_kernel(
@@ -57,12 +59,13 @@ def tile_list_returns_chute_grading_kernel(
         def bank(index):
             return psum.tile([P, BANK], F32, name=f"bank{index}")
 
-        def quantize(name, grouped, tag="", codes=None):
+        def quantize(name, grouped, tag="", codes=None, scales=None):
             width = grouped.shape[1] // PACK
             if codes is None:
                 codes = keep.tile([P, width], U32, name=name + "_codes", tag=tag, align_bytes=ALIGN)[:]
-            scales = keep.tile([P, width], U8, name=name + "_scales", tag=name + "_scales", align_bytes=ALIGN)
-            nc.vector.quantize_mx(out=codes.bitcast(FP8X4), scales=scales[:], in_=grouped)
+            if scales is None:
+                scales = keep.tile([P, width], U8, name=name + "_scales", tag=name + "_scales", align_bytes=ALIGN)[:]
+            nc.vector.quantize_mx(out=codes.bitcast(FP8X4), scales=scales, in_=grouped)
             return codes, scales
 
         def group_rows(copy, dst, rows):
@@ -153,10 +156,10 @@ def tile_list_returns_chute_grading_kernel(
                 nc.tensor.transpose(back[:, P * block : P * (block + 1)], picked[:, first : first + P], identity[:])
             nc.scalar.copy(out=wgs_dealt[:, S * s : S * (s + 1)], in_=back[:])
 
-        def group_w1(copy, dst, side, a):
+        def group_w1(copy, dst, side, a, part=slice(0, PACK)):
             copy(
-                out=dst.rearrange("p (s m i) -> p m i s", s=PACK, i=PACK),
-                in_=w1_raw[side, a][:].rearrange("p i (m s) -> p m i s", s=PACK),
+                out=dst.rearrange("p (s m i) -> p m i s", s=PACK, i=PACK)[:, :, :, part],
+                in_=w1_raw[side, a][:].rearrange("p i (m s) -> p m i s", s=PACK)[:, :, :, part],
             )
 
         w1_q = {}
@@ -257,45 +260,49 @@ def tile_list_returns_chute_grading_kernel(
         def level_tile(n, tag):
             return reuse(f"level{n}", [P, T2], F32, tag)[:]
 
-        h_abs0 = reuse("h_abs0", [P, S], F32, "h_abs0")
-        def half_of_slab0(half, acc):
-            entries, columns = LIST_PIECES[half]
-            first_product(0, acc[:, 0 : entries.stop - entries.start], entries)
-            take_abs(0, h_abs0[:, entries])
-            nc.vector.tensor_tensor(
-                page_of[0][:].indirect(idx2[:, columns]), h_abs0[:, entries], wgs_dealt[:, entries], ALU.mult
-            )
-
-        half_of_slab0(0, bank(LOW))
-        half_of_slab0(1, bank(LOW + 1))
-        first_product(1, bank(LOW + 2)[:], slice(0, S))
+        for piece, (entries, columns) in enumerate(LIST_PIECES):
+            count = entries.stop - entries.start
+            first_product(0, bank(LOW + piece)[:, 0:count], entries)
+            take_abs(0, reuse(f"h_abs0{piece}", [P, count], F32, f"h_abs0{piece}")[:])
+            window = page_of[0][:].indirect(idx2[:, columns])
+            if piece < 2:
+                nc.vector.tensor_tensor(window, h_abs[0], wgs_dealt[:, entries], ALU.mult)
+            else:
+                weighted[0] = reuse("weighted0", [P, count], F32, "weighted0")[:]
+                nc.vector.tensor_tensor(weighted[0], h_abs[0], wgs_dealt[:, entries], ALU.mult)
+                nc.vector.tensor_copy(window, weighted[0])
+        first_product(1, bank(2 * LOW - 1)[:], slice(0, S))
         take_abs(1, reuse("h_abs1", [P, S], F32, "h_abs1")[:])
-        weighted[1] = reuse("weighted1", [P, S], F32, "weighted1")[:]
-        nc.vector.tensor_tensor(weighted[1], h_abs[1], weights_of(1, 1), ALU.mult)
-        half_of_slab0(2, bank(2 * LOW - 1))
+        weighted[1] = reuse("weighted1", [P, S], F32, "h_abs02")[:]
+        nc.gpsimd.tensor_tensor(weighted[1], h_abs[1], weights_of(1, 1), ALU.mult)
         h_abs23 = products_of_pair(2)
         place(1)
         weigh_pair(2, h_abs23, reuse("weighted23", [P, 2 * S], F32, "h_abs1")[:])
-        w1_g1 = reuse("w1_g1", [P, PASSES * KP * PACK], BF16, "w1_q01")
-        z_high = reuse("z_high", [P, PACK * T2], BF16, "z_high")
-        for rows in (w1_g1, z_high):
-            z_rows.append(rows[:].rearrange("p (half i t) -> p half i t", half=2, i=PACK))
-        w1_gh = [w1_g1[:, KP * PACK * a : KP * PACK * (a + 1)] for a in range(PASSES)]
+        shared = reuse("shared", [P, PACK * T2 + BANK + T2], BF16, "w1_q01")
+        tail_at = PACK * T2 - BANK - Z6_VECTOR
+        z_high = reuse("z_high", [P, tail_at + 2 * S], BF16, "z_high")
+        for rows in (shared[:, 0 : PACK * T2], z_high[:, 0 : PACK * T2]):
+            z_rows.append(rows.rearrange("p (half i t) -> p half i t", half=2, i=PACK))
+        w1_gh = [shared[:, BANK + KP * PACK * (1 - a) : BANK + KP * PACK * (2 - a)] for a in range(PASSES)]
+        level0 = shared[:, PACK * T2 + BANK :].bitcast(F32)
+        group_w1(nc.scalar.copy, w1_gh[0], 1, 0, slice(0, 2))
+        nc.scalar.activation(out=level0, in_=page_of[0][:, HALVES[0]], func=ACT.Identity, bias=rest_of(0))
+        nc.gpsimd.tensor_tensor(z_rows[0][:, 0, 0, :], level0, gains_sb[0][:, HALVES[0]], ALU.mult)
+        group_w1(nc.scalar.copy, w1_gh[0], 1, 0, slice(2, PACK))
+        group_w1(nc.scalar.copy, w1_gh[1], 1, 1)
         for a in range(PASSES):
-            group_w1(nc.scalar.copy, w1_gh[a], 1, a)
-            codes = quantize(f"w1_1{a}", w1_gh[a], tag=["weighted1", "chain"][a])
+            codes = quantize(f"w1_1{a}", w1_gh[a], tag=["h_abs02", "chain"][a])
             for s in range(PACK):
                 w1_q[LOW + s, a] = (codes, P * s)
-            make_z(0, a)
             if a == 0:
                 for n in range(LOW, 2 * LOW):
                     first_product(n, bank(n - LOW)[:], slice(0, S), [0])
-                make_z(1, 0)
+            make_z(1 - a, 1)
         load_gains(4)
         level1 = reuse("level1", [P, BANK], F32, "w1_raw11")
-        nc.scalar.activation(out=level1[:], in_=page_of[1][:, HALVES[1]], func=ACT.Identity, bias=rest_of(1))
+        nc.scalar.activation(out=level1[:], in_=page_of[1][:, HALVES[0]], func=ACT.Identity, bias=rest_of(1))
         place(2)
-        nc.gpsimd.tensor_tensor(z_rows[0][:, 1, 1, :], level1[:], gains_sb[1][:, HALVES[1]], ALU.mult)
+        nc.gpsimd.tensor_tensor(z_rows[0][:, 0, 1, :], level1[:], gains_sb[1][:, HALVES[0]], ALU.mult)
         load_gains(5)
         h_abs45 = products_of_pair(4)
         h_abs67 = products_of_pair(6)
@@ -315,7 +322,10 @@ def tile_list_returns_chute_grading_kernel(
                     w2_raw[a, pair][:],
                 )
 
-        weigh_pair(6, h_abs67, reuse("weighted67", [P, 2 * S], F32, "chain")[:])
+        weighted[6] = reuse("weighted6", [P, S], F32, "chain")[:]
+        weighted[7] = z_high[:, tail_at:].bitcast(F32)
+        for n in (6, 7):
+            nc.gpsimd.tensor_tensor(weighted[n], h_abs[n], weights_of(n, 1), ALU.mult)
         group_w2(0)
         add_rest(3, level_tile(3, "w2_raw00"))
         place(4)
@@ -343,67 +353,93 @@ def tile_list_returns_chute_grading_kernel(
         apply_gains(5)
         z_g_low = [reuse("z_g_low0", [P, BANK * PACK], BF16, "w1_g00")]
         group_rows(nc.scalar.copy, z_g_low[0][:], z_rows[0][:, 0])
-        add_rest(6, level_tile(6, "w2_raw10"))
+        front, back = slice(0, BANK - Z6_VECTOR), slice(BANK - Z6_VECTOR, BANK)
+
+        def by_halves(rows, slots):
+            return rows.rearrange("p (half t) -> p half t", half=2)[:, :, slots]
+
+        level6 = reuse("level6", [P, 2, front.stop], F32, "w2_raw10")
+        nc.scalar.activation(out=level6[:], in_=by_halves(page_of[6][:], front), func=ACT.Identity, bias=rest_of(6))
         place(7)
-        apply_gains(6)
+        nc.gpsimd.tensor_tensor(z_rows[1][:, :, 2, front], level6[:], by_halves(gains_sb[6][:], front), ALU.mult)
         z_g_low.append(reuse("z_g_low1", [P, BANK * PACK], BF16, "gains1"))
         group_rows(nc.scalar.copy, z_g_low[1][:], z_rows[0][:, 1])
-        for half in range(2):
-            make_z(7, half)
-        late_codes = reuse("late_codes", [P, 3 * BANK], U32, "chain")
-        w2_q = [quantize("w2_0", w2_g[0], codes=late_codes[:, 0:BANK])]
-        z_q = {(0, 0): (quantize("z_00", z_g_low[0][:], codes=late_codes[:, BANK : 2 * BANK]), 0)}
+        nc.vector.scalar_tensor_tensor(
+            out=z_rows[1][:, :, 2, back],
+            in0=by_halves(page_of[6][:], back),
+            scalar=rest_of(6),
+            in1=by_halves(gains_sb[6][:], back),
+            op0=ALU.add,
+            op1=ALU.mult,
+        )
+        late_codes = reuse("late_codes", [P, 3 * BANK], U32, "gains6")
+        z_q = {}
         z_g_high = [reuse(f"z_g_high{half}", [P, BANK * PACK], BF16, ["late", "picked"][half]) for half in range(2)]
         split = BANK - VECTOR_SLOTS
+        make_z(7, 0)
         group_rows(nc.scalar.copy, z_g_high[0][:, 0 : split * PACK], z_rows[1][:, 0, :, 0:split])
+        z_q[0, 0] = (quantize("z_00", z_g_low[0][:], codes=late_codes[:, BANK : 2 * BANK]), 0)
+        make_z(7, 1)
+        for part in QUARTERS:
+            group_rows(nc.scalar.copy, z_g_high[1][:, part.start * PACK : part.stop * PACK], z_rows[1][:, 1, :, part])
         group_rows(nc.vector.tensor_copy, z_g_high[0][:, split * PACK :], z_rows[1][:, 0, :, split:BANK])
-        group_rows(nc.scalar.copy, z_g_high[1][:], z_rows[1][:, 1])
+        w2_q = [quantize("w2_0", w2_g[0], codes=late_codes[:, 0:BANK])]
         z_q[1, 0] = (quantize("z_10", z_g_high[0][:]), 0)
         z_q[0, 1] = (quantize("z_01", z_g_low[1][:], codes=late_codes[:, 2 * BANK : 3 * BANK]), 0)
-        z_q[1, 1] = (quantize("z_11", z_g_high[1][:]), 0)
+        last_codes = reuse("z_11_codes", [P, BANK], U32, "z_11_codes")
+        last_scales = reuse("z_11_scales", [P, BANK], U8, "z_11_scales")
+        for part in QUARTERS:
+            grouped = z_g_high[1][:, part.start * PACK : part.stop * PACK]
+            quantize("z_11", grouped, codes=last_codes[:, part], scales=last_scales[:, part])
+        z_q[1, 1] = ((last_codes[:], last_scales[:]), 0)
         w2_q.append(quantize("w2_1", w2_g[1], tag="picked"))
 
         y_sb = {}
         x_sb = {}
 
         def scores(c):
-            accs = {}
-            halves = (1, 0) if c == 1 else (0, 1)
-            for half in halves:
-                accs[half] = tuple(bank(index) for index in SCORE_BANKS[c][half])
-                order = (1, 0) if (c, half) == (1, 1) else (0, 1)
-                for a in order:
-                    ya, yb = accs[half]
-                    (z_codes, z_scales), first_slot = z_q[a, half]
-                    slots = slice(first_slot, first_slot + BANK)
-                    nc.tensor.matmul_mx(
-                        out=yb[:],
-                        lhsT=w3_w[:, a, 2 * P * c : 2 * P * (c + 1)].bitcast(FP4X4),
-                        lhsT_scale=w3_s[:, a, P * c : P * (c + 1)],
-                        rhs=z_codes[:, slots].bitcast(FP8X4),
-                        rhs_scale=z_scales[:, slots],
-                        start=(a == order[0]),
-                        stop=(a == order[1]),
-                    )
-                    codes, scales = w2_q[c // 2]
-                    first = 2 * P * a + P * (c % 2)
-                    nc.tensor.matmul_mx(
-                        out=ya[:],
-                        lhsT=codes[:, first : first + P].bitcast(FP8X4),
-                        lhsT_scale=scales[:, first : first + P],
-                        rhs=z_codes[:, slots].bitcast(FP8X4),
-                        rhs_scale=z_scales[:, slots],
-                        start=(a == order[0]),
-                        stop=(a == order[1]),
-                    )
+            whole = slice(0, BANK)
+            pieces = [(0, whole), (1, QUARTERS[0]), (1, QUARTERS[1])] if c == 0 else [(0, whole), (1, whole)]
+            accs = [tuple(bank(index)[:, part] for index in SCORE_BANKS[c][k]) for k, (half, part) in enumerate(pieces)]
+            halves = (1, 0) if c == 1 else range(len(pieces))
+            steps = [(k, a) for k in halves for a in ((1, 0) if (c, k) == (1, 1) else (0, 1))]
+            if c == 0:
+                steps = steps[0:2] + sorted(steps[2:], key=lambda step: step[1])
+            for k, a in steps:
+                order = (1, 0) if (c, k) == (1, 1) else (0, 1)
+                ya, yb = accs[k]
+                half, slots = pieces[k]
+                (z_codes, z_scales), first_slot = z_q[a, half]
+                nc.tensor.matmul_mx(
+                    out=yb,
+                    lhsT=w3_w[:, a, 2 * P * c : 2 * P * (c + 1)].bitcast(FP4X4),
+                    lhsT_scale=w3_s[:, a, P * c : P * (c + 1)],
+                    rhs=z_codes[:, slots].bitcast(FP8X4),
+                    rhs_scale=z_scales[:, slots],
+                    start=(a == order[0]),
+                    stop=(a == order[1]),
+                )
+                codes, scales = w2_q[c // 2]
+                first = 2 * P * a + P * (c % 2)
+                nc.tensor.matmul_mx(
+                    out=ya,
+                    lhsT=codes[:, first : first + P].bitcast(FP8X4),
+                    lhsT_scale=scales[:, first : first + P],
+                    rhs=z_codes[:, slots].bitcast(FP8X4),
+                    rhs_scale=z_scales[:, slots],
+                    start=(a == order[0]),
+                    stop=(a == order[1]),
+                )
             if c < 2:
                 y_sb[c] = reuse(f"y{c}", [P, T2], F32, ["w1_raw01", "y1"][c])
-                for half in halves:
-                    ya, yb = accs[half]
-                    yb_sb = reuse(f"yb{c}{half}", [P, BANK], F32, ["h_abs0", "weighted1", "h_abs2", "h_abs6"][2 * c + half])
-                    nc.scalar.copy(out=yb_sb[:], in_=yb[:])
-                    nc.vector.tensor_tensor(y_sb[c][:, HALVES[half]], ya[:], yb_sb[:], ALU.mult)
-                    if (c, half) == (1, 1):
+                for k in halves:
+                    ya, yb = accs[k]
+                    half, slots = pieces[k]
+                    tag = [["h_abs00", "h_abs02", "h_abs01"], ["h_abs2", "h_abs6"]][c][k]
+                    yb_sb = reuse(f"yb{c}{k}", [P, slots.stop - slots.start], F32, tag)
+                    nc.scalar.copy(out=yb_sb[:], in_=yb)
+                    nc.vector.tensor_tensor(y_sb[c][:, HALVES[half]][:, slots], ya, yb_sb[:], ALU.mult)
+                    if (c, k) == (1, 1):
                         xw_sb[0] = reuse("xw0", [P, S], F32, "xw0")
                         nc.gpsimd.tensor_tensor(xw_sb[0][:], x_sb[0][:], wgo_sb[:], ALU.mult)
             else:
@@ -411,7 +447,7 @@ def tile_list_returns_chute_grading_kernel(
                 for half in range(2):
                     for part in range(2):
                         first = T2 * part + BANK * half
-                        nc.scalar.copy(out=both[:, first : first + BANK], in_=accs[half][part][:])
+                        nc.scalar.copy(out=both[:, first : first + BANK], in_=accs[half][part])
                 y_sb[c] = reuse(f"y{c}", [P, T2], F32, "x1" if c == 2 else "w1_raw10")
                 nc.gpsimd.tensor_tensor(y_sb[c][:], both[:, 0:T2], both[:, T2 : 2 * T2], ALU.mult)
 

from contextlib import ExitStack

import concourse.mybir as mybir
from concourse.masks import make_identity

K, T, S, H, T2, N = 1024, 2048, 512, 1024, 1024, 512
FLOPS = 2 * K * H * S + 2 * 2 * H * N * T2

F32 = mybir.dt.float32
BF16 = mybir.dt.bfloat16
I32 = mybir.dt.int32
U32 = mybir.dt.uint32
U16 = mybir.dt.uint16
U8 = mybir.dt.uint8
FP8X4 = mybir.dt.float8_e4m3fn_x4
FP4X4 = mybir.dt.float4_e2m1fn_x4
ALU = mybir.AluOpType
ACT = mybir.ActivationFunctionType

P = 128
PACK = 4
KP = P * PACK
PASSES = 2
BANK = 512
QUAD = 32
QUADS = P // QUAD
SCALE_ROWS = 4
LOW = 4
HALVES = [slice(0, BANK), slice(BANK, 2 * BANK)]
LIST_PIECES = [(slice(first, last), slice(first // 16, last // 16)) for first, last in ((0, 128), (128, 256), (256, 512))]
ALIGN = 64
VECTOR_SLOTS = T2 // 4
Z6_VECTOR = 128
QUARTERS = [slice(0, BANK // 2), slice(BANK // 2, BANK)]
SCORE_BANKS = [[(0, 1), (2, 3), (6, 7)], [(0, 3), (4, 5)], [(2, 5), (4, 3)], [(0, 5), (2, 4)]]


def tile_list_returns_chute_grading_kernel(
    tc, tab_words, tab_scales, offs, w1, wgs, offs2, rest, gains, w2, w3_words, w3_scales, offs3, expected, wgo, offs4, out
):
    nc = tc.nc
    with ExitStack() as ctx:
        keep = ctx.enter_context(tc.tile_pool(name="keep", bufs=1))
        psum = ctx.enter_context(tc.psum_pool(name="psum", bufs=1))

        def load(name, shape, dtype, src, tag=""):
            loaded = keep.tile(shape, dtype, name=name, tag=tag, align_bytes=ALIGN)
            nc.sync.dma_start(out=loaded[:], in_=src)
            return loaded

        def load_list(name, src):
            loaded = keep.tile([P, S // 16], U16, name=name)
            nc.sync.dma_start(loaded[:], src)
            return loaded

        def pass_rows(weight, a, cols):
            return weight[KP * a : KP * (a + 1), cols].rearrange("(p i) c -> p i c", i=PACK)

        def bank(index):
            return psum.tile([P, BANK], F32, name=f"bank{index}")

        def quantize(name, grouped, tag="", codes=None, scales=None):
            width = grouped.shape[1] // PACK
            if codes is None:
                codes = keep.tile([P, width], U32, name=name + "_codes", tag=tag, align_bytes=ALIGN)[:]
            if scales is None:
                scales = keep.tile([P, width], U8, name=name + "_scales", tag=name + "_scales", align_bytes=ALIGN)[:]
            nc.vector.quantize_mx(out=codes.bitcast(FP8X4), scales=scales, in_=grouped)
            return codes, scales

        def group_rows(copy, dst, rows):
            copy(
                out=dst.rearrange("p (c j i) -> p c i j", i=PACK, j=PACK),
                in_=rows.rearrange("p i (c j) -> p c i j", j=PACK),
            )

        def group_passes(copy, name, rows):
            width = rows[0].shape[2] * PACK
            grouped = keep.tile([P, PASSES * width], BF16, name=name, align_bytes=ALIGN)
            for a in range(PASSES):
                group_rows(copy, grouped[:, width * a : width * (a + 1)], rows[a])
            return grouped

        tab_s = keep.tile([P, T], U8, name="tab_s", tag="w1_g00", align_bytes=ALIGN)
        nc.gpsimd.memset(tab_s[:].bitcast(I32), 0)
        w3_s = keep.tile([P, PASSES, N], U8, name="w3_s", align_bytes=ALIGN)
        nc.vector.memset(w3_s[:].bitcast(I32), 0)
        identity = keep.tile([P, P], F32, name="identity")
        make_identity(nc, identity[:])
        pages = [keep.tile([P, T2], F32, name=f"page{index}") for index in range(2)]
        for window in pages:
            nc.vector.memset(window[:], 0.0)

        def reuse(name, shape, dtype, tag):
            return keep.tile(shape, dtype, name=name, tag=tag, align_bytes=ALIGN)

        def load_w1(side, a):
            cols = slice(KP * side, KP * (side + 1))
            return load(f"w1_raw{side}{a}", [P, PACK, KP], F32, pass_rows(w1, a, cols), tag=f"w1_raw{side}{a}")

        def load_table(a):
            words = tab_words[a].rearrange("p t i -> p (t i)").bitcast(I32)
            return load(f"tab_w{a}", [P, T], I32, words, tag=f"tab_w{a}")

        gains_rows = gains.rearrange("(side p i) t -> side i p t", side=2, i=PACK)
        gains_sb = {}

        def load_gains(n):
            gains_sb[n] = load(f"gains{n}", [P, T2], F32, gains_rows[n // PACK, n % PACK], tag=f"gains{n % PACK if n < 6 else n}")

        wgs_sb = load("wgs_sb", [P, S], F32, wgs)
        tab_s_rows = keep.tile([P, T // PACK], I32, name="tab_s_rows")
        for q in range(QUADS):
            rows = slice(QUAD * q, QUAD * q + PASSES * SCALE_ROWS)
            nc.sync.dma_start(
                out=tab_s_rows[rows, :], in_=tab_scales[:, SCALE_ROWS * q : SCALE_ROWS * (q + 1), :].bitcast(I32)
            )
            nc.vector.tensor_copy(tab_s[rows, :].bitcast(I32), tab_s_rows[rows, :])
        idx = load_list("idx", offs)
        w1_raw = {}
        tab_w = []
        for a in range(PASSES):
            w1_raw[0, a] = load_w1(0, a)
        for a in range(PASSES):
            tab_w.append(load_table(a))
        idx2 = load_list("idx2", offs2)
        rest_sb = load("rest_sb", [P, 2, PACK], F32, rest.rearrange("(side p i) -> p side i", side=2, i=PACK))
        for a in range(PASSES):
            w1_raw[1, a] = load_w1(1, a)
        load_gains(0)
        load_gains(1)
        w2_raw = {}
        for a in range(PASSES):
            for pair in range(2):
                cols = slice(2 * P * pair, 2 * P * (pair + 1))
                name = f"w2_raw{a}{pair}"
                w2_raw[a, pair] = load(name, [P, PACK, 2 * P], F32, pass_rows(w2, a, cols), tag=name)
        load_gains(2)
        load_gains(3)
        load_gains(6)
        load_gains(7)

        turned = bank(LOW)
        for block in range(PACK):
            nc.tensor.transpose(turned[:, P * block : P * (block + 1)], wgs_sb[:, P * block : P * (block + 1)], identity[:])
        picked = reuse("picked", [P, PACK * S], F32, "picked")
        nc.scalar.copy(
            out=picked[:].rearrange("p (b s q m) -> p b s q m", b=PACK, s=PACK, q=QUADS),
            in_=turned[:].rearrange("p (b m s) -> p b s m", b=PACK, s=PACK).unsqueeze(3).to_broadcast([P, PACK, PACK, QUADS, QUAD]),
        )
        wgs_dealt = keep.tile([P, PACK * S], F32, name="wgs_dealt")
        for s in range(PACK):
            back = bank(LOW + s)
            for block in range(PACK):
                first = S * block + P * s
                nc.tensor.transpose(back[:, P * block : P * (block + 1)], picked[:, first : first + P], identity[:])
            nc.scalar.copy(out=wgs_dealt[:, S * s : S * (s + 1)], in_=back[:])

        def group_w1(copy, dst, side, a, part=slice(0, PACK)):
            copy(
                out=dst.rearrange("p (s m i) -> p m i s", s=PACK, i=PACK)[:, :, :, part],
                in_=w1_raw[side, a][:].rearrange("p i (m s) -> p m i s", s=PACK)[:, :, :, part],
            )

        w1_q = {}
        v_w = []
        v_s = reuse("v_s", [P, S], U8, "v_s")
        nc.vector.tensor_copy(v_s[:], tab_s[:].indirect(idx[:]))
        for a in range(PASSES):
            grouped = reuse(f"w1_g0{a}", [P, KP * PACK], BF16, "w1_g00")
            group_w1(nc.vector.tensor_copy, grouped[:], 0, a)
            codes = quantize(f"w1_0{a}", grouped[:], tag=f"w1_q0{a}")
            for s in range(PACK):
                w1_q[s, a] = (codes, P * s)
        for a in range(PASSES):
            words = reuse(f"v_w{a}", [P, S], U32, ["w1_g00", "tab_w0"][a])
            v_w.append(words)
            if a == 0:
                nc.vector.tensor_copy(words[:], tab_w[a][:].bitcast(U32).indirect(idx[:]))
            else:
                for entries, columns in LIST_PIECES:
                    nc.vector.tensor_copy(words[:, entries], tab_w[a][:].bitcast(U32).indirect(idx[:, columns]))

        cages = {1: reuse("cage1", [P, T2], F32, "w1_raw00")}
        nc.vector.memset(cages[1][:], 0.0)

        h_abs = {}
        weighted = {}
        level = {}
        page_of = [pages[0], pages[1]] + [pages[(n + 1) % 2] for n in range(2, 2 * LOW)]

        h_acc = {}

        def first_product(n, acc, entries, passes=range(PASSES)):
            h_acc[n] = acc
            for a in passes:
                (codes, scales), first = w1_q[n, a]
                nc.tensor.matmul_mx(
                    out=acc,
                    lhsT=codes[:, first : first + P].bitcast(FP8X4),
                    lhsT_scale=scales[:, first : first + P],
                    rhs=v_w[a][:, entries].bitcast(FP8X4),
                    rhs_scale=v_s[SCALE_ROWS * a : P, entries],
                    start=(a == 0),
                    stop=(a == PASSES - 1),
                )

        def take_abs(n, dst):
            h_abs[n] = dst
            nc.scalar.activation(out=dst, in_=h_acc[n], func=ACT.Abs)

        def weights_of(n, count):
            return wgs_dealt[:, S * (n % PACK) : S * (n % PACK + count)]

        def products_of_pair(n):
            both = reuse(f"h_abs{n}", [P, 2 * S], F32, f"h_abs{n}")
            for k in range(2):
                if n < LOW:
                    first_product(n + k, bank(LOW + (n + k + 2) % LOW)[:], slice(0, S))
                else:
                    first_product(n + k, h_acc[n + k], slice(0, S), [1])
                take_abs(n + k, both[:, S * k : S * (k + 1)])
            return both

        def weigh_pair(n, both, dst):
            nc.gpsimd.tensor_tensor(dst, both[:], weights_of(n, 2), ALU.mult)
            weighted[n] = dst[:, 0:S]
            weighted[n + 1] = dst[:, S : 2 * S]

        def place(n):
            nc.vector.tensor_copy(page_of[n][:].indirect(idx2[:]), weighted[n])

        def rest_of(n):
            return rest_sb[:, n // PACK, n % PACK : n % PACK + 1]

        z_rows = []

        def make_z(n, half):
            nc.vector.scalar_tensor_tensor(
                out=z_rows[n // PACK][:, half, n % PACK, :],
                in0=page_of[n][:, HALVES[half]],
                scalar=rest_of(n),
                in1=gains_sb[n][:, HALVES[half]],
                op0=ALU.add,
                op1=ALU.mult,
            )

        def add_rest(n, dst):
            level[n] = dst
            nc.scalar.activation(out=dst, in_=page_of[n][:], func=ACT.Identity, bias=rest_of(n))

        def apply_gains(n):
            nc.gpsimd.tensor_tensor(
                z_rows[n // PACK][:, :, n % PACK, :],
                level[n].rearrange("p (half t) -> p half t", half=2),
                gains_sb[n][:].rearrange("p (half t) -> p half t", half=2),
                ALU.mult,
            )

        def level_tile(n, tag):
            return reuse(f"level{n}", [P, T2], F32, tag)[:]

        for piece, (entries, columns) in enumerate(LIST_PIECES):
            count = entries.stop - entries.start
            first_product(0, bank(LOW + piece)[:, 0:count], entries)
            take_abs(0, reuse(f"h_abs0{piece}", [P, count], F32, f"h_abs0{piece}")[:])
            window = page_of[0][:].indirect(idx2[:, columns])
            if piece < 2:
                nc.vector.tensor_tensor(window, h_abs[0], wgs_dealt[:, entries], ALU.mult)
            else:
                weighted[0] = reuse("weighted0", [P, count], F32, "weighted0")[:]
                nc.vector.tensor_tensor(weighted[0], h_abs[0], wgs_dealt[:, entries], ALU.mult)
                nc.vector.tensor_copy(window, weighted[0])
        first_product(1, bank(2 * LOW - 1)[:], slice(0, S))
        take_abs(1, reuse("h_abs1", [P, S], F32, "h_abs1")[:])
        weighted[1] = reuse("weighted1", [P, S], F32, "h_abs02")[:]
        nc.gpsimd.tensor_tensor(weighted[1], h_abs[1], weights_of(1, 1), ALU.mult)
        h_abs23 = products_of_pair(2)
        place(1)
        weigh_pair(2, h_abs23, reuse("weighted23", [P, 2 * S], F32, "h_abs1")[:])
        shared = reuse("shared", [P, PACK * T2 + BANK + T2], BF16, "w1_q01")
        tail_at = PACK * T2 - BANK - Z6_VECTOR
        z_high = reuse("z_high", [P, tail_at + 2 * S], BF16, "z_high")
        for rows in (shared[:, 0 : PACK * T2], z_high[:, 0 : PACK * T2]):
            z_rows.append(rows.rearrange("p (half i t) -> p half i t", half=2, i=PACK))
        w1_gh = [shared[:, BANK + KP * PACK * (1 - a) : BANK + KP * PACK * (2 - a)] for a in range(PASSES)]
        level0 = shared[:, PACK * T2 + BANK :].bitcast(F32)
        group_w1(nc.scalar.copy, w1_gh[0], 1, 0, slice(0, 2))
        nc.scalar.activation(out=level0, in_=page_of[0][:, HALVES[0]], func=ACT.Identity, bias=rest_of(0))
        nc.gpsimd.tensor_tensor(z_rows[0][:, 0, 0, :], level0, gains_sb[0][:, HALVES[0]], ALU.mult)
        group_w1(nc.scalar.copy, w1_gh[0], 1, 0, slice(2, PACK))
        group_w1(nc.scalar.copy, w1_gh[1], 1, 1)
        for a in range(PASSES):
            codes = quantize(f"w1_1{a}", w1_gh[a], tag=["h_abs02", "chain"][a])
            for s in range(PACK):
                w1_q[LOW + s, a] = (codes, P * s)
            if a == 0:
                for n in range(LOW, 2 * LOW):
                    first_product(n, bank(n - LOW)[:], slice(0, S), [0])
            make_z(1 - a, 1)
        load_gains(4)
        level1 = reuse("level1", [P, BANK], F32, "w1_raw11")
        nc.scalar.activation(out=level1[:], in_=page_of[1][:, HALVES[0]], func=ACT.Identity, bias=rest_of(1))
        place(2)
        nc.gpsimd.tensor_tensor(z_rows[0][:, 0, 1, :], level1[:], gains_sb[1][:, HALVES[0]], ALU.mult)
        load_gains(5)
        h_abs45 = products_of_pair(4)
        h_abs67 = products_of_pair(6)
        weigh_pair(4, h_abs45, reuse("weighted45", [P, 2 * S], F32, "weighted45")[:])
        add_rest(2, level_tile(2, "chain"))
        place(3)
        apply_gains(2)

        w2_both = reuse("w2_both", [P, PASSES * N * PACK], BF16, "w1_11_scales")
        w2_g = [w2_both[:, N * PACK * pair : N * PACK * (pair + 1)] for pair in range(2)]

        def group_w2(a):
            for pair in range(2):
                group_rows(
                    nc.scalar.copy,
                    w2_g[pair][:, 2 * P * PACK * a : 2 * P * PACK * (a + 1)],
                    w2_raw[a, pair][:],
                )

        weighted[6] = reuse("weighted6", [P, S], F32, "chain")[:]
        weighted[7] = z_high[:, tail_at:].bitcast(F32)
        for n in (6, 7):
            nc.gpsimd.tensor_tensor(weighted[n], h_abs[n], weights_of(n, 1), ALU.mult)
        group_w2(0)
        add_rest(3, level_tile(3, "w2_raw00"))
        place(4)
        apply_gains(3)
        group_w2(1)
        add_rest(4, level_tile(4, "w2_raw10"))
        place(5)

        w3_w = keep.tile([P, PASSES, 2 * N], U8, name="w3_w", align_bytes=ALIGN)
        nc.sync.dma_start(out=w3_w[:].bitcast(I32), in_=w3_words.rearrange("a p n -> p a n").bitcast(I32))
        for q in range(QUADS):
            nc.sync.dma_start(
                out=w3_s[QUAD * q : QUAD * q + SCALE_ROWS, :, :].bitcast(I32),
                in_=w3_scales[:, SCALE_ROWS * q : SCALE_ROWS * (q + 1), :].rearrange("a r n -> r a n").bitcast(I32),
            )
        idx3 = load_list("idx3", offs3)
        idx4 = load_list("idx4", offs4)
        wgo_sb = load("wgo_sb", [P, S], F32, wgo)
        exp_all = load("exp_all", [P, N // P, S], F32, expected.rearrange("(c p) m -> p c m", p=P), tag="tab_w0")
        exp_sb = [exp_all[:, c, :] for c in range(N // P)]

        apply_gains(4)
        add_rest(5, level_tile(5, "w2_raw01"))
        place(6)
        apply_gains(5)
        z_g_low = [reuse("z_g_low0", [P, BANK * PACK], BF16, "w1_g00")]
        group_rows(nc.scalar.copy, z_g_low[0][:], z_rows[0][:, 0])
        front, back = slice(0, BANK - Z6_VECTOR), slice(BANK - Z6_VECTOR, BANK)

        def by_halves(rows, slots):
            return rows.rearrange("p (half t) -> p half t", half=2)[:, :, slots]

        level6 = reuse("level6", [P, 2, front.stop], F32, "w2_raw10")
        nc.scalar.activation(out=level6[:], in_=by_halves(page_of[6][:], front), func=ACT.Identity, bias=rest_of(6))
        place(7)
        nc.gpsimd.tensor_tensor(z_rows[1][:, :, 2, front], level6[:], by_halves(gains_sb[6][:], front), ALU.mult)
        z_g_low.append(reuse("z_g_low1", [P, BANK * PACK], BF16, "gains1"))
        group_rows(nc.scalar.copy, z_g_low[1][:], z_rows[0][:, 1])
        nc.vector.scalar_tensor_tensor(
            out=z_rows[1][:, :, 2, back],
            in0=by_halves(page_of[6][:], back),
            scalar=rest_of(6),
            in1=by_halves(gains_sb[6][:], back),
            op0=ALU.add,
            op1=ALU.mult,
        )
        late_codes = reuse("late_codes", [P, 3 * BANK], U32, "gains6")
        z_q = {}
        z_g_high = [reuse(f"z_g_high{half}", [P, BANK * PACK], BF16, ["late", "picked"][half]) for half in range(2)]
        split = BANK - VECTOR_SLOTS
        make_z(7, 0)
        group_rows(nc.scalar.copy, z_g_high[0][:, 0 : split * PACK], z_rows[1][:, 0, :, 0:split])
        z_q[0, 0] = (quantize("z_00", z_g_low[0][:], codes=late_codes[:, BANK : 2 * BANK]), 0)
        make_z(7, 1)
        for part in QUARTERS:
            group_rows(nc.scalar.copy, z_g_high[1][:, part.start * PACK : part.stop * PACK], z_rows[1][:, 1, :, part])
        group_rows(nc.vector.tensor_copy, z_g_high[0][:, split * PACK :], z_rows[1][:, 0, :, split:BANK])
        w2_q = [quantize("w2_0", w2_g[0], codes=late_codes[:, 0:BANK])]
        z_q[1, 0] = (quantize("z_10", z_g_high[0][:]), 0)
        z_q[0, 1] = (quantize("z_01", z_g_low[1][:], codes=late_codes[:, 2 * BANK : 3 * BANK]), 0)
        last_codes = reuse("z_11_codes", [P, BANK], U32, "z_11_codes")
        last_scales = reuse("z_11_scales", [P, BANK], U8, "z_11_scales")
        for part in QUARTERS:
            grouped = z_g_high[1][:, part.start * PACK : part.stop * PACK]
            quantize("z_11", grouped, codes=last_codes[:, part], scales=last_scales[:, part])
        z_q[1, 1] = ((last_codes[:], last_scales[:]), 0)
        w2_q.append(quantize("w2_1", w2_g[1], tag="picked"))

        y_sb = {}
        x_sb = {}

        def scores(c):
            whole = slice(0, BANK)
            pieces = [(0, whole), (1, QUARTERS[0]), (1, QUARTERS[1])] if c == 0 else [(0, whole), (1, whole)]
            accs = [tuple(bank(index)[:, part] for index in SCORE_BANKS[c][k]) for k, (half, part) in enumerate(pieces)]
            halves = (1, 0) if c == 1 else range(len(pieces))
            steps = [(k, a) for k in halves for a in ((1, 0) if (c, k) == (1, 1) else (0, 1))]
            if c == 0:
                steps = steps[0:2] + sorted(steps[2:], key=lambda step: step[1])
            for k, a in steps:
                order = (1, 0) if (c, k) == (1, 1) else (0, 1)
                ya, yb = accs[k]
                half, slots = pieces[k]
                (z_codes, z_scales), first_slot = z_q[a, half]
                nc.tensor.matmul_mx(
                    out=yb,
                    lhsT=w3_w[:, a, 2 * P * c : 2 * P * (c + 1)].bitcast(FP4X4),
                    lhsT_scale=w3_s[:, a, P * c : P * (c + 1)],
                    rhs=z_codes[:, slots].bitcast(FP8X4),
                    rhs_scale=z_scales[:, slots],
                    start=(a == order[0]),
                    stop=(a == order[1]),
                )
                codes, scales = w2_q[c // 2]
                first = 2 * P * a + P * (c % 2)
                nc.tensor.matmul_mx(
                    out=ya,
                    lhsT=codes[:, first : first + P].bitcast(FP8X4),
                    lhsT_scale=scales[:, first : first + P],
                    rhs=z_codes[:, slots].bitcast(FP8X4),
                    rhs_scale=z_scales[:, slots],
                    start=(a == order[0]),
                    stop=(a == order[1]),
                )
            if c < 2:
                y_sb[c] = reuse(f"y{c}", [P, T2], F32, ["w1_raw01", "y1"][c])
                for k in halves:
                    ya, yb = accs[k]
                    half, slots = pieces[k]
                    tag = [["h_abs00", "h_abs02", "h_abs01"], ["h_abs2", "h_abs6"]][c][k]
                    yb_sb = reuse(f"yb{c}{k}", [P, slots.stop - slots.start], F32, tag)
                    nc.scalar.copy(out=yb_sb[:], in_=yb)
                    nc.vector.tensor_tensor(y_sb[c][:, HALVES[half]][:, slots], ya, yb_sb[:], ALU.mult)
                    if (c, k) == (1, 1):
                        xw_sb[0] = reuse("xw0", [P, S], F32, "xw0")
                        nc.gpsimd.tensor_tensor(xw_sb[0][:], x_sb[0][:], wgo_sb[:], ALU.mult)
            else:
                both = reuse(f"y_parts{c}", [P, 2 * T2], F32, f"w1_raw1{c - 2}")
                for half in range(2):
                    for part in range(2):
                        first = T2 * part + BANK * half
                        nc.scalar.copy(out=both[:, first : first + BANK], in_=accs[half][part])
                y_sb[c] = reuse(f"y{c}", [P, T2], F32, "x1" if c == 2 else "w1_raw10")
                nc.gpsimd.tensor_tensor(y_sb[c][:], both[:, 0:T2], both[:, T2 : 2 * T2], ALU.mult)

        def pick(c):
            x_sb[c] = reuse(f"x{c}", [P, S], F32, "w1_raw11" if c == 2 else f"x{c}")
            nc.vector.tensor_tensor(x_sb[c][:], y_sb[c][:].indirect(idx3[:]), exp_sb[c], ALU.subtract)

        def put(c):
            cage = cages[c % 2]
            if c < 2:
                nc.vector.tensor_copy(cage[:].indirect(idx4[:]), xw_sb[c][:])
            else:
                nc.vector.tensor_tensor(cage[:].indirect(idx4[:]), x_sb[c][:], wgo_sb[:], ALU.mult)
            nc.sync.dma_start(out=out[P * c : P * (c + 1), :], in_=cage[:])

        xw_sb = {}
        scores(0)
        pick(0)
        scores(1)
        cages[0] = reuse("cage0", [P, T2], F32, "h_abs2")
        nc.gpsimd.memset(cages[0][:], 0.0)
        pick(1)
        xw_sb[1] = reuse("xw1", [P, S], F32, "xw1")
        nc.gpsimd.tensor_tensor(xw_sb[1][:], x_sb[1][:], wgo_sb[:], ALU.mult)
        put(0)
        put(1)
        scores(2)
        scores(3)
        pick(2)
        pick(3)
        put(2)
        put(3)
